import numpy as np
import ml_dtypes


def mxq(x, axis, fmt="e4m3"):
    dtype, down = {"e4m3": (ml_dtypes.float8_e4m3fn, 7), "e5m2": (ml_dtypes.float8_e5m2, 14)}[fmt]
    v = np.moveaxis(np.asarray(x, np.float32).astype(ml_dtypes.bfloat16).astype(np.float64), axis, -1)
    blocks = v.reshape(v.shape[:-1] + (-1, 32))
    amax = np.abs(blocks).max(-1, keepdims=True)
    byte = np.maximum(np.where(amax > 0, np.frexp(amax)[1] - 1 + 127, 0) - down, 1)
    scale = np.exp2(byte - 127.0)
    codes = (blocks / scale).astype(np.float32).astype(dtype).astype(np.float64)
    return np.moveaxis((codes * scale).reshape(v.shape), -1, axis)


WIDE = False


def mx_kscale(k):
    if not WIDE:
        return np.ones(k)
    levels = np.array([10, -10, 5, -5, 0])
    if k % 512:
        return np.exp2(np.random.permutation(np.resize(levels, k // 32))).repeat(32)
    a = np.empty((k // 512, 16))
    for p in range(k // 512):
        a[p, :8] = np.random.permutation(np.resize(levels, 8))
        for g in range(8):
            far = levels[np.abs(levels - a[p, g]) >= 10]
            a[p, g + 8] = far[np.random.randint(len(far))]
    return np.exp2(a.ravel()).repeat(32)


def f64(x):
    return np.asarray(x).astype(np.float64)


def striped(idx):
    return np.tile(idx.reshape(-1, 16).T, (8, 1)).astype(np.uint16)


def unstriped(offs):
    return offs[:16].T.reshape(-1).astype(np.int64)


E2M1 = np.array([0.0, 0.5, 1.0, 1.5, 2.0, 3.0, 4.0, 6.0, -0.0, -0.5, -1.0, -1.5, -2.0, -3.0, -4.0, -6.0])


def pack_weight(w, fmt):
    k, n = w.shape
    w = f64(np.asarray(w, np.float32).astype(ml_dtypes.bfloat16)).reshape(k // 32, 32, n)
    amax = np.abs(w).max(1)
    if fmt == "e4m3":
        byte = np.frexp(amax)[1] - 1 + 127 - 7
    else:
        mant, ex = np.frexp(amax / 6.0)
        byte = np.where(mant > 0.5, ex, ex - 1) + 127
    byte = np.clip(np.where(amax > 0, byte, 1), 1, 254)
    scaled = (w * np.exp2(127.0 - byte)[:, None, :]).reshape(k, n).astype(np.float32)
    by_word = np.ascontiguousarray(scaled.reshape(k // 512, 128, 4, n).transpose(0, 1, 3, 2))
    if fmt == "e4m3":
        words = by_word.astype(ml_dtypes.float8_e4m3fn).view(np.uint8)
    else:
        c = by_word.astype(ml_dtypes.float4_e2m1fn).view(np.uint8) & 0xF
        words = (c[..., 0::2] | (c[..., 1::2] << 4)).reshape(k // 512, 128, 2 * n)
    return np.ascontiguousarray(words), np.ascontiguousarray(byte.astype(np.uint8).reshape(k // 512, 16, n))


def unpack_weight(words, scales, fmt):
    g, _, n = scales.shape
    words = np.ascontiguousarray(words).reshape(g, 128, n, -1)
    if fmt == "e4m3":
        vals = words.view(ml_dtypes.float8_e4m3fn).astype(np.float64)
    else:
        nib = np.empty((g, 128, n, 4), np.uint8)
        nib[..., 0::2] = words & 0xF
        nib[..., 1::2] = words >> 4
        vals = E2M1[nib]
    vals = vals * np.repeat(np.exp2(scales.astype(np.float64) - 127.0), 8, axis=1)[..., None]
    return vals.transpose(0, 1, 3, 2).reshape(g * 512, n)


def gelu(v):
    return 0.5 * v * (1.0 + np.tanh(np.sqrt(2.0 / np.pi) * (v + 0.044715 * v**3)))


def striped8(idx):
    return np.concatenate([v.reshape(-1, 16).T for v in idx]).astype(np.uint16)


def unstriped8(offs):
    return np.stack([offs[16 * g:16 * g + 16].T.reshape(-1) for g in range(8)]).astype(np.int64)


def put_heads(h, wgs, idx8, t2):
    r = np.arange(h.shape[0])
    page = np.zeros((h.shape[0], t2))
    page[r[:, None], idx8[r % 512 // 64]] = wgs[r // 4 % 128] * h
    return page


def bf(x):
    return np.asarray(x, np.float32).astype(ml_dtypes.bfloat16)


def planes(Y):
    n, m = Y.shape
    b = f64(bf(Y)).reshape(n // 32, 32, m)
    amax = np.abs(b).max(1)
    byte = np.clip(np.where(amax > 0, np.frexp(amax)[1] - 1 + 127 - 7, 1), 1, 254)
    codes = (b * np.exp2(127.0 - byte)[:, None, :]).reshape(n, m).astype(np.float32).astype(ml_dtypes.float8_e4m3fn).view(np.uint8)
    words = codes.reshape(n // 512, 128, 4, m).transpose(0, 1, 3, 2)
    return np.ascontiguousarray(words), np.ascontiguousarray(byte.astype(np.uint8).reshape(n // 512, 16, m))


K, T, S, T2, H, N = 1024, 2048, 512, 1024, 1024, 1024

def setup_inputs():
    n = np.random.standard_normal
    s = mx_kscale(K)[:, None]
    u = mx_kscale(H)[:, None]
    tab_words, tab_scales = pack_weight(n((K, T)) * s, "e4m3")
    offs = striped(np.random.permutation(T)[:S])
    we = (n((K, H)) / np.sqrt(K) / s * u.T).astype(np.float32)
    wf_words, wf_scales = pack_weight(n((K, H)) / np.sqrt(K) / s, "e2m1")
    wgs = np.repeat(np.random.uniform(0.5, 2.0, (8, S)), 16, axis=0).astype(np.float32)
    offs2 = striped8(np.stack([np.random.permutation(T2)[:S] for _ in range(8)]))
    sp = (n((H, T2)) * u).astype(np.float32)
    wc_words, wc_scales = pack_weight(n((H, N)) / np.sqrt(H) / u * np.exp(0.8 * n(N)), "e4m3")
    return {"tab_words": tab_words, "tab_scales": tab_scales, "offs": offs,
            "we": we, "wf_words": wf_words, "wf_scales": wf_scales,
            "wgs": wgs, "offs2": offs2, "sp": sp,
            "wc_words": wc_words, "wc_scales": wc_scales}

def reference(tab_words, tab_scales, offs, we, wf_words, wf_scales, wgs, offs2, sp, wc_words, wc_scales):
    v = unpack_weight(tab_words, tab_scales, "e4m3")[:, unstriped(offs)]
    e = mxq(f64(we), 0, "e4m3").T @ v
    f = unpack_weight(wf_words, wf_scales, "e2m1").T @ v
    h = e * (1.0 - np.square(np.tanh(f)))
    page = put_heads(h, f64(wgs), unstriped8(offs2), T2)
    z = f64(sp) - page
    y = unpack_weight(wc_words, wc_scales, "e4m3").T @ mxq(z, 0, "e4m3")
    words, scales = planes(y)
    return y, words, scales

@@ -1,0 +1,320 @@
+from contextlib import ExitStack
+
+import concourse.mybir as mybir
+from concourse.masks import make_identity
+
+K, T, S, T2, H, N = 1024, 2048, 512, 1024, 1024, 1024
+FLOPS = 2 * K * H * S * 2 + 2 * H * N * T2
+
+F32 = mybir.dt.float32
+BF16 = mybir.dt.bfloat16
+I32 = mybir.dt.int32
+U32 = mybir.dt.uint32
+U16 = mybir.dt.uint16
+U8 = mybir.dt.uint8
+FP8X4 = mybir.dt.float8_e4m3fn_x4
+FP4X4 = mybir.dt.float4_e2m1fn_x4
+ADD = mybir.AluOpType.add
+MULT = mybir.AluOpType.mult
+TANH = mybir.ActivationFunctionType.Tanh
+SQUARE = mybir.ActivationFunctionType.Square
+
+P = 128
+PACK = 4
+KP = P * PACK
+BANK = 512
+
+
+def tile_list_headbox_setpoint_step_kernel(
+    tc, tab_words, tab_scales, offs, we, wf_words, wf_scales, wgs, offs2, sp, wc_words, wc_scales, out_0, out_1, out_2
+):
+    nc = tc.nc
+    with ExitStack() as ctx:
+        lists = ctx.enter_context(tc.tile_pool(name="lists", bufs=1))
+        sb = ctx.enter_context(tc.tile_pool(name="sb", bufs=1))
+        psum = ctx.enter_context(tc.psum_pool(name="psum", bufs=1))
+
+        def new(name, shape, dtype, tag=None):
+            return sb.tile([P] + shape, dtype, name=name, tag=tag or name, align_bytes=64)
+
+        banks = [psum.tile([P, BANK], F32, name=f"bank{u}") for u in range(8)]
+        low, high = banks[:4], banks[4:]
+
+        tab_s = new("tab_s", [2, T], U8)
+        wf_s = new("wf_s", [2, H], U8)
+        wc_s = new("wc_s", [N], U8)
+        nc.gpsimd.memset(tab_s[:].bitcast(I32), 0)
+        nc.vector.memset(wf_s[:].bitcast(I32), 0)
+        nc.vector.memset(wc_s[:].bitcast(I32), 0)
+
+        pick = lists.tile([P, S // 16], U16, name="pick")
+        place = lists.tile([P, S // 16], U16, name="place")
+        nc.sync.dma_start(pick[:], offs)
+
+        def load_words(tile_ap, words):
+            nc.sync.dma_start(tile_ap, words.rearrange("p c i -> p (c i)").bitcast(I32))
+
+        def load_planes(queue, plane, scales):
+            for q in range(4):
+                queue.dma_start(
+                    plane[32 * q : 32 * q + 4, :, :].bitcast(I32),
+                    scales[:, 4 * q : 4 * q + 4, :].rearrange("a r c -> r a c").bitcast(I32),
+                )
+
+        tab_w = [new(f"tab_w{a}", [T], I32) for a in range(2)]
+        nc.sync.dma_start(place[:], offs2)
+        load_words(tab_w[0][:], tab_words[0])
+        load_planes(nc.gpsimd, tab_s, tab_scales)
+        load_planes(nc.scalar, wf_s, wf_scales)
+        ident = new("ident", [P], F32)
+        make_identity(nc, ident[:])
+
+        def new_page(name, tag=None):
+            page = new(name, [T2], F32, tag=tag)
+            nc.gpsimd.memset(page[:], 0.0)
+            return page
+
+        pages = [[new_page(f"page0{i}") for i in range(PACK)]]
+
+        wf_w = [new(f"wf_w{b}", [2, 2 * KP], U8) for b in range(2)]
+
+        def load_wf(b):
+            nc.sync.dma_start(
+                wf_w[b][:].bitcast(I32),
+                wf_words[:, :, 2 * KP * b : 2 * KP * (b + 1)].rearrange("a p c -> p a c").bitcast(I32),
+            )
+
+        def load_we(name, a, c0, width):
+            raw = new(name, [PACK, width], F32)
+            nc.sync.dma_start(raw[:], we[KP * a : KP * (a + 1), c0 : c0 + width].rearrange("(p j) c -> p j c", j=PACK))
+            return raw
+
+        load_wf(0)
+        load_words(tab_w[1][:], tab_words[1])
+        we_raw = {(0, 0): [load_we("we00", 0, 0, KP)]}
+        we_raw[0, 1] = [load_we(f"we01{u}", 1, u * KP // 2, KP // 2) for u in range(2)]
+        step = new("step", [S], F32)
+        nc.sync.dma_start(step[:], wgs)
+        we_raw[1, 0] = [load_we("we10", 0, KP, KP)]
+        we_raw[1, 1] = [load_we("we11", 1, KP, KP)]
+        load_wf(1)
+
+        v_w = [new(f"v_w{a}", [S], U32) for a in range(2)]
+        v_s = [new(f"v_s{a}", [S], U8) for a in range(2)]
+        nc.vector.tensor_copy(v_w[0][:], tab_w[0][:].bitcast(U32).indirect(pick[:]))
+        for a in range(2):
+            nc.vector.tensor_copy(v_s[a][:], tab_s[:, a, :].indirect(pick[:]))
+        nc.vector.tensor_copy(v_w[1][:], tab_w[1][:].bitcast(U32).indirect(pick[:]))
+
+        def forward(b, group):
+            for a in range(2):
+                for jb in range(4):
+                    cols = slice(jb * P, (jb + 1) * P)
+                    nc.tensor.matmul_mx(
+                        group[jb][:],
+                        lhsT=v_w[a][:, cols].bitcast(FP8X4),
+                        lhsT_scale=v_s[a][:, cols],
+                        rhs=wf_w[b][:, a, :].bitcast(FP4X4),
+                        rhs_scale=wf_s[:, a, KP * b : KP * (b + 1)],
+                        start=(a == 0),
+                        stop=(a == 1),
+                    )
+            turned = []
+            for jb in range(4):
+                th = new(f"th{b}{jb}", [PACK, P], F32, tag=f"th{jb}")
+                nc.scalar.activation(th[:], group[jb][:].rearrange("j (p i) -> j i p", i=PACK), TANH)
+                turned.append(th)
+            return turned
+
+        def square(b, i, turned, bank):
+            for jb in range(4):
+                nc.tensor.transpose(bank[:, jb * P : (jb + 1) * P], turned[jb][:, i, :], ident[:])
+            sq = new(f"sq{b}{i}", [S], F32)
+            nc.scalar.activation(sq[:], bank[:], SQUARE)
+            return sq
+
+        def quantize_we(b, copy):
+            codes, scales = [], []
+            for a in range(2):
+                rounded = new(f"we_bf{b}{a}", [PACK * KP], BF16)
+                target = rounded[:].rearrange("p (i m j) -> p m j i", i=PACK, j=PACK)
+                m0 = 0
+                for raw in we_raw[b, a]:
+                    source = raw[:].rearrange("p j (m i) -> p m j i", i=PACK)
+                    count = source.shape[1]
+                    copy(target[:, m0 : m0 + count], source)
+                    m0 = m0 + count
+                c = new(f"we_c{b}{a}", [KP], U32)
+                s = new(f"we_s{b}{a}", [KP], U8)
+                for u in range(2):
+                    nc.vector.quantize_mx(
+                        c[:, u * 256 : (u + 1) * 256].bitcast(FP8X4),
+                        s[:, u * 256 : (u + 1) * 256],
+                        rounded[:, u * 1024 : (u + 1) * 1024],
+                    )
+                codes.append(c)
+                scales.append(s)
+            return codes, scales
+
+        def error(b, i, codes, scales, bank):
+            cols = slice(i * P, (i + 1) * P)
+            for a in range(2):
+                nc.tensor.matmul_mx(
+                    bank[:],
+                    lhsT=codes[a][:, cols].bitcast(FP8X4),
+                    lhsT_scale=scales[a][:, cols],
+                    rhs=v_w[a][:].bitcast(FP8X4),
+                    rhs_scale=v_s[a][:],
+                    start=(a == 0),
+                    stop=(a == 1),
+                )
+            e = new(f"e{b}{i}", [S], F32)
+            nc.scalar.copy(e[:], bank[:])
+            return e
+
+        def scatter(b, i, e, sq, factor):
+            nc.vector.scalar_tensor_tensor(factor[:], sq[:], -1.0, step[:], ADD, MULT)
+            nc.vector.tensor_tensor(pages[b][i][:].indirect(place[:]), e[:], factor[:], MULT)
+
+        turned = forward(0, low)
+        codes0, scales0 = quantize_we(0, nc.vector.tensor_copy)
+        sq0, e0 = [], []
+        for i in range(PACK):
+            sq0.append(square(0, i, turned, high[i]))
+            e0.append(error(0, i, codes0, scales0, low[i]))
+        for i in range(PACK - 1):
+            scatter(0, i, e0[i], sq0[i], sq0[i])
+        codes1, scales1 = quantize_we(1, nc.scalar.copy)
+        scatter(0, PACK - 1, e0[-1], sq0[-1], new("factor", [S], F32, tag="we_bf11"))
+        pages.append([new_page(f"page1{i}", tag) for i, tag in enumerate(("sq00", "e00", "sq01", "e01"))])
+        turned = forward(1, high)
+        sq1, e1 = [], []
+        for i in range(PACK):
+            sq1.append(square(1, i, turned, low[i]))
+            e1.append(error(1, i, codes1, scales1, high[i]))
+
+        sp_t = {}
+        for b, h, tag in ((0, 0, "sp00"), (0, 1, "sp01"), (1, 0, "we00"), (1, 1, "tab_w1")):
+            sp_t[b, h] = new(f"sp{b}{h}", [2, T2], F32, tag=tag)
+            rows = sp[KP * b : KP * (b + 1), :].rearrange("(p i) m -> p i m", i=PACK)
+            nc.sync.dma_start(sp_t[b, h][:], rows[:, 2 * h : 2 * h + 2, :])
+        for q in range(4):
+            nc.sync.dma_start(
+                wc_s[32 * q : 32 * q + 8, :].bitcast(I32), wc_scales[:, 4 * q : 4 * q + 4, :].bitcast(I32)
+            )
+        wc_w = new("wc_w", [2, N], I32, tag="tab_w0")
+        nc.sync.dma_start(wc_w[:], wc_words.rearrange("a p c i -> p a (c i)").bitcast(I32))
+
+        def add_turned(b, h, group, terms, quarters):
+            sources = [sp_t[b, h][:, e, :] for e in range(2)] + [pages[b][2 * h + e][:] for e in range(2)]
+            for u in terms:
+                for mq in quarters:
+                    view = group[mq][:].rearrange("m (mb e p) -> m mb e p", mb=2, e=2)
+                    for mb in range(2):
+                        c0 = (2 * mq + mb) * P
+                        nc.tensor.matmul(
+                            view[:, mb, u % 2, :],
+                            sources[u][:, c0 : c0 + P],
+                            ident[:],
+                            start=(u == 0 and mb == 0),
+                            stop=(u == 3 and mb == 1),
+                            is_transpose=True,
+                        )
+
+        def round_turned(h, group, z_turned, quarters):
+            for mq in quarters:
+                nc.scalar.copy(
+                    z_turned[mq][:, :, h, :].rearrange("m mb (p e) -> m mb p e", e=2),
+                    group[mq][:].rearrange("m (mb e p) -> m mb p e", mb=2, e=2),
+                )
+
+        def turn_back(halves, z_turned, group, quarters=range(4)):
+            for mq in quarters:
+                view = group[mq][:].rearrange("p (mb h m) -> p mb h m", mb=2, h=2)
+                words = z_turned[mq][:].bitcast(F32)
+                for mb in range(2):
+                    for h in range(2):
+                        nc.tensor.transpose(view[:, mb, h, :], words[:, mb, h, :], ident[:])
+                target = halves[mq // 2][:].bitcast(F32).rearrange("p (q mb m h) -> p q mb m h", q=2, mb=2, h=2)
+                nc.scalar.copy(target[:, mq % 2], view.rearrange("p mb h m -> p mb m h"))
+
+        z_bf = [[new(f"z_bf{b}{mh}", [BANK * PACK], BF16) for mh in range(2)] for b in range(2)]
+
+        zt0 = [new(f"zt0{mq}", [2, 2, 2 * P], BF16, tag=f"zt{mq}") for mq in range(4)]
+        for h, group in enumerate((low, high)):
+            add_turned(0, h, group, range(4), range(4))
+            round_turned(h, group, zt0, range(4))
+        turn_back(z_bf[0], zt0, low)
+        for i in range(PACK):
+            scatter(1, i, e1[i], sq1[i], sq1[i])
+        zt1 = [new(f"zt1{mq}", [2, 2, 2 * P], BF16, tag=f"zt{mq}") for mq in range(4)]
+        add_turned(1, 0, high, range(4), range(4))
+        round_turned(0, high, zt1, range(4))
+        add_turned(1, 1, low, range(3), range(4))
+
+        wc_dw = new("wc_dw", [2 * N], I32, tag="e13")
+        nc.vector.tensor_copy(
+            wc_dw[:].rearrange("p (g t n) -> p g n t", g=4, t=PACK),
+            wc_w[:].rearrange("p a (g n t) -> p (a g) n t", g=2, t=PACK),
+        )
+        wc_ds = new("wc_ds", [N], U8, tag="sq13")
+        nc.vector.tensor_copy(
+            wc_ds[:].rearrange("p (g t n) -> p g t n", g=2, t=PACK),
+            wc_s[:].rearrange("p (g n t) -> p g t n", g=2, t=PACK),
+        )
+
+        z_c = [new(f"z_c{b}", [T2], U32) for b in range(2)]
+        z_s = [new("z_s0", [T2], U8, tag="wc_s"), new("z_s1", [T2], U8)]
+
+        def quantize_z(b, mh):
+            cols = slice(mh * BANK, (mh + 1) * BANK)
+            nc.vector.quantize_mx(z_c[b][:, cols].bitcast(FP8X4), z_s[b][:, cols], z_bf[b][mh][:])
+
+        for mh in range(2):
+            quantize_z(0, mh)
+        for mh in range(2):
+            quarters = (2 * mh, 2 * mh + 1)
+            add_turned(1, 1, low, [3], quarters)
+            round_turned(1, low, zt1, quarters)
+            turn_back(z_bf[1], zt1, [banks[4], banks[5], banks[0], banks[1]], quarters)
+            quantize_z(1, mh)
+
+        groups = ([banks[6], banks[7], banks[2], banks[3]], [banks[4], banks[5], banks[0], banks[1]])
+        y_tags = ("we10", "we11", "sp00", "sp01")
+        for mh in range(2):
+            cols = slice(mh * BANK, (mh + 1) * BANK)
+            y_s = new(f"y_s{mh}", [2, BANK], U8)
+            for g in range(2):
+                y = new(f"y{mh}{g}", [PACK, BANK], F32, tag=y_tags[2 * mh + g])
+                rows = out_0[KP * g : KP * (g + 1), cols].rearrange("(p t) m -> p t m", t=PACK)
+                for t in range(PACK):
+                    c0 = KP * g + P * t
+                    for a in range(2):
+                        nc.tensor.matmul_mx(
+                            groups[g][t][:],
+                            lhsT=wc_dw[:, N * a + c0 : N * a + c0 + P].bitcast(FP8X4),
+                            lhsT_scale=wc_ds[4 * a :, c0 : c0 + P],
+                            rhs=z_c[a][:, cols].bitcast(FP8X4),
+                            rhs_scale=z_s[a][:, cols],
+                            start=(a == 0),
+                            stop=(a == 1),
+                        )
+                    nc.scalar.copy(y[:, t, :], groups[g][t][:])
+                    run = 1 if (mh, g) == (0, 0) else 2
+                    if (t + 1) % run == 0:
+                        nc.sync.dma_start(rows[:, t + 1 - run : t + 1, :], y[:, t + 1 - run : t + 1, :])
+                y_bf = new(f"y_bf{mh}{g}", [BANK * PACK], BF16, tag=f"we_bf0{g}")
+                nc.vector.tensor_copy(
+                    y_bf[:].rearrange("p (c i t) -> p c t i", i=4, t=PACK),
+                    y[:].rearrange("p t (c i) -> p c t i", i=4),
+                )
+                y_c = new(f"y_c{mh}{g}", [BANK], U32)
+                nc.vector.quantize_mx(y_c[:].bitcast(FP8X4), y_s[:, g, :], y_bf[:])
+                nc.sync.dma_start(
+                    out_1[g, :, cols, :].rearrange("p m t -> p (m t)").bitcast(I32), y_c[:].bitcast(I32)
+                )
+            for q in range(4):
+                nc.sync.dma_start(
+                    out_2[:, 4 * q : 4 * q + 4, cols].rearrange("g r m -> r g m").bitcast(I32),
+                    y_s[32 * q : 32 * q + 4, :, :].bitcast(I32),
+                )

@@ -18,6 +18,7 @@ ADD = mybir.AluOpType.add
 MULT = mybir.AluOpType.mult
 TANH = mybir.ActivationFunctionType.Tanh
 SQUARE = mybir.ActivationFunctionType.Square
+IDENTITY = mybir.ActivationFunctionType.Identity
 
 P = 128
 PACK = 4
@@ -41,41 +42,38 @@ def tile_list_headbox_setpoint_step_kernel(
         low, high = banks[:4], banks[4:]
 
         tab_s = new("tab_s", [2, T], U8)
-        wf_s = new("wf_s", [2, H], U8)
+        wf_s = [new(f"wf_s{b}", [2, KP], U8) for b in range(2)]
         wc_s = new("wc_s", [N], U8)
-        nc.gpsimd.memset(tab_s[:].bitcast(I32), 0)
-        nc.vector.memset(wf_s[:].bitcast(I32), 0)
-        nc.vector.memset(wc_s[:].bitcast(I32), 0)
+        nc.vector.memset(tab_s[:].bitcast(I32), 0)
+        pages = [new(f"page{u}", [T2], F32) for u in range(3)]
+        for plane in (wf_s[0], wf_s[1], wc_s):
+            nc.gpsimd.memset(plane[:].bitcast(I32), 0)
+        nc.gpsimd.memset(pages[2][:], 0.0)
+        for page in pages[:2]:
+            nc.vector.memset(page[:], 0.0)
+        ident = new("ident", [P], F32)
+        make_identity(nc, ident[:])
 
         pick = lists.tile([P, S // 16], U16, name="pick")
         place = lists.tile([P, S // 16], U16, name="place")
-        nc.sync.dma_start(pick[:], offs)
 
         def load_words(tile_ap, words):
             nc.sync.dma_start(tile_ap, words.rearrange("p c i -> p (c i)").bitcast(I32))
 
-        def load_planes(queue, plane, scales):
+        def load_rows(rows, scales):
             for q in range(4):
-                queue.dma_start(
-                    plane[32 * q : 32 * q + 4, :, :].bitcast(I32),
+                nc.sync.dma_start(
+                    rows[32 * q : 32 * q + 4, :, :].bitcast(I32),
                     scales[:, 4 * q : 4 * q + 4, :].rearrange("a r c -> r a c").bitcast(I32),
                 )
+            return rows
+
+        def fill_plane(engine, plane, rows):
+            for q in range(4):
+                live = slice(32 * q, 32 * q + 4)
+                engine.tensor_copy(plane[live, :, :].bitcast(I32), rows[live, :, :].bitcast(I32))
 
         tab_w = [new(f"tab_w{a}", [T], I32) for a in range(2)]
-        nc.sync.dma_start(place[:], offs2)
-        load_words(tab_w[0][:], tab_words[0])
-        load_planes(nc.gpsimd, tab_s, tab_scales)
-        load_planes(nc.scalar, wf_s, wf_scales)
-        ident = new("ident", [P], F32)
-        make_identity(nc, ident[:])
-
-        def new_page(name, tag=None):
-            page = new(name, [T2], F32, tag=tag)
-            nc.gpsimd.memset(page[:], 0.0)
-            return page
-
-        pages = [[new_page(f"page0{i}") for i in range(PACK)]]
-
         wf_w = [new(f"wf_w{b}", [2, 2 * KP], U8) for b in range(2)]
 
         def load_wf(b):
@@ -84,29 +82,49 @@ def tile_list_headbox_setpoint_step_kernel(
                 wf_words[:, :, 2 * KP * b : 2 * KP * (b + 1)].rearrange("a p c -> p a c").bitcast(I32),
             )
 
-        def load_we(name, a, c0, width):
-            raw = new(name, [PACK, width], F32)
+        def load_we(name, a, c0, width, tag=None):
+            raw = new(name, [PACK, width], F32, tag=tag)
             nc.sync.dma_start(raw[:], we[KP * a : KP * (a + 1), c0 : c0 + width].rearrange("(p j) c -> p j c", j=PACK))
             return raw
 
+        nc.sync.dma_start(pick[:], offs)
+        tab_rows = load_rows(new("tab_rows", [2, T], U8), tab_scales)
+        load_words(tab_w[0][:], tab_words[0])
         load_wf(0)
+        wf_rows = load_rows(new("wf_rows", [2, KP], U8), wf_scales[:, :, :KP])
         load_words(tab_w[1][:], tab_words[1])
         we_raw = {(0, 0): [load_we("we00", 0, 0, KP)]}
         we_raw[0, 1] = [load_we(f"we01{u}", 1, u * KP // 2, KP // 2) for u in range(2)]
         step = new("step", [S], F32)
         nc.sync.dma_start(step[:], wgs)
-        we_raw[1, 0] = [load_we("we10", 0, KP, KP)]
-        we_raw[1, 1] = [load_we("we11", 1, KP, KP)]
+        nc.sync.dma_start(place[:], offs2)
         load_wf(1)
+        load_rows(wf_s[1], wf_scales[:, :, KP:])
+        for q in range(4):
+            nc.sync.dma_start(
+                wc_s[32 * q : 32 * q + 8, :].bitcast(I32), wc_scales[:, 4 * q : 4 * q + 4, :].bitcast(I32)
+            )
+        sp_t = {}
+
+        def load_sp(b, h, tag):
+            sp_t[b, h] = new(f"sp{b}{h}", [2, T2], F32, tag=tag)
+            rows = sp[KP * b : KP * (b + 1), :].rearrange("(p i) m -> p i m", i=PACK)
+            nc.sync.dma_start(sp_t[b, h][:], rows[:, 2 * h : 2 * h + 2, :])
 
         v_w = [new(f"v_w{a}", [S], U32) for a in range(2)]
         v_s = [new(f"v_s{a}", [S], U8) for a in range(2)]
+        fill_plane(nc.vector, tab_s, tab_rows)
+        nc.vector.tensor_copy(v_s[0][:], tab_s[:, 0, :].indirect(pick[:]))
         nc.vector.tensor_copy(v_w[0][:], tab_w[0][:].bitcast(U32).indirect(pick[:]))
+        fill_plane(nc.gpsimd, wf_s[0], wf_rows)
+        nc.vector.tensor_copy(v_s[1][:], tab_s[:, 1, :].indirect(pick[:]))
+        for u in range(2):
+            entries = pick[:, u * 16 : (u + 1) * 16]
+            nc.vector.tensor_copy(v_w[1][:, u * 256 : (u + 1) * 256], tab_w[1][:].bitcast(U32).indirect(entries))
         for a in range(2):
-            nc.vector.tensor_copy(v_s[a][:], tab_s[:, a, :].indirect(pick[:]))
-        nc.vector.tensor_copy(v_w[1][:], tab_w[1][:].bitcast(U32).indirect(pick[:]))
+            we_raw[1, a] = [load_we(f"we1{a}", a, KP, KP, f"tab_w{a}")]
 
-        def forward(b, group):
+        def forward(b, group, parts, tag):
             for a in range(2):
                 for jb in range(4):
                     cols = slice(jb * P, (jb + 1) * P)
@@ -115,35 +133,34 @@ def tile_list_headbox_setpoint_step_kernel(
                         lhsT=v_w[a][:, cols].bitcast(FP8X4),
                         lhsT_scale=v_s[a][:, cols],
                         rhs=wf_w[b][:, a, :].bitcast(FP4X4),
-                        rhs_scale=wf_s[:, a, KP * b : KP * (b + 1)],
+                        rhs_scale=wf_s[b][:, a, :],
                         start=(a == 0),
                         stop=(a == 1),
                     )
-            turned = []
-            for jb in range(4):
-                th = new(f"th{b}{jb}", [PACK, P], F32, tag=f"th{jb}")
-                nc.scalar.activation(th[:], group[jb][:].rearrange("j (p i) -> j i p", i=PACK), TANH)
-                turned.append(th)
+            turned = new(f"th{b}", [4, PACK, P], F32, tag=tag)
+            for part in parts:
+                for jb in range(4):
+                    source = group[jb][:].rearrange("j (p i) -> j i p", i=PACK)
+                    nc.scalar.activation(turned[:, jb, part, :], source[:, part, :], TANH)
             return turned
 
         def square(b, i, turned, bank):
             for jb in range(4):
-                nc.tensor.transpose(bank[:, jb * P : (jb + 1) * P], turned[jb][:, i, :], ident[:])
+                nc.tensor.transpose(bank[:, jb * P : (jb + 1) * P], turned[:, jb, i, :], ident[:])
             sq = new(f"sq{b}{i}", [S], F32)
             nc.scalar.activation(sq[:], bank[:], SQUARE)
             return sq
 
-        def quantize_we(b, copy):
+        def quantize_we(b, copies):
             codes, scales = [], []
             for a in range(2):
                 rounded = new(f"we_bf{b}{a}", [PACK * KP], BF16)
-                target = rounded[:].rearrange("p (i m j) -> p m j i", i=PACK, j=PACK)
-                m0 = 0
-                for raw in we_raw[b, a]:
-                    source = raw[:].rearrange("p j (m i) -> p m j i", i=PACK)
-                    count = source.shape[1]
-                    copy(target[:, m0 : m0 + count], source)
-                    m0 = m0 + count
+                raws = we_raw[b, a]
+                count = P // len(copies[a])
+                for u, (copy, walk) in enumerate(copies[a]):
+                    source = raws[u][:].rearrange(f"p j (m i) -> p {walk}", i=PACK)
+                    target = rounded[:].rearrange("p (i m j) -> p i m j", i=PACK, j=PACK)
+                    copy(target[:, :, u * count : (u + 1) * count].rearrange(f"p i m j -> p {walk}"), source)
                 c = new(f"we_c{b}{a}", [KP], U32)
                 s = new(f"we_s{b}{a}", [KP], U8)
                 for u in range(2):
@@ -168,45 +185,53 @@ def tile_list_headbox_setpoint_step_kernel(
                     start=(a == 0),
                     stop=(a == 1),
                 )
+
+        z_bf = [[new(f"z_bf{b}{mh}", [BANK * PACK], BF16) for mh in range(2)] for b in range(2)]
+        on_scalar, on_vector = (nc.scalar.copy, "m j i"), (nc.vector.tensor_copy, "m j i")
+
+        def prepare(b, i, codes, scales, turned, square_bank, error_bank):
+            sq = square(b, i, turned, square_bank)
+            if b == 1:
+                nc.scalar.activation(sq[:], sq[:], IDENTITY, bias=-1.0)
+            error(b, i, codes, scales, error_bank)
             e = new(f"e{b}{i}", [S], F32)
-            nc.scalar.copy(e[:], bank[:])
-            return e
+            nc.scalar.copy(e[:], error_bank[:])
+            return sq, e
 
-        def scatter(b, i, e, sq, factor):
+        def scatter(page, sq, e, factor):
             nc.vector.scalar_tensor_tensor(factor[:], sq[:], -1.0, step[:], ADD, MULT)
-            nc.vector.tensor_tensor(pages[b][i][:].indirect(place[:]), e[:], factor[:], MULT)
+            nc.vector.tensor_tensor(page[:].indirect(place[:]), e[:], factor[:], MULT)
 
-        turned = forward(0, low)
-        codes0, scales0 = quantize_we(0, nc.vector.tensor_copy)
-        sq0, e0 = [], []
-        for i in range(PACK):
-            sq0.append(square(0, i, turned, high[i]))
-            e0.append(error(0, i, codes0, scales0, low[i]))
-        for i in range(PACK - 1):
-            scatter(0, i, e0[i], sq0[i], sq0[i])
-        codes1, scales1 = quantize_we(1, nc.scalar.copy)
-        scatter(0, PACK - 1, e0[-1], sq0[-1], new("factor", [S], F32, tag="we_bf11"))
-        pages.append([new_page(f"page1{i}", tag) for i, tag in enumerate(("sq00", "e00", "sq01", "e01"))])
-        turned = forward(1, high)
-        sq1, e1 = [], []
-        for i in range(PACK):
-            sq1.append(square(1, i, turned, low[i]))
-            e1.append(error(1, i, codes1, scales1, high[i]))
-
-        sp_t = {}
-        for b, h, tag in ((0, 0, "sp00"), (0, 1, "sp01"), (1, 0, "we00"), (1, 1, "tab_w1")):
-            sp_t[b, h] = new(f"sp{b}{h}", [2, T2], F32, tag=tag)
-            rows = sp[KP * b : KP * (b + 1), :].rearrange("(p i) m -> p i m", i=PACK)
-            nc.sync.dma_start(sp_t[b, h][:], rows[:, 2 * h : 2 * h + 2, :])
-        for q in range(4):
-            nc.sync.dma_start(
-                wc_s[32 * q : 32 * q + 8, :].bitcast(I32), wc_scales[:, 4 * q : 4 * q + 4, :].bitcast(I32)
-            )
-        wc_w = new("wc_w", [2, N], I32, tag="tab_w0")
+        codes0, scales0 = quantize_we(0, ((on_scalar,), (on_vector, on_vector)))
+        pages.append(new("page3", [T2], F32, tag="we_bf01"))
+        nc.gpsimd.memset(pages[3][:], 0.0)
+        load_sp(0, 0, "we010")
+        load_sp(0, 1, "we011")
+        wc_w = new("wc_w", [2, N], I32, tag="we_bf00")
         nc.sync.dma_start(wc_w[:], wc_words.rearrange("a p c i -> p a (c i)").bitcast(I32))
+        turned = forward(0, low, (slice(0, 1), slice(1, PACK)), "we00")
+        for i in range(PACK):
+            sq, e = prepare(0, i, codes0, scales0, turned, high[i], ([high[3]] + low)[i])
+            if i < PACK - 1:
+                scatter(pages[i], sq, e, sq)
+        load_sp(1, 0, "we00")
+        codes1, scales1 = quantize_we(1, ((on_scalar,), (on_scalar,)))
+        load_sp(1, 1, "tab_w0")
+        factor = new("factor", [S], F32, tag="we_bf11")
+        nc.vector.scalar_tensor_tensor(factor[:], sq[:], -1.0, step[:], ADD, MULT)
+        nc.vector.tensor_tensor(sq[:], e[:], factor[:], MULT)
+        nc.vector.tensor_copy(pages[3][:].indirect(place[:]), sq[:])
+        turned = forward(1, high, (slice(0, PACK),), "tab_w1")
+        ready = []
+        for i in range(PACK):
+            sq, e = prepare(1, i, codes1, scales1, turned, high[i], high[i])
+            factor = new(f"factor{i}", [S], F32, tag="e03")
+            nc.gpsimd.tensor_tensor(factor[:], sq[:], step[:], MULT)
+            nc.gpsimd.tensor_tensor(sq[:], e[:], factor[:], MULT)
+            ready.append(sq)
 
-        def add_turned(b, h, group, terms, quarters):
-            sources = [sp_t[b, h][:, e, :] for e in range(2)] + [pages[b][2 * h + e][:] for e in range(2)]
+        def add_turned(b, h, group, terms, quarters, first, last):
+            sources = [sp_t[b, h][:, e, :] for e in range(2)] + [pages[2 * h + e][:] for e in range(2)]
             for u in terms:
                 for mq in quarters:
                     view = group[mq][:].rearrange("m (mb e p) -> m mb e p", mb=2, e=2)
@@ -216,8 +241,8 @@ def tile_list_headbox_setpoint_step_kernel(
                             view[:, mb, u % 2, :],
                             sources[u][:, c0 : c0 + P],
                             ident[:],
-                            start=(u == 0 and mb == 0),
-                            stop=(u == 3 and mb == 1),
+                            start=(u == first and mb == 0),
+                            stop=(u == last and mb == 1),
                             is_transpose=True,
                         )
 
@@ -228,41 +253,42 @@ def tile_list_headbox_setpoint_step_kernel(
                     group[mq][:].rearrange("m (mb e p) -> m mb p e", mb=2, e=2),
                 )
 
-        def turn_back(halves, z_turned, group, quarters=range(4)):
+        def turn_back(halves, z_turned, group, quarters, copies):
             for mq in quarters:
                 view = group[mq][:].rearrange("p (mb h m) -> p mb h m", mb=2, h=2)
-                words = z_turned[mq][:].bitcast(F32)
+                words = z_turned[mq].bitcast(F32)
                 for mb in range(2):
                     for h in range(2):
                         nc.tensor.transpose(view[:, mb, h, :], words[:, mb, h, :], ident[:])
                 target = halves[mq // 2][:].bitcast(F32).rearrange("p (q mb m h) -> p q mb m h", q=2, mb=2, h=2)
-                nc.scalar.copy(target[:, mq % 2], view.rearrange("p mb h m -> p mb m h"))
+                copies[mq](target[:, mq % 2], view.rearrange("p mb h m -> p mb m h"))
 
-        z_bf = [[new(f"z_bf{b}{mh}", [BANK * PACK], BF16) for mh in range(2)] for b in range(2)]
-
-        zt0 = [new(f"zt0{mq}", [2, 2, 2 * P], BF16, tag=f"zt{mq}") for mq in range(4)]
-        for h, group in enumerate((low, high)):
-            add_turned(0, h, group, range(4), range(4))
-            round_turned(h, group, zt0, range(4))
-        turn_back(z_bf[0], zt0, low)
-        for i in range(PACK):
-            scatter(1, i, e1[i], sq1[i], sq1[i])
-        zt1 = [new(f"zt1{mq}", [2, 2, 2 * P], BF16, tag=f"zt{mq}") for mq in range(4)]
-        add_turned(1, 0, high, range(4), range(4))
+        zt_half = [new(f"zt{mh}", [2, 2, 2, 2 * P], BF16, tag=f"we_c1{mh}") for mh in range(2)]
+        zt0 = [zt_half[mq // 2][:, mq % 2] for mq in range(4)]
+        add_turned(0, 0, low, (0, 1, 2, 3), range(4), 0, 3)
+        round_turned(0, low, zt0, range(4))
+        add_turned(0, 1, high, (2, 3, 0, 1), range(4), 2, 1)
+        round_turned(1, high, zt0, range(4))
+        turn_back(z_bf[0], zt0, low, range(4), (nc.scalar.copy,) * 4)
+        for i in range(2):
+            nc.vector.tensor_copy(pages[i][:].indirect(place[:]), ready[i][:])
+        zt1 = [new(f"zt1{mq}", [2, 2, 2 * P], BF16)[:] for mq in range(4)]
+        add_turned(1, 0, high, (0, 1, 2, 3), range(4), 0, 3)
         round_turned(0, high, zt1, range(4))
-        add_turned(1, 1, low, range(3), range(4))
+        for i in range(2, PACK):
+            nc.vector.tensor_copy(pages[i][:].indirect(place[:]), ready[i][:])
+        add_turned(1, 1, low, (0, 1, 2), range(4), 0, 3)
 
         wc_dw = new("wc_dw", [2 * N], I32, tag="e13")
-        nc.vector.tensor_copy(
-            wc_dw[:].rearrange("p (g t n) -> p g n t", g=4, t=PACK),
-            wc_w[:].rearrange("p a (g n t) -> p (a g) n t", g=2, t=PACK),
+        nc.gpsimd.tensor_copy(
+            wc_dw[:].rearrange("p (g t n) -> p g t n", g=4, t=PACK),
+            wc_w[:].rearrange("p a (g n t) -> p (a g) t n", g=2, t=PACK),
         )
         wc_ds = new("wc_ds", [N], U8, tag="sq13")
         nc.vector.tensor_copy(
             wc_ds[:].rearrange("p (g t n) -> p g t n", g=2, t=PACK),
             wc_s[:].rearrange("p (g n t) -> p g t n", g=2, t=PACK),
         )
-
         z_c = [new(f"z_c{b}", [T2], U32) for b in range(2)]
         z_s = [new("z_s0", [T2], U8, tag="wc_s"), new("z_s1", [T2], U8)]
 
@@ -274,47 +300,55 @@ def tile_list_headbox_setpoint_step_kernel(
             quantize_z(0, mh)
         for mh in range(2):
             quarters = (2 * mh, 2 * mh + 1)
-            add_turned(1, 1, low, [3], quarters)
+            add_turned(1, 1, low, (3,), quarters, 0, 3)
             round_turned(1, low, zt1, quarters)
-            turn_back(z_bf[1], zt1, [banks[4], banks[5], banks[0], banks[1]], quarters)
+            turn_back(z_bf[1], zt1, [high[0], high[1], low[0], low[1]], quarters, (nc.scalar.copy,) + (nc.vector.tensor_copy,) * 3)
             quantize_z(1, mh)
 
-        groups = ([banks[6], banks[7], banks[2], banks[3]], [banks[4], banks[5], banks[0], banks[1]])
-        y_tags = ("we10", "we11", "sp00", "sp01")
-        for mh in range(2):
-            cols = slice(mh * BANK, (mh + 1) * BANK)
-            y_s = new(f"y_s{mh}", [2, BANK], U8)
-            for g in range(2):
-                y = new(f"y{mh}{g}", [PACK, BANK], F32, tag=y_tags[2 * mh + g])
-                rows = out_0[KP * g : KP * (g + 1), cols].rearrange("(p t) m -> p t m", t=PACK)
-                for t in range(PACK):
-                    c0 = KP * g + P * t
-                    for a in range(2):
-                        nc.tensor.matmul_mx(
-                            groups[g][t][:],
-                            lhsT=wc_dw[:, N * a + c0 : N * a + c0 + P].bitcast(FP8X4),
-                            lhsT_scale=wc_ds[4 * a :, c0 : c0 + P],
-                            rhs=z_c[a][:, cols].bitcast(FP8X4),
-                            rhs_scale=z_s[a][:, cols],
-                            start=(a == 0),
-                            stop=(a == 1),
-                        )
-                    nc.scalar.copy(y[:, t, :], groups[g][t][:])
-                    run = 1 if (mh, g) == (0, 0) else 2
-                    if (t + 1) % run == 0:
-                        nc.sync.dma_start(rows[:, t + 1 - run : t + 1, :], y[:, t + 1 - run : t + 1, :])
-                y_bf = new(f"y_bf{mh}{g}", [BANK * PACK], BF16, tag=f"we_bf0{g}")
-                nc.vector.tensor_copy(
-                    y_bf[:].rearrange("p (c i t) -> p c t i", i=4, t=PACK),
-                    y[:].rearrange("p t (c i) -> p c t i", i=4),
-                )
-                y_c = new(f"y_c{mh}{g}", [BANK], U32)
-                nc.vector.quantize_mx(y_c[:].bitcast(FP8X4), y_s[:, g, :], y_bf[:])
-                nc.sync.dma_start(
-                    out_1[g, :, cols, :].rearrange("p m t -> p (m t)").bitcast(I32), y_c[:].bitcast(I32)
-                )
-            for q in range(4):
-                nc.sync.dma_start(
-                    out_2[:, 4 * q : 4 * q + 4, cols].rearrange("g r m -> r g m").bitcast(I32),
-                    y_s[32 * q : 32 * q + 4, :, :].bitcast(I32),
-                )
+        groups = ([high[2], high[3], low[2], low[3]], [high[0], high[1], low[0], low[1]])
+        y_s = [new(f"y_s{mh}", [2, BANK], U8) for mh in range(2)]
+        units = ((0, 0, BANK, "we010"), (1, 0, BANK, "tab_w1"), (0, BANK, BANK, "we00"))
+        units = units + ((1, BANK, BANK // 2, "we011"), (1, BANK + BANK // 2, BANK // 2, "tab_w0"))
+
+        def last_pass(u, t, a):
+            g, m0, width, tag = units[u]
+            c0 = KP * g + P * t
+            nc.tensor.matmul_mx(
+                groups[u % 2][t][:, :width],
+                lhsT=wc_dw[:, N * a + c0 : N * a + c0 + P].bitcast(FP8X4),
+                lhsT_scale=wc_ds[4 * a :, c0 : c0 + P],
+                rhs=z_c[a][:, m0 : m0 + width].bitcast(FP8X4),
+                rhs_scale=z_s[a][:, m0 : m0 + width],
+                start=(a == 0),
+                stop=(a == 1),
+            )
+
+        for u, (g, m0, width, tag) in enumerate(units):
+            cols = slice(m0, m0 + width)
+            y = new(f"y{u}", [PACK, width], F32, tag=tag)
+            rows = out_0[KP * g : KP * (g + 1), cols].rearrange("(p t) m -> p t m", t=PACK)
+            run = (1, 2, 2, 4, 4)[u]
+            for t in range(PACK):
+                bank = groups[u % 2][t]
+                for a in range(2):
+                    last_pass(u, t, a)
+                copy = nc.vector.tensor_copy if (u, t) == (0, PACK - 1) else nc.scalar.copy
+                copy(y[:, t, :], bank[:, :width])
+                if (t + 1) % run == 0:
+                    nc.sync.dma_start(rows[:, t + 1 - run : t + 1, :], y[:, t + 1 - run : t + 1, :])
+            y_bf = new(f"y_bf{u}", [width * PACK], BF16, tag=f"we_bf0{u % 2}")
+            nc.vector.tensor_copy(
+                y_bf[:].rearrange("p (c i t) -> p c t i", i=4, t=PACK),
+                y[:].rearrange("p t (c i) -> p c t i", i=4),
+            )
+            y_c = new(f"y_c{u}", [width], U32)
+            plane = y_s[m0 // BANK]
+            nc.vector.quantize_mx(y_c[:].bitcast(FP8X4), plane[:, g, m0 % BANK : m0 % BANK + width], y_bf[:])
+            nc.sync.dma_start(out_1[g, :, cols, :].rearrange("p m t -> p (m t)").bitcast(I32), y_c[:].bitcast(I32))
+            if g == 1 and (m0 + width) % BANK == 0:
+                half = slice(m0 + width - BANK, m0 + width)
+                for q in range(4):
+                    nc.sync.dma_start(
+                        out_2[:, 4 * q : 4 * q + 4, half].rearrange("g r m -> r g m").bitcast(I32),
+                        plane[32 * q : 32 * q + 4, :, :].bitcast(I32),
+                    )

@@ -39,18 +39,16 @@ def tile_list_headbox_setpoint_step_kernel(
             return sb.tile([P] + shape, dtype, name=name, tag=tag or name, align_bytes=64)
 
         banks = [psum.tile([P, BANK], F32, name=f"bank{u}") for u in range(8)]
-        low, high = banks[:4], banks[4:]
 
         tab_s = new("tab_s", [2, T], U8)
-        wf_s = [new(f"wf_s{b}", [2, KP], U8) for b in range(2)]
+        wf_s = new("wf_s", [2, H], U8)
         wc_s = new("wc_s", [N], U8)
         nc.vector.memset(tab_s[:].bitcast(I32), 0)
-        pages = [new(f"page{u}", [T2], F32) for u in range(3)]
-        for plane in (wf_s[0], wf_s[1], wc_s):
+        for plane in (wf_s, wc_s):
             nc.gpsimd.memset(plane[:].bitcast(I32), 0)
-        nc.gpsimd.memset(pages[2][:], 0.0)
-        for page in pages[:2]:
-            nc.vector.memset(page[:], 0.0)
+        pages = [new(f"page{u}", [T2], F32) for u in range(6)]
+        for page in pages:
+            nc.gpsimd.memset(page[:], 0.0)
         ident = new("ident", [P], F32)
         make_identity(nc, ident[:])
 
@@ -66,12 +64,17 @@ def tile_list_headbox_setpoint_step_kernel(
                     rows[32 * q : 32 * q + 4, :, :].bitcast(I32),
                     scales[:, 4 * q : 4 * q + 4, :].rearrange("a r c -> r a c").bitcast(I32),
                 )
-            return rows
 
-        def fill_plane(engine, plane, rows):
-            for q in range(4):
-                live = slice(32 * q, 32 * q + 4)
-                engine.tensor_copy(plane[live, :, :].bitcast(I32), rows[live, :, :].bitcast(I32))
+        def load_we(name, a, c0, width):
+            raw = new(name, [PACK, width], F32)
+            nc.sync.dma_start(raw[:], we[KP * a : KP * (a + 1), c0 : c0 + width].rearrange("(p j) c -> p j c", j=PACK))
+            return raw
+
+        def load_sp(b, h, tag):
+            rows = new(f"sp{b}{h}", [2, T2], F32, tag=tag)
+            source = sp[KP * b : KP * (b + 1), :].rearrange("(p i) m -> p i m", i=PACK)
+            nc.sync.dma_start(rows[:], source[:, 2 * h : 2 * h + 2, :])
+            return rows
 
         tab_w = [new(f"tab_w{a}", [T], I32) for a in range(2)]
         wf_w = [new(f"wf_w{b}", [2, 2 * KP], U8) for b in range(2)]
@@ -82,260 +85,300 @@ def tile_list_headbox_setpoint_step_kernel(
                 wf_words[:, :, 2 * KP * b : 2 * KP * (b + 1)].rearrange("a p c -> p a c").bitcast(I32),
             )
 
-        def load_we(name, a, c0, width, tag=None):
-            raw = new(name, [PACK, width], F32, tag=tag)
-            nc.sync.dma_start(raw[:], we[KP * a : KP * (a + 1), c0 : c0 + width].rearrange("(p j) c -> p j c", j=PACK))
-            return raw
-
         nc.sync.dma_start(pick[:], offs)
-        tab_rows = load_rows(new("tab_rows", [2, T], U8), tab_scales)
+        load_rows(tab_s, tab_scales)
         load_words(tab_w[0][:], tab_words[0])
         load_wf(0)
-        wf_rows = load_rows(new("wf_rows", [2, KP], U8), wf_scales[:, :, :KP])
+        load_rows(wf_s, wf_scales)
         load_words(tab_w[1][:], tab_words[1])
         we_raw = {(0, 0): [load_we("we00", 0, 0, KP)]}
         we_raw[0, 1] = [load_we(f"we01{u}", 1, u * KP // 2, KP // 2) for u in range(2)]
+        load_wf(1)
         step = new("step", [S], F32)
         nc.sync.dma_start(step[:], wgs)
         nc.sync.dma_start(place[:], offs2)
-        load_wf(1)
-        load_rows(wf_s[1], wf_scales[:, :, KP:])
+        for a in range(2):
+            we_raw[1, a] = [load_we(f"we1{a}", a, KP, KP)]
+        sp_t = {(0, h): load_sp(0, h, None) for h in range(2)}
+        wc_w = new("wc_w", [2, N], I32)
+        nc.sync.dma_start(wc_w[:], wc_words.rearrange("a p c i -> p a (c i)").bitcast(I32))
         for q in range(4):
             nc.sync.dma_start(
                 wc_s[32 * q : 32 * q + 8, :].bitcast(I32), wc_scales[:, 4 * q : 4 * q + 4, :].bitcast(I32)
             )
-        sp_t = {}
-
-        def load_sp(b, h, tag):
-            sp_t[b, h] = new(f"sp{b}{h}", [2, T2], F32, tag=tag)
-            rows = sp[KP * b : KP * (b + 1), :].rearrange("(p i) m -> p i m", i=PACK)
-            nc.sync.dma_start(sp_t[b, h][:], rows[:, 2 * h : 2 * h + 2, :])
 
         v_w = [new(f"v_w{a}", [S], U32) for a in range(2)]
         v_s = [new(f"v_s{a}", [S], U8) for a in range(2)]
-        fill_plane(nc.vector, tab_s, tab_rows)
-        nc.vector.tensor_copy(v_s[0][:], tab_s[:, 0, :].indirect(pick[:]))
         nc.vector.tensor_copy(v_w[0][:], tab_w[0][:].bitcast(U32).indirect(pick[:]))
-        fill_plane(nc.gpsimd, wf_s[0], wf_rows)
-        nc.vector.tensor_copy(v_s[1][:], tab_s[:, 1, :].indirect(pick[:]))
-        for u in range(2):
-            entries = pick[:, u * 16 : (u + 1) * 16]
-            nc.vector.tensor_copy(v_w[1][:, u * 256 : (u + 1) * 256], tab_w[1][:].bitcast(U32).indirect(entries))
         for a in range(2):
-            we_raw[1, a] = [load_we(f"we1{a}", a, KP, KP, f"tab_w{a}")]
+            nc.vector.tensor_copy(v_s[a][:], tab_s[:, a, :].indirect(pick[:]))
+        nc.vector.tensor_copy(v_w[1][:], tab_w[1][:].bitcast(U32).indirect(pick[:]))
+        for h in range(2):
+            sp_t[1, h] = load_sp(1, h, f"tab_w{h}")
 
-        def forward(b, group, parts, tag):
-            for a in range(2):
-                for jb in range(4):
-                    cols = slice(jb * P, (jb + 1) * P)
-                    nc.tensor.matmul_mx(
-                        group[jb][:],
-                        lhsT=v_w[a][:, cols].bitcast(FP8X4),
-                        lhsT_scale=v_s[a][:, cols],
-                        rhs=wf_w[b][:, a, :].bitcast(FP4X4),
-                        rhs_scale=wf_s[b][:, a, :],
-                        start=(a == 0),
-                        stop=(a == 1),
-                    )
-            turned = new(f"th{b}", [4, PACK, P], F32, tag=tag)
-            for part in parts:
-                for jb in range(4):
-                    source = group[jb][:].rearrange("j (p i) -> j i p", i=PACK)
-                    nc.scalar.activation(turned[:, jb, part, :], source[:, part, :], TANH)
-            return turned
+        wf_dw, wf_ds = [], []
 
-        def square(b, i, turned, bank):
-            for jb in range(4):
-                nc.tensor.transpose(bank[:, jb * P : (jb + 1) * P], turned[:, jb, i, :], ident[:])
-            sq = new(f"sq{b}{i}", [S], F32)
-            nc.scalar.activation(sq[:], bank[:], SQUARE)
-            return sq
+        def deal_wf(b, tags):
+            words = new(f"wf_dw{b}", [2, PACK, P], U16, tag=tags[0])
+            nc.vector.tensor_copy(words[:], wf_w[b][:].bitcast(U16).rearrange("p a (m i) -> p a i m", i=PACK))
+            scales = new(f"wf_ds{b}", [2, PACK, P], U8, tag=tags[1])
+            nc.vector.tensor_copy(
+                scales[:], wf_s[:, :, KP * b : KP * (b + 1)].rearrange("p a (m i) -> p a i m", i=PACK)
+            )
+            wf_dw.append(words)
+            wf_ds.append(scales)
 
-        def quantize_we(b, copies):
-            codes, scales = [], []
-            for a in range(2):
-                rounded = new(f"we_bf{b}{a}", [PACK * KP], BF16)
-                raws = we_raw[b, a]
-                count = P // len(copies[a])
-                for u, (copy, walk) in enumerate(copies[a]):
-                    source = raws[u][:].rearrange(f"p j (m i) -> p {walk}", i=PACK)
-                    target = rounded[:].rearrange("p (i m j) -> p i m j", i=PACK, j=PACK)
-                    copy(target[:, :, u * count : (u + 1) * count].rearrange(f"p i m j -> p {walk}"), source)
-                c = new(f"we_c{b}{a}", [KP], U32)
-                s = new(f"we_s{b}{a}", [KP], U8)
-                for u in range(2):
-                    nc.vector.quantize_mx(
-                        c[:, u * 256 : (u + 1) * 256].bitcast(FP8X4),
-                        s[:, u * 256 : (u + 1) * 256],
-                        rounded[:, u * 1024 : (u + 1) * 1024],
-                    )
-                codes.append(c)
-                scales.append(s)
+        deal_wf(0, (None, None))
+
+        def round_we(b, a, copies):
+            rounded = new(f"we_bf{b}{a}", [PACK * KP], BF16)
+            raws = we_raw[b, a]
+            count = P // len(copies)
+            target = rounded[:].rearrange("p (i m j) -> p i m j", i=PACK, j=PACK)
+            for u, copy in enumerate(copies):
+                raw = raws[u][:] if len(raws) > 1 else raws[0][:, :, PACK * count * u : PACK * count * (u + 1)]
+                copy(
+                    target[:, :, u * count : (u + 1) * count].rearrange("p i m j -> p m j i"),
+                    raw.rearrange("p j (m i) -> p m j i", i=PACK),
+                )
+            return rounded
+
+        def quantize_we(b, a, rounded, cuts):
+            codes = new(f"we_c{b}{a}", [KP], U32)
+            scales = new(f"we_s{b}{a}", [KP], U8)
+            for c0, c1 in zip(cuts, cuts[1:]):
+                nc.vector.quantize_mx(
+                    codes[:, c0:c1].bitcast(FP8X4), scales[:, c0:c1], rounded[:, PACK * c0 : PACK * c1]
+                )
             return codes, scales
 
-        def error(b, i, codes, scales, bank):
-            cols = slice(i * P, (i + 1) * P)
+        def forward(b, i):
+            bank = banks[4 + i]
             for a in range(2):
                 nc.tensor.matmul_mx(
                     bank[:],
-                    lhsT=codes[a][:, cols].bitcast(FP8X4),
-                    lhsT_scale=scales[a][:, cols],
+                    lhsT=wf_dw[b][:, a, i, :].bitcast(FP4X4),
+                    lhsT_scale=wf_ds[b][:, a, i, :],
                     rhs=v_w[a][:].bitcast(FP8X4),
                     rhs_scale=v_s[a][:],
                     start=(a == 0),
                     stop=(a == 1),
                 )
+            return bank
 
-        z_bf = [[new(f"z_bf{b}{mh}", [BANK * PACK], BF16) for mh in range(2)] for b in range(2)]
-        on_scalar, on_vector = (nc.scalar.copy, "m j i"), (nc.vector.tensor_copy, "m j i")
+        def error(b, i, quantized):
+            bank = banks[4 * b + i]
+            cols = slice(i * P, (i + 1) * P)
+            for a, (codes, scales) in enumerate(quantized):
+                nc.tensor.matmul_mx(
+                    bank[:],
+                    lhsT=codes[:, cols].bitcast(FP8X4),
+                    lhsT_scale=scales[:, cols],
+                    rhs=v_w[a][:].bitcast(FP8X4),
+                    rhs_scale=v_s[a][:],
+                    start=(a == 0),
+                    stop=(a == 1),
+                )
+            return bank
 
-        def prepare(b, i, codes, scales, turned, square_bank, error_bank):
-            sq = square(b, i, turned, square_bank)
-            if b == 1:
+        rounded00 = round_we(0, 0, (nc.scalar.copy, nc.vector.tensor_copy))
+        tanh = {0: new("th0", [PACK, S], F32, tag="we00")}
+
+        def tanh_of(b, i):
+            nc.scalar.activation(tanh[b][:, i, :], forward(b, i)[:], TANH)
+
+        def square_of(b, i):
+            sq = new(f"sq{b}{i}", [S], F32)
+            nc.scalar.activation(sq[:], tanh[b][:, i, :], SQUARE)
+            return sq
+
+        rounded01 = round_we(0, 1, (nc.vector.tensor_copy, nc.vector.tensor_copy))
+        we0 = [quantize_we(0, 0, rounded00, (0, 512)), quantize_we(0, 1, rounded01, (0, 128, 256, 512))]
+        deal_wf(1, ("we_bf01", "we_bf00"))
+        sq0 = []
+        for pair in ((0, 1), (2, 3)):
+            for i in pair:
+                tanh_of(0, i)
+            sq0.extend(square_of(0, i) for i in pair)
+        for i in range(2):
+            nc.vector.scalar_tensor_tensor(sq0[i][:], sq0[i][:], -1.0, error(0, i, we0)[:], ADD, MULT)
+        for i in range(2):
+            nc.vector.tensor_tensor(pages[i][:].indirect(place[:]), sq0[i][:], step[:], MULT)
+        we1 = [quantize_we(1, a, round_we(1, a, (nc.scalar.copy,)), (0, 512)) for a in range(2)]
+        tanh[1] = new("th1", [PACK, S], F32, tag="we11")
+        slope = new("slope", [2, S], F32, tag="we_bf11")
+        for i in (3, 2):
+            nc.vector.scalar_tensor_tensor(slope[:, i % 2, :], sq0[i][:], -1.0, error(0, i, we0)[:], ADD, MULT)
+        nc.vector.tensor_tensor(sq0[3][:], slope[:, 1, :], step[:], MULT)
+        nc.vector.tensor_tensor(pages[2][:].indirect(place[:]), slope[:, 0, :], step[:], MULT)
+        nc.vector.tensor_copy(pages[3][:].indirect(place[:]), sq0[3][:])
+
+        errors = []
+
+        def corrections(pair):
+            made = [square_of(1, i) for i in pair]
+            for i, sq in zip(pair, made):
                 nc.scalar.activation(sq[:], sq[:], IDENTITY, bias=-1.0)
-            error(b, i, codes, scales, error_bank)
-            e = new(f"e{b}{i}", [S], F32)
-            nc.scalar.copy(e[:], error_bank[:])
-            return sq, e
+                e = new(f"e1{i}", [S], F32)
+                nc.scalar.copy(e[:], error(1, i, we1)[:])
+                errors.append(e)
+            return made
 
-        def scatter(page, sq, e, factor):
-            nc.vector.scalar_tensor_tensor(factor[:], sq[:], -1.0, step[:], ADD, MULT)
-            nc.vector.tensor_tensor(page[:].indirect(place[:]), e[:], factor[:], MULT)
-
-        codes0, scales0 = quantize_we(0, ((on_scalar,), (on_vector, on_vector)))
-        pages.append(new("page3", [T2], F32, tag="we_bf01"))
-        nc.gpsimd.memset(pages[3][:], 0.0)
-        load_sp(0, 0, "we010")
-        load_sp(0, 1, "we011")
-        wc_w = new("wc_w", [2, N], I32, tag="we_bf00")
-        nc.sync.dma_start(wc_w[:], wc_words.rearrange("a p c i -> p a (c i)").bitcast(I32))
-        turned = forward(0, low, (slice(0, 1), slice(1, PACK)), "we00")
-        for i in range(PACK):
-            sq, e = prepare(0, i, codes0, scales0, turned, high[i], ([high[3]] + low)[i])
-            if i < PACK - 1:
-                scatter(pages[i], sq, e, sq)
-        load_sp(1, 0, "we00")
-        codes1, scales1 = quantize_we(1, ((on_scalar,), (on_scalar,)))
-        load_sp(1, 1, "tab_w0")
-        factor = new("factor", [S], F32, tag="we_bf11")
-        nc.vector.scalar_tensor_tensor(factor[:], sq[:], -1.0, step[:], ADD, MULT)
-        nc.vector.tensor_tensor(sq[:], e[:], factor[:], MULT)
-        nc.vector.tensor_copy(pages[3][:].indirect(place[:]), sq[:])
-        turned = forward(1, high, (slice(0, PACK),), "tab_w1")
-        ready = []
-        for i in range(PACK):
-            sq, e = prepare(1, i, codes1, scales1, turned, high[i], high[i])
-            factor = new(f"factor{i}", [S], F32, tag="e03")
-            nc.gpsimd.tensor_tensor(factor[:], sq[:], step[:], MULT)
-            nc.gpsimd.tensor_tensor(sq[:], e[:], factor[:], MULT)
-            ready.append(sq)
-
-        def add_turned(b, h, group, terms, quarters, first, last):
-            sources = [sp_t[b, h][:, e, :] for e in range(2)] + [pages[2 * h + e][:] for e in range(2)]
-            for u in terms:
-                for mq in quarters:
-                    view = group[mq][:].rearrange("m (mb e p) -> m mb e p", mb=2, e=2)
+        def add_turned(b, h, pair_pages, sums, quarters):
+            sources = [sp_t[b, h][:, e, :] for e in range(2)] + [page[:] for page in pair_pages]
+            for mq in quarters:
+                view = sums[mq][:].rearrange("m (mb e p) -> m mb e p", mb=2, e=2)
+                for u in range(4):
                     for mb in range(2):
                         c0 = (2 * mq + mb) * P
                         nc.tensor.matmul(
                             view[:, mb, u % 2, :],
                             sources[u][:, c0 : c0 + P],
                             ident[:],
-                            start=(u == first and mb == 0),
-                            stop=(u == last and mb == 1),
+                            start=(u == 0 and mb == 0),
+                            stop=(u == 3 and mb == 1),
                             is_transpose=True,
                         )
 
-        def round_turned(h, group, z_turned, quarters):
+        def round_turned(targets, sums, quarters):
             for mq in quarters:
                 nc.scalar.copy(
-                    z_turned[mq][:, :, h, :].rearrange("m mb (p e) -> m mb p e", e=2),
-                    group[mq][:].rearrange("m (mb e p) -> m mb p e", mb=2, e=2),
+                    targets[mq].rearrange("m mb (p e) -> m mb p e", e=2),
+                    sums[mq][:].rearrange("m (mb e p) -> m mb p e", mb=2, e=2),
                 )
 
-        def turn_back(halves, z_turned, group, quarters, copies):
-            for mq in quarters:
-                view = group[mq][:].rearrange("p (mb h m) -> p mb h m", mb=2, h=2)
-                words = z_turned[mq].bitcast(F32)
-                for mb in range(2):
-                    for h in range(2):
-                        nc.tensor.transpose(view[:, mb, h, :], words[:, mb, h, :], ident[:])
-                target = halves[mq // 2][:].bitcast(F32).rearrange("p (q mb m h) -> p q mb m h", q=2, mb=2, h=2)
-                copies[mq](target[:, mq % 2], view.rearrange("p mb h m -> p mb m h"))
-
-        zt_half = [new(f"zt{mh}", [2, 2, 2, 2 * P], BF16, tag=f"we_c1{mh}") for mh in range(2)]
-        zt0 = [zt_half[mq // 2][:, mq % 2] for mq in range(4)]
-        add_turned(0, 0, low, (0, 1, 2, 3), range(4), 0, 3)
-        round_turned(0, low, zt0, range(4))
-        add_turned(0, 1, high, (2, 3, 0, 1), range(4), 2, 1)
-        round_turned(1, high, zt0, range(4))
-        turn_back(z_bf[0], zt0, low, range(4), (nc.scalar.copy,) * 4)
+        high, low = banks[:4], banks[4:]
+        for i in range(PACK):
+            tanh_of(1, i)
+        ready = corrections((0, 1)) + corrections((2, 3))
+        for i in range(PACK):
+            factor = new(f"factor{i}", [S], F32, tag="we_c10")
+            nc.gpsimd.tensor_tensor(factor[:], ready[i][:], step[:], MULT)
+            if i < PACK - 1:
+                nc.gpsimd.tensor_tensor(ready[i][:], errors[i][:], factor[:], MULT)
+        wc_ds = new("wc_ds", [N], U8, tag="sq13")
+        nc.gpsimd.tensor_copy(
+            wc_ds[:].rearrange("p (g t n) -> p g t n", g=2, t=PACK),
+            wc_s[:].rearrange("p (g n t) -> p g t n", g=2, t=PACK),
+        )
+        zt0 = [new(f"zt0{mh}", [2, 2, 2, 2 * P], BF16, tag=tag) for mh, tag in enumerate(("we_c11", "we11"))]
+        add_turned(0, 0, pages[0:2], high, range(4))
+        round_turned([zt0[mq // 2][:, mq % 2, :, 0, :] for mq in range(4)], high, range(4))
+        late_pages = [pages[4], pages[5], pages[0], pages[1]]
         for i in range(2):
-            nc.vector.tensor_copy(pages[i][:].indirect(place[:]), ready[i][:])
-        zt1 = [new(f"zt1{mq}", [2, 2, 2 * P], BF16)[:] for mq in range(4)]
-        add_turned(1, 0, high, (0, 1, 2, 3), range(4), 0, 3)
-        round_turned(0, high, zt1, range(4))
-        for i in range(2, PACK):
-            nc.vector.tensor_copy(pages[i][:].indirect(place[:]), ready[i][:])
-        add_turned(1, 1, low, (0, 1, 2), range(4), 0, 3)
+            nc.vector.tensor_copy(late_pages[i][:].indirect(place[:]), ready[i][:])
+        add_turned(0, 1, pages[2:4], low, range(4))
+        round_turned([zt0[mq // 2][:, mq % 2, :, 1, :] for mq in range(4)], low, range(4))
+        z_bf0 = new("z_bf0", [T2 * PACK], BF16)
+        for mq in range(4):
+            view = high[mq][:].rearrange("p (mb h m) -> p mb h m", mb=2, h=2)
+            words = zt0[mq // 2][:, mq % 2].bitcast(F32)
+            for mb in range(2):
+                for h in range(2):
+                    nc.tensor.transpose(view[:, mb, h, :], words[:, mb, h, :], ident[:])
+            target = z_bf0[:].bitcast(F32).rearrange("p (q mb m h) -> p q mb m h", q=4, mb=2, h=2)
+            nc.scalar.copy(target[:, mq], view.rearrange("p mb h m -> p mb m h"))
+        nc.vector.tensor_copy(late_pages[2][:].indirect(place[:]), ready[2][:])
+        z_c = [new(f"z_c{b}", [T2], U32) for b in range(2)]
+        z_s = [new(f"z_s{b}", [T2], U8) for b in range(2)]
+        nc.vector.quantize_mx(z_c[0][:].bitcast(FP8X4), z_s[0][:], z_bf0[:])
 
-        wc_dw = new("wc_dw", [2 * N], I32, tag="e13")
+        wc_dw = new("wc_dw", [2 * N], I32, tag="we_c11")
         nc.gpsimd.tensor_copy(
             wc_dw[:].rearrange("p (g t n) -> p g t n", g=4, t=PACK),
             wc_w[:].rearrange("p a (g n t) -> p (a g) t n", g=2, t=PACK),
         )
-        wc_ds = new("wc_ds", [N], U8, tag="sq13")
-        nc.vector.tensor_copy(
-            wc_ds[:].rearrange("p (g t n) -> p g t n", g=2, t=PACK),
-            wc_s[:].rearrange("p (g n t) -> p g t n", g=2, t=PACK),
-        )
-        z_c = [new(f"z_c{b}", [T2], U32) for b in range(2)]
-        z_s = [new("z_s0", [T2], U8, tag="wc_s"), new("z_s1", [T2], U8)]
+        ready[3] = new("last_correction", [S], F32, tag="we11")
+        nc.gpsimd.tensor_tensor(ready[3][:], errors[3][:], factor[:], MULT)
+        add_turned(1, 0, late_pages[0:2], low, (3, 2, 0, 1))
+        zt1 = [new(f"zt1{mq}", [2, 2 * P], BF16)[:] for mq in range(4)]
+        z_bf1 = [new(f"z_bf1{c}", [width * PACK], BF16) for c, width in enumerate((256, 256, 512))]
+        for quarters in ((3, 2, 0), (1,)):
+            round_turned(zt1, low, quarters)
+            for mq in quarters:
+                words = zt1[mq].bitcast(F32)
+                for mb in range(2):
+                    nc.tensor.transpose(high[mq][:, mb * P : (mb + 1) * P], words[:, mb, :], ident[:])
+                target = z_bf1[min(mq, 2)][:].bitcast(F32).rearrange("p (q m h) -> p q m h", m=2 * P, h=2)
+                nc.scalar.copy(target[:, max(mq - 2, 0), :, 0], high[mq][:, : 2 * P])
 
-        def quantize_z(b, mh):
-            cols = slice(mh * BANK, (mh + 1) * BANK)
-            nc.vector.quantize_mx(z_c[b][:, cols].bitcast(FP8X4), z_s[b][:, cols], z_bf[b][mh][:])
+        first_rows = new("first_rows", [2, 2, 256], BF16, tag="z_bf0")
+        last_rows = [first_rows[:, 0], first_rows[:, 1], new("wide_rows", [2, 512], BF16, tag="zt11")[:]]
+        chunks = ((0, 256), (256, 256), (512, 512))
+        for c, (c0, width) in enumerate(chunks):
+            cols = slice(c0, c0 + width)
+            nc.gpsimd.tensor_tensor(last_rows[c][:, 0, :], sp_t[1, 1][:, 0, cols], late_pages[2][:, cols], ADD)
+        nc.vector.tensor_copy(late_pages[3][:].indirect(place[:]), ready[3][:])
 
-        for mh in range(2):
-            quantize_z(0, mh)
-        for mh in range(2):
-            quarters = (2 * mh, 2 * mh + 1)
-            add_turned(1, 1, low, (3,), quarters, 0, 3)
-            round_turned(1, low, zt1, quarters)
-            turn_back(z_bf[1], zt1, [high[0], high[1], low[0], low[1]], quarters, (nc.scalar.copy,) + (nc.vector.tensor_copy,) * 3)
-            quantize_z(1, mh)
+        def last_sum(c):
+            cols = slice(chunks[c][0], sum(chunks[c]))
+            nc.vector.tensor_tensor(last_rows[c][:, 1, :], sp_t[1, 1][:, 1, cols], late_pages[3][:, cols], ADD)
 
-        groups = ([high[2], high[3], low[2], low[3]], [high[0], high[1], low[0], low[1]])
-        y_s = [new(f"y_s{mh}", [2, BANK], U8) for mh in range(2)]
-        units = ((0, 0, BANK, "we010"), (1, 0, BANK, "tab_w1"), (0, BANK, BANK, "we00"))
-        units = units + ((1, BANK, BANK // 2, "we011"), (1, BANK + BANK // 2, BANK // 2, "tab_w0"))
-
-        def last_pass(u, t, a):
-            g, m0, width, tag = units[u]
-            c0 = KP * g + P * t
-            nc.tensor.matmul_mx(
-                groups[u % 2][t][:, :width],
-                lhsT=wc_dw[:, N * a + c0 : N * a + c0 + P].bitcast(FP8X4),
-                lhsT_scale=wc_ds[4 * a :, c0 : c0 + P],
-                rhs=z_c[a][:, m0 : m0 + width].bitcast(FP8X4),
-                rhs_scale=z_s[a][:, m0 : m0 + width],
-                start=(a == 0),
-                stop=(a == 1),
+        def pair_up(c):
+            nc.vector.tensor_copy(
+                z_bf1[c][:].rearrange("p (m h e) -> p m h e", h=2, e=2)[:, :, 1, :],
+                last_rows[c].rearrange("p e m -> p m e"),
             )
 
-        for u, (g, m0, width, tag) in enumerate(units):
+        def quantize_z(c):
+            cols = slice(chunks[c][0], sum(chunks[c]))
+            nc.vector.quantize_mx(z_c[1][:, cols].bitcast(FP8X4), z_s[1][:, cols], z_bf1[c][:])
+
+        y_s = [new(f"y_s{mh}", [2, BANK], U8) for mh in range(2)]
+        units = (
+            (0, 0, 256, low[:2], "we010"),
+            (1, 0, 256, low[2:], "we011"),
+            (0, 256, 256, high[:2], "sp00"),
+            (1, 256, 256, high[2:], "sp01"),
+            (0, 512, 512, low, "we00"),
+            (1, 512, 256, high[:2], "tab_w0"),
+            (1, 768, 256, high[2:], "we11"),
+        )
+        early = 4
+
+        def last_passes(u, k, a):
+            g, m0, width, group, tag = units[u]
+            cols = slice(m0, m0 + width)
+            share = BANK // width
+            for s in range(share):
+                c0 = KP * g + P * (share * k + s)
+                nc.tensor.matmul_mx(
+                    group[k][:, s * width : (s + 1) * width],
+                    lhsT=wc_dw[:, N * a + c0 : N * a + c0 + P].bitcast(FP8X4),
+                    lhsT_scale=wc_ds[4 * a :, c0 : c0 + P],
+                    rhs=z_c[a][:, cols].bitcast(FP8X4),
+                    rhs_scale=z_s[a][:, cols],
+                    start=(a == 0 and s == 0),
+                    stop=(a == 1 and s == share - 1),
+                )
+
+        for u in range(early):
+            for k in range(2):
+                last_passes(u, k, 0)
+
+        last_sum(0)
+        last_sum(1)
+        pair_up(0)
+        pair_up(1)
+        quantize_z(0)
+        last_sum(2)
+        quantize_z(1)
+        pair_up(2)
+        quantize_z(2)
+
+        for u, (g, m0, width, group, tag) in enumerate(units):
             cols = slice(m0, m0 + width)
             y = new(f"y{u}", [PACK, width], F32, tag=tag)
             rows = out_0[KP * g : KP * (g + 1), cols].rearrange("(p t) m -> p t m", t=PACK)
-            run = (1, 2, 2, 4, 4)[u]
-            for t in range(PACK):
-                bank = groups[u % 2][t]
-                for a in range(2):
-                    last_pass(u, t, a)
-                copy = nc.vector.tensor_copy if (u, t) == (0, PACK - 1) else nc.scalar.copy
-                copy(y[:, t, :], bank[:, :width])
-                if (t + 1) % run == 0:
-                    nc.sync.dma_start(rows[:, t + 1 - run : t + 1, :], y[:, t + 1 - run : t + 1, :])
+            share = BANK // width
+            for k, bank in enumerate(group):
+                for a in range(1 if u < early else 0, 2):
+                    last_passes(u, k, a)
+                done = share * (k + 1)
+                nc.scalar.copy(y[:, done - share : done, :], bank[:].rearrange("p (s m) -> p s m", s=share))
+                run = 2 if u in (0, 4) else PACK
+                if done % run == 0:
+                    nc.sync.dma_start(rows[:, done - run : done, :], y[:, done - run : done, :])
             y_bf = new(f"y_bf{u}", [width * PACK], BF16, tag=f"we_bf0{u % 2}")
             nc.vector.tensor_copy(
                 y_bf[:].rearrange("p (c i t) -> p c t i", i=4, t=PACK),

@@ -43,12 +43,12 @@ def tile_list_headbox_setpoint_step_kernel(
         tab_s = new("tab_s", [2, T], U8)
         wf_s = new("wf_s", [2, H], U8)
         wc_s = new("wc_s", [N], U8)
-        nc.vector.memset(tab_s[:].bitcast(I32), 0)
-        for plane in (wf_s, wc_s):
-            nc.gpsimd.memset(plane[:].bitcast(I32), 0)
-        pages = [new(f"page{u}", [T2], F32) for u in range(6)]
-        for page in pages:
-            nc.gpsimd.memset(page[:], 0.0)
+        for plane in (tab_s, wf_s):
+            nc.vector.memset(plane[:].bitcast(I32), 0)
+        pages = [new(f"page{u}", [T2], F32) for u in range(2)]
+        nc.vector.memset(pages[0][:], 0.0)
+        nc.gpsimd.memset(wc_s[:].bitcast(I32), 0)
+        nc.gpsimd.memset(pages[1][:], 0.0)
         ident = new("ident", [P], F32)
         make_identity(nc, ident[:])
 
@@ -204,11 +204,15 @@ def tile_list_headbox_setpoint_step_kernel(
             nc.vector.scalar_tensor_tensor(sq0[i][:], sq0[i][:], -1.0, error(0, i, we0)[:], ADD, MULT)
         for i in range(2):
             nc.vector.tensor_tensor(pages[i][:].indirect(place[:]), sq0[i][:], step[:], MULT)
+        slope_banks = {i: error(0, i, we0) for i in (3, 2)}
+        for u, tag in enumerate(("wf_w1", "wf_s", "we_c00", "we_c01")):
+            pages.append(new(f"page{u + 2}", [T2], F32, tag=tag))
+            nc.gpsimd.memset(pages[-1][:], 0.0)
         we1 = [quantize_we(1, a, round_we(1, a, (nc.scalar.copy,)), (0, 512)) for a in range(2)]
         tanh[1] = new("th1", [PACK, S], F32, tag="we11")
         slope = new("slope", [2, S], F32, tag="we_bf11")
         for i in (3, 2):
-            nc.vector.scalar_tensor_tensor(slope[:, i % 2, :], sq0[i][:], -1.0, error(0, i, we0)[:], ADD, MULT)
+            nc.vector.scalar_tensor_tensor(slope[:, i % 2, :], sq0[i][:], -1.0, slope_banks[i][:], ADD, MULT)
         nc.vector.tensor_tensor(sq0[3][:], slope[:, 1, :], step[:], MULT)
         nc.vector.tensor_tensor(pages[2][:].indirect(place[:]), slope[:, 0, :], step[:], MULT)
         nc.vector.tensor_copy(pages[3][:].indirect(place[:]), sq0[3][:])
@@ -251,13 +255,12 @@ def tile_list_headbox_setpoint_step_kernel(
         for i in range(PACK):
             tanh_of(1, i)
         ready = corrections((0, 1)) + corrections((2, 3))
-        for i in range(PACK):
+        for i in range(PACK - 1):
             factor = new(f"factor{i}", [S], F32, tag="we_c10")
             nc.gpsimd.tensor_tensor(factor[:], ready[i][:], step[:], MULT)
-            if i < PACK - 1:
-                nc.gpsimd.tensor_tensor(ready[i][:], errors[i][:], factor[:], MULT)
-        wc_ds = new("wc_ds", [N], U8, tag="sq13")
-        nc.gpsimd.tensor_copy(
+            nc.gpsimd.tensor_tensor(ready[i][:], errors[i][:], factor[:], MULT)
+        wc_ds = new("wc_ds", [N], U8, tag="e12")
+        nc.vector.tensor_copy(
             wc_ds[:].rearrange("p (g t n) -> p g t n", g=2, t=PACK),
             wc_s[:].rearrange("p (g n t) -> p g t n", g=2, t=PACK),
         )
@@ -284,11 +287,12 @@ def tile_list_headbox_setpoint_step_kernel(
         nc.vector.quantize_mx(z_c[0][:].bitcast(FP8X4), z_s[0][:], z_bf0[:])
 
         wc_dw = new("wc_dw", [2 * N], I32, tag="we_c11")
-        nc.gpsimd.tensor_copy(
-            wc_dw[:].rearrange("p (g t n) -> p g t n", g=4, t=PACK),
-            wc_w[:].rearrange("p a (g n t) -> p (a g) t n", g=2, t=PACK),
+        nc.vector.tensor_copy(
+            wc_dw[:].rearrange("p (g t n) -> p g n t", g=4, t=PACK),
+            wc_w[:].rearrange("p a (g n t) -> p (a g) n t", g=2, t=PACK),
         )
-        ready[3] = new("last_correction", [S], F32, tag="we11")
+        factor = new("last_factor", [S], F32, tag="we11")
+        nc.gpsimd.tensor_tensor(factor[:], ready[3][:], step[:], MULT)
         nc.gpsimd.tensor_tensor(ready[3][:], errors[3][:], factor[:], MULT)
         add_turned(1, 0, late_pages[0:2], low, (3, 2, 0, 1))
         zt1 = [new(f"zt1{mq}", [2, 2 * P], BF16)[:] for mq in range(4)]
@@ -375,7 +379,8 @@ def tile_list_headbox_setpoint_step_kernel(
                 for a in range(1 if u < early else 0, 2):
                     last_passes(u, k, a)
                 done = share * (k + 1)
-                nc.scalar.copy(y[:, done - share : done, :], bank[:].rearrange("p (s m) -> p s m", s=share))
+                copy = nc.vector.tensor_copy if (u, done) in ((1, PACK), (4, PACK)) else nc.scalar.copy
+                copy(y[:, done - share : done, :], bank[:].rearrange("p (s m) -> p s m", s=share))
                 run = 2 if u in (0, 4) else PACK
                 if done % run == 0:
                     nc.sync.dma_start(rows[:, done - run : done, :], y[:, done - run : done, :])

@@ -45,10 +45,10 @@ def tile_list_headbox_setpoint_step_kernel(
         wc_s = new("wc_s", [N], U8)
         for plane in (tab_s, wf_s):
             nc.vector.memset(plane[:].bitcast(I32), 0)
-        pages = [new(f"page{u}", [T2], F32) for u in range(2)]
-        nc.vector.memset(pages[0][:], 0.0)
+        pages = [new(f"page{u}", [T2], F32) for u in range(PACK)]
         nc.gpsimd.memset(wc_s[:].bitcast(I32), 0)
-        nc.gpsimd.memset(pages[1][:], 0.0)
+        for page, engine in zip(pages, (nc.vector, nc.vector, nc.gpsimd, nc.gpsimd)):
+            engine.memset(page[:], 0.0)
         ident = new("ident", [P], F32)
         make_identity(nc, ident[:])
 
@@ -99,13 +99,13 @@ def tile_list_headbox_setpoint_step_kernel(
         nc.sync.dma_start(place[:], offs2)
         for a in range(2):
             we_raw[1, a] = [load_we(f"we1{a}", a, KP, KP)]
-        sp_t = {(0, h): load_sp(0, h, None) for h in range(2)}
         wc_w = new("wc_w", [2, N], I32)
         nc.sync.dma_start(wc_w[:], wc_words.rearrange("a p c i -> p a (c i)").bitcast(I32))
         for q in range(4):
             nc.sync.dma_start(
                 wc_s[32 * q : 32 * q + 8, :].bitcast(I32), wc_scales[:, 4 * q : 4 * q + 4, :].bitcast(I32)
             )
+        sp_t = {(0, h): load_sp(0, h, None) for h in range(2)}
 
         v_w = [new(f"v_w{a}", [S], U32) for a in range(2)]
         v_s = [new(f"v_s{a}", [S], U8) for a in range(2)]
@@ -204,15 +204,24 @@ def tile_list_headbox_setpoint_step_kernel(
             nc.vector.scalar_tensor_tensor(sq0[i][:], sq0[i][:], -1.0, error(0, i, we0)[:], ADD, MULT)
         for i in range(2):
             nc.vector.tensor_tensor(pages[i][:].indirect(place[:]), sq0[i][:], step[:], MULT)
-        slope_banks = {i: error(0, i, we0) for i in (3, 2)}
-        for u, tag in enumerate(("wf_w1", "wf_s", "we_c00", "we_c01")):
-            pages.append(new(f"page{u + 2}", [T2], F32, tag=tag))
+        for u, tag in enumerate(("wf_w1", "wf_s")):
+            pages.append(new(f"page{u + PACK}", [T2], F32, tag=tag))
             nc.gpsimd.memset(pages[-1][:], 0.0)
         we1 = [quantize_we(1, a, round_we(1, a, (nc.scalar.copy,)), (0, 512)) for a in range(2)]
+        wc_dw = new("wc_dw", [2 * N], I32, tag="we_bf10")
+        nc.vector.tensor_copy(
+            wc_dw[:].rearrange("p (g t n) -> p g n t", g=4, t=PACK),
+            wc_w[:].rearrange("p a (g n t) -> p (a g) n t", g=2, t=PACK),
+        )
+        wc_ds = new("wc_ds", [N], U8)
+        nc.vector.tensor_copy(
+            wc_ds[:].rearrange("p (g t n) -> p g t n", g=2, t=PACK),
+            wc_s[:].rearrange("p (g n t) -> p g t n", g=2, t=PACK),
+        )
         tanh[1] = new("th1", [PACK, S], F32, tag="we11")
         slope = new("slope", [2, S], F32, tag="we_bf11")
         for i in (3, 2):
-            nc.vector.scalar_tensor_tensor(slope[:, i % 2, :], sq0[i][:], -1.0, slope_banks[i][:], ADD, MULT)
+            nc.vector.scalar_tensor_tensor(slope[:, i % 2, :], sq0[i][:], -1.0, error(0, i, we0)[:], ADD, MULT)
         nc.vector.tensor_tensor(sq0[3][:], slope[:, 1, :], step[:], MULT)
         nc.vector.tensor_tensor(pages[2][:].indirect(place[:]), slope[:, 0, :], step[:], MULT)
         nc.vector.tensor_copy(pages[3][:].indirect(place[:]), sq0[3][:])
@@ -255,15 +264,10 @@ def tile_list_headbox_setpoint_step_kernel(
         for i in range(PACK):
             tanh_of(1, i)
         ready = corrections((0, 1)) + corrections((2, 3))
-        for i in range(PACK - 1):
-            factor = new(f"factor{i}", [S], F32, tag="we_c10")
+        for i in range(PACK):
+            factor = new(f"factor{i}", [S], F32, tag="we_bf11")
             nc.gpsimd.tensor_tensor(factor[:], ready[i][:], step[:], MULT)
             nc.gpsimd.tensor_tensor(ready[i][:], errors[i][:], factor[:], MULT)
-        wc_ds = new("wc_ds", [N], U8, tag="e12")
-        nc.vector.tensor_copy(
-            wc_ds[:].rearrange("p (g t n) -> p g t n", g=2, t=PACK),
-            wc_s[:].rearrange("p (g n t) -> p g t n", g=2, t=PACK),
-        )
         zt0 = [new(f"zt0{mh}", [2, 2, 2, 2 * P], BF16, tag=tag) for mh, tag in enumerate(("we_c11", "we11"))]
         add_turned(0, 0, pages[0:2], high, range(4))
         round_turned([zt0[mq // 2][:, mq % 2, :, 0, :] for mq in range(4)], high, range(4))
@@ -282,22 +286,10 @@ def tile_list_headbox_setpoint_step_kernel(
             target = z_bf0[:].bitcast(F32).rearrange("p (q mb m h) -> p q mb m h", q=4, mb=2, h=2)
             nc.scalar.copy(target[:, mq], view.rearrange("p mb h m -> p mb m h"))
         nc.vector.tensor_copy(late_pages[2][:].indirect(place[:]), ready[2][:])
-        z_c = [new(f"z_c{b}", [T2], U32) for b in range(2)]
-        z_s = [new(f"z_s{b}", [T2], U8) for b in range(2)]
-        nc.vector.quantize_mx(z_c[0][:].bitcast(FP8X4), z_s[0][:], z_bf0[:])
-
-        wc_dw = new("wc_dw", [2 * N], I32, tag="we_c11")
-        nc.vector.tensor_copy(
-            wc_dw[:].rearrange("p (g t n) -> p g n t", g=4, t=PACK),
-            wc_w[:].rearrange("p a (g n t) -> p (a g) n t", g=2, t=PACK),
-        )
-        factor = new("last_factor", [S], F32, tag="we11")
-        nc.gpsimd.tensor_tensor(factor[:], ready[3][:], step[:], MULT)
-        nc.gpsimd.tensor_tensor(ready[3][:], errors[3][:], factor[:], MULT)
-        add_turned(1, 0, late_pages[0:2], low, (3, 2, 0, 1))
+        add_turned(1, 0, late_pages[0:2], low, range(4))
         zt1 = [new(f"zt1{mq}", [2, 2 * P], BF16)[:] for mq in range(4)]
         z_bf1 = [new(f"z_bf1{c}", [width * PACK], BF16) for c, width in enumerate((256, 256, 512))]
-        for quarters in ((3, 2, 0), (1,)):
+        for quarters in ((0, 1), (2, 3)):
             round_turned(zt1, low, quarters)
             for mq in quarters:
                 words = zt1[mq].bitcast(F32)
@@ -306,17 +298,18 @@ def tile_list_headbox_setpoint_step_kernel(
                 target = z_bf1[min(mq, 2)][:].bitcast(F32).rearrange("p (q m h) -> p q m h", m=2 * P, h=2)
                 nc.scalar.copy(target[:, max(mq - 2, 0), :, 0], high[mq][:, : 2 * P])
 
-        first_rows = new("first_rows", [2, 2, 256], BF16, tag="z_bf0")
-        last_rows = [first_rows[:, 0], first_rows[:, 1], new("wide_rows", [2, 512], BF16, tag="zt11")[:]]
+        first_rows = new("first_rows", [2, 2, 256], BF16, tag="e13")
+        last_rows = [first_rows[:, 0], first_rows[:, 1], new("wide_rows", [2, 512], BF16, tag="zt13")[:]]
         chunks = ((0, 256), (256, 256), (512, 512))
-        for c, (c0, width) in enumerate(chunks):
+        for c, (c0, width) in enumerate(chunks[:2]):
             cols = slice(c0, c0 + width)
             nc.gpsimd.tensor_tensor(last_rows[c][:, 0, :], sp_t[1, 1][:, 0, cols], late_pages[2][:, cols], ADD)
         nc.vector.tensor_copy(late_pages[3][:].indirect(place[:]), ready[3][:])
 
         def last_sum(c):
             cols = slice(chunks[c][0], sum(chunks[c]))
-            nc.vector.tensor_tensor(last_rows[c][:, 1, :], sp_t[1, 1][:, 1, cols], late_pages[3][:, cols], ADD)
+            for e in range(0 if c == 2 else 1, 2):
+                nc.vector.tensor_tensor(last_rows[c][:, e, :], sp_t[1, 1][:, e, cols], late_pages[2 + e][:, cols], ADD)
 
         def pair_up(c):
             nc.vector.tensor_copy(
@@ -324,9 +317,17 @@ def tile_list_headbox_setpoint_step_kernel(
                 last_rows[c].rearrange("p e m -> p m e"),
             )
 
+        z_q = {}
+
         def quantize_z(c):
             cols = slice(chunks[c][0], sum(chunks[c]))
-            nc.vector.quantize_mx(z_c[1][:, cols].bitcast(FP8X4), z_s[1][:, cols], z_bf1[c][:])
+            whole = slice(PACK * cols.start, PACK * cols.stop)
+            for b, source in enumerate((z_bf0[:, whole], z_bf1[c][:])):
+                tag = "zt12" if (b, c) == (0, 2) else None
+                codes = new(f"z_c{b}{c}", [chunks[c][1]], U32, tag=tag)
+                scales = new(f"z_s{b}{c}", [chunks[c][1]], U8)
+                nc.vector.quantize_mx(codes[:].bitcast(FP8X4), scales[:], source)
+                z_q[b, c] = (codes, scales)
 
         y_s = [new(f"y_s{mh}", [2, BANK], U8) for mh in range(2)]
         units = (
@@ -338,11 +339,12 @@ def tile_list_headbox_setpoint_step_kernel(
             (1, 512, 256, high[:2], "tab_w0"),
             (1, 768, 256, high[2:], "we11"),
         )
-        early = 4
 
         def last_passes(u, k, a):
             g, m0, width, group, tag = units[u]
-            cols = slice(m0, m0 + width)
+            c = min(m0 // 256, 2)
+            cols = slice(m0 - chunks[c][0], m0 - chunks[c][0] + width)
+            codes, scales = z_q[a, c]
             share = BANK // width
             for s in range(share):
                 c0 = KP * g + P * (share * k + s)
@@ -350,15 +352,11 @@ def tile_list_headbox_setpoint_step_kernel(
                     group[k][:, s * width : (s + 1) * width],
                     lhsT=wc_dw[:, N * a + c0 : N * a + c0 + P].bitcast(FP8X4),
                     lhsT_scale=wc_ds[4 * a :, c0 : c0 + P],
-                    rhs=z_c[a][:, cols].bitcast(FP8X4),
-                    rhs_scale=z_s[a][:, cols],
+                    rhs=codes[:, cols].bitcast(FP8X4),
+                    rhs_scale=scales[:, cols],
                     start=(a == 0 and s == 0),
                     stop=(a == 1 and s == share - 1),
                 )
-
-        for u in range(early):
-            for k in range(2):
-                last_passes(u, k, 0)
 
         last_sum(0)
         last_sum(1)
@@ -376,11 +374,10 @@ def tile_list_headbox_setpoint_step_kernel(
             rows = out_0[KP * g : KP * (g + 1), cols].rearrange("(p t) m -> p t m", t=PACK)
             share = BANK // width
             for k, bank in enumerate(group):
-                for a in range(1 if u < early else 0, 2):
+                for a in range(2):
                     last_passes(u, k, a)
                 done = share * (k + 1)
-                copy = nc.vector.tensor_copy if (u, done) in ((1, PACK), (4, PACK)) else nc.scalar.copy
-                copy(y[:, done - share : done, :], bank[:].rearrange("p (s m) -> p s m", s=share))
+                nc.scalar.copy(y[:, done - share : done, :], bank[:].rearrange("p (s m) -> p s m", s=share))
                 run = 2 if u in (0, 4) else PACK
                 if done % run == 0:
                     nc.sync.dma_start(rows[:, done - run : done, :], y[:, done - run : done, :])

@@ -59,10 +59,10 @@ def tile_list_headbox_setpoint_step_kernel(
             nc.sync.dma_start(tile_ap, words.rearrange("p c i -> p (c i)").bitcast(I32))
 
         def load_rows(rows, scales):
-            for q in range(4):
+            for r in range(4):
                 nc.sync.dma_start(
-                    rows[32 * q : 32 * q + 4, :, :].bitcast(I32),
-                    scales[:, 4 * q : 4 * q + 4, :].rearrange("a r c -> r a c").bitcast(I32),
+                    rows[r:P:32, :, :].bitcast(I32),
+                    scales[:, r:16:4, :].rearrange("a q c -> q a c").bitcast(I32),
                 )
 
         def load_we(name, a, c0, width):
@@ -118,17 +118,17 @@ def tile_list_headbox_setpoint_step_kernel(
 
         wf_dw, wf_ds = [], []
 
-        def deal_wf(b, tags):
-            words = new(f"wf_dw{b}", [2, PACK, P], U16, tag=tags[0])
+        def deal_wf(b):
+            words = new(f"wf_dw{b}", [2, PACK, P], U16)
             nc.vector.tensor_copy(words[:], wf_w[b][:].bitcast(U16).rearrange("p a (m i) -> p a i m", i=PACK))
-            scales = new(f"wf_ds{b}", [2, PACK, P], U8, tag=tags[1])
+            scales = new(f"wf_ds{b}", [2, PACK, P], U8)
             nc.vector.tensor_copy(
                 scales[:], wf_s[:, :, KP * b : KP * (b + 1)].rearrange("p a (m i) -> p a i m", i=PACK)
             )
             wf_dw.append(words)
             wf_ds.append(scales)
 
-        deal_wf(0, (None, None))
+        deal_wf(0)
 
         def round_we(b, a, copies):
             rounded = new(f"we_bf{b}{a}", [PACK * KP], BF16)
@@ -194,7 +194,7 @@ def tile_list_headbox_setpoint_step_kernel(
 
         rounded01 = round_we(0, 1, (nc.vector.tensor_copy, nc.vector.tensor_copy))
         we0 = [quantize_we(0, 0, rounded00, (0, 512)), quantize_we(0, 1, rounded01, (0, 128, 256, 512))]
-        deal_wf(1, ("we_bf01", "we_bf00"))
+        deal_wf(1)
         sq0 = []
         for pair in ((0, 1), (2, 3)):
             for i in pair:
@@ -204,7 +204,7 @@ def tile_list_headbox_setpoint_step_kernel(
             nc.vector.scalar_tensor_tensor(sq0[i][:], sq0[i][:], -1.0, error(0, i, we0)[:], ADD, MULT)
         for i in range(2):
             nc.vector.tensor_tensor(pages[i][:].indirect(place[:]), sq0[i][:], step[:], MULT)
-        for u, tag in enumerate(("wf_w1", "wf_s")):
+        for u, tag in enumerate(("wf_w1", "we_c01")):
             pages.append(new(f"page{u + PACK}", [T2], F32, tag=tag))
             nc.gpsimd.memset(pages[-1][:], 0.0)
         we1 = [quantize_we(1, a, round_we(1, a, (nc.scalar.copy,)), (0, 512)) for a in range(2)]
@@ -298,17 +298,17 @@ def tile_list_headbox_setpoint_step_kernel(
                 target = z_bf1[min(mq, 2)][:].bitcast(F32).rearrange("p (q m h) -> p q m h", m=2 * P, h=2)
                 nc.scalar.copy(target[:, max(mq - 2, 0), :, 0], high[mq][:, : 2 * P])
 
-        first_rows = new("first_rows", [2, 2, 256], BF16, tag="e13")
-        last_rows = [first_rows[:, 0], first_rows[:, 1], new("wide_rows", [2, 512], BF16, tag="zt13")[:]]
         chunks = ((0, 256), (256, 256), (512, 512))
-        for c, (c0, width) in enumerate(chunks[:2]):
-            cols = slice(c0, c0 + width)
-            nc.gpsimd.tensor_tensor(last_rows[c][:, 0, :], sp_t[1, 1][:, 0, cols], late_pages[2][:, cols], ADD)
+        last_rows = [
+            new(f"last_rows{c}", [2, width], BF16, tag=tag)[:]
+            for c, ((c0, width), tag) in enumerate(zip(chunks, ("e13", "zt11", "zt13")))
+        ]
+        nc.gpsimd.tensor_tensor(last_rows[0][:, 0, :], sp_t[1, 1][:, 0, :256], late_pages[2][:, :256], ADD)
         nc.vector.tensor_copy(late_pages[3][:].indirect(place[:]), ready[3][:])
 
         def last_sum(c):
             cols = slice(chunks[c][0], sum(chunks[c]))
-            for e in range(0 if c == 2 else 1, 2):
+            for e in range(1 if c == 0 else 0, 2):
                 nc.vector.tensor_tensor(last_rows[c][:, e, :], sp_t[1, 1][:, e, cols], late_pages[2 + e][:, cols], ADD)
 
         def pair_up(c):
@@ -323,7 +323,7 @@ def tile_list_headbox_setpoint_step_kernel(
             cols = slice(chunks[c][0], sum(chunks[c]))
             whole = slice(PACK * cols.start, PACK * cols.stop)
             for b, source in enumerate((z_bf0[:, whole], z_bf1[c][:])):
-                tag = "zt12" if (b, c) == (0, 2) else None
+                tag = {(0, 1): "zt10", (0, 2): "zt12"}.get((b, c))
                 codes = new(f"z_c{b}{c}", [chunks[c][1]], U32, tag=tag)
                 scales = new(f"z_s{b}{c}", [chunks[c][1]], U8)
                 nc.vector.quantize_mx(codes[:].bitcast(FP8X4), scales[:], source)
@@ -358,15 +358,10 @@ def tile_list_headbox_setpoint_step_kernel(
                     stop=(a == 1 and s == share - 1),
                 )
 
-        last_sum(0)
-        last_sum(1)
-        pair_up(0)
-        pair_up(1)
-        quantize_z(0)
-        last_sum(2)
-        quantize_z(1)
-        pair_up(2)
-        quantize_z(2)
+        for c in range(3):
+            last_sum(c)
+            pair_up(c)
+            quantize_z(c)
 
         for u, (g, m0, width, group, tag) in enumerate(units):
             cols = slice(m0, m0 + width)
@@ -392,8 +387,8 @@ def tile_list_headbox_setpoint_step_kernel(
             nc.sync.dma_start(out_1[g, :, cols, :].rearrange("p m t -> p (m t)").bitcast(I32), y_c[:].bitcast(I32))
             if g == 1 and (m0 + width) % BANK == 0:
                 half = slice(m0 + width - BANK, m0 + width)
-                for q in range(4):
+                for r in range(4):
                     nc.sync.dma_start(
-                        out_2[:, 4 * q : 4 * q + 4, half].rearrange("g r m -> r g m").bitcast(I32),
-                        plane[32 * q : 32 * q + 4, :, :].bitcast(I32),
+                        out_2[:, r:16:4, half].rearrange("g q m -> q g m").bitcast(I32),
+                        plane[r:P:32, :, :].bitcast(I32),
                     )

@@ -43,12 +43,11 @@ def tile_list_headbox_setpoint_step_kernel(
         tab_s = new("tab_s", [2, T], U8)
         wf_s = new("wf_s", [2, H], U8)
         wc_s = new("wc_s", [N], U8)
-        for plane in (tab_s, wf_s):
+        for plane in (tab_s, wf_s, wc_s):
             nc.vector.memset(plane[:].bitcast(I32), 0)
-        pages = [new(f"page{u}", [T2], F32) for u in range(PACK)]
-        nc.gpsimd.memset(wc_s[:].bitcast(I32), 0)
-        for page, engine in zip(pages, (nc.vector, nc.vector, nc.gpsimd, nc.gpsimd)):
-            engine.memset(page[:], 0.0)
+        pages = [new(f"page{u}", [T2], F32) for u in range(2)]
+        for page in pages:
+            nc.vector.memset(page[:], 0.0)
         ident = new("ident", [P], F32)
         make_identity(nc, ident[:])
 
@@ -204,14 +203,15 @@ def tile_list_headbox_setpoint_step_kernel(
             nc.vector.scalar_tensor_tensor(sq0[i][:], sq0[i][:], -1.0, error(0, i, we0)[:], ADD, MULT)
         for i in range(2):
             nc.vector.tensor_tensor(pages[i][:].indirect(place[:]), sq0[i][:], step[:], MULT)
-        for u, tag in enumerate(("wf_w1", "we_c01")):
-            pages.append(new(f"page{u + PACK}", [T2], F32, tag=tag))
+        error_banks = {i: error(0, i, we0) for i in (3, 2)}
+        for u, tag in enumerate(("wf_w1", "we_c00", "we_c01", "we_s01")):
+            pages.append(new(f"page{u + 2}", [T2], F32, tag=tag))
             nc.gpsimd.memset(pages[-1][:], 0.0)
         we1 = [quantize_we(1, a, round_we(1, a, (nc.scalar.copy,)), (0, 512)) for a in range(2)]
-        wc_dw = new("wc_dw", [2 * N], I32, tag="we_bf10")
+        wc_dw = [new("wc_dw0", [N], I32, tag="we_bf10")]
         nc.vector.tensor_copy(
-            wc_dw[:].rearrange("p (g t n) -> p g n t", g=4, t=PACK),
-            wc_w[:].rearrange("p a (g n t) -> p (a g) n t", g=2, t=PACK),
+            wc_dw[0][:].rearrange("p (g t n) -> p g n t", g=2, t=PACK),
+            wc_w[:, 0, :].rearrange("p (g n t) -> p g n t", g=2, t=PACK),
         )
         wc_ds = new("wc_ds", [N], U8)
         nc.vector.tensor_copy(
@@ -221,7 +221,7 @@ def tile_list_headbox_setpoint_step_kernel(
         tanh[1] = new("th1", [PACK, S], F32, tag="we11")
         slope = new("slope", [2, S], F32, tag="we_bf11")
         for i in (3, 2):
-            nc.vector.scalar_tensor_tensor(slope[:, i % 2, :], sq0[i][:], -1.0, error(0, i, we0)[:], ADD, MULT)
+            nc.vector.scalar_tensor_tensor(slope[:, i % 2, :], sq0[i][:], -1.0, error_banks[i][:], ADD, MULT)
         nc.vector.tensor_tensor(sq0[3][:], slope[:, 1, :], step[:], MULT)
         nc.vector.tensor_tensor(pages[2][:].indirect(place[:]), slope[:, 0, :], step[:], MULT)
         nc.vector.tensor_copy(pages[3][:].indirect(place[:]), sq0[3][:])
@@ -268,6 +268,11 @@ def tile_list_headbox_setpoint_step_kernel(
             factor = new(f"factor{i}", [S], F32, tag="we_bf11")
             nc.gpsimd.tensor_tensor(factor[:], ready[i][:], step[:], MULT)
             nc.gpsimd.tensor_tensor(ready[i][:], errors[i][:], factor[:], MULT)
+        wc_dw.append(new("wc_dw1", [N], I32, tag="we_bf11"))
+        nc.gpsimd.tensor_copy(
+            wc_dw[1][:].rearrange("p (g t n) -> p g t n", g=2, t=PACK),
+            wc_w[:, 1, :].rearrange("p (g n t) -> p g t n", g=2, t=PACK),
+        )
         zt0 = [new(f"zt0{mh}", [2, 2, 2, 2 * P], BF16, tag=tag) for mh, tag in enumerate(("we_c11", "we11"))]
         add_turned(0, 0, pages[0:2], high, range(4))
         round_turned([zt0[mq // 2][:, mq % 2, :, 0, :] for mq in range(4)], high, range(4))
@@ -350,7 +355,7 @@ def tile_list_headbox_setpoint_step_kernel(
                 c0 = KP * g + P * (share * k + s)
                 nc.tensor.matmul_mx(
                     group[k][:, s * width : (s + 1) * width],
-                    lhsT=wc_dw[:, N * a + c0 : N * a + c0 + P].bitcast(FP8X4),
+                    lhsT=wc_dw[a][:, c0 : c0 + P].bitcast(FP8X4),
                     lhsT_scale=wc_ds[4 * a :, c0 : c0 + P],
                     rhs=codes[:, cols].bitcast(FP8X4),
                     rhs_scale=scales[:, cols],

@@ -48,8 +48,6 @@ def tile_list_headbox_setpoint_step_kernel(
         pages = [new(f"page{u}", [T2], F32) for u in range(2)]
         for page in pages:
             nc.vector.memset(page[:], 0.0)
-        ident = new("ident", [P], F32)
-        make_identity(nc, ident[:])
 
         pick = lists.tile([P, S // 16], U16, name="pick")
         place = lists.tile([P, S // 16], U16, name="place")
@@ -207,6 +205,8 @@ def tile_list_headbox_setpoint_step_kernel(
         for u, tag in enumerate(("wf_w1", "we_c00", "we_c01", "we_s01")):
             pages.append(new(f"page{u + 2}", [T2], F32, tag=tag))
             nc.gpsimd.memset(pages[-1][:], 0.0)
+        ident = new("ident", [P], F32, tag="we_s00")
+        make_identity(nc, ident[:])
         we1 = [quantize_we(1, a, round_we(1, a, (nc.scalar.copy,)), (0, 512)) for a in range(2)]
         wc_dw = [new("wc_dw0", [N], I32, tag="we_bf10")]
         nc.vector.tensor_copy(

@@ -33,6 +33,7 @@ def tile_list_headbox_setpoint_step_kernel(
     with ExitStack() as ctx:
         lists = ctx.enter_context(tc.tile_pool(name="lists", bufs=1))
         sb = ctx.enter_context(tc.tile_pool(name="sb", bufs=1))
+        late = ctx.enter_context(tc.tile_pool(name="late", bufs=1))
         psum = ctx.enter_context(tc.psum_pool(name="psum", bufs=1))
 
         def new(name, shape, dtype, tag=None):
@@ -55,9 +56,9 @@ def tile_list_headbox_setpoint_step_kernel(
         def load_words(tile_ap, words):
             nc.sync.dma_start(tile_ap, words.rearrange("p c i -> p (c i)").bitcast(I32))
 
-        def load_rows(rows, scales):
+        def load_rows(queue, rows, scales):
             for r in range(4):
-                nc.sync.dma_start(
+                queue.dma_start(
                     rows[r:P:32, :, :].bitcast(I32),
                     scales[:, r:16:4, :].rearrange("a q c -> q a c").bitcast(I32),
                 )
@@ -83,11 +84,13 @@ def tile_list_headbox_setpoint_step_kernel(
             )
 
         nc.sync.dma_start(pick[:], offs)
-        load_rows(tab_s, tab_scales)
         load_words(tab_w[0][:], tab_words[0])
-        load_wf(0)
-        load_rows(wf_s, wf_scales)
+        load_rows(nc.sync, tab_s, tab_scales)
         load_words(tab_w[1][:], tab_words[1])
+        load_wf(0)
+        load_rows(nc.sync, wf_s, wf_scales)
+        ident = new("ident", [P], F32)
+        make_identity(nc, ident[:])
         we_raw = {(0, 0): [load_we("we00", 0, 0, KP)]}
         we_raw[0, 1] = [load_we(f"we01{u}", 1, u * KP // 2, KP // 2) for u in range(2)]
         load_wf(1)
@@ -96,13 +99,14 @@ def tile_list_headbox_setpoint_step_kernel(
         nc.sync.dma_start(place[:], offs2)
         for a in range(2):
             we_raw[1, a] = [load_we(f"we1{a}", a, KP, KP)]
-        wc_w = new("wc_w", [2, N], I32)
-        nc.sync.dma_start(wc_w[:], wc_words.rearrange("a p c i -> p a (c i)").bitcast(I32))
         for q in range(4):
             nc.sync.dma_start(
                 wc_s[32 * q : 32 * q + 8, :].bitcast(I32), wc_scales[:, 4 * q : 4 * q + 4, :].bitcast(I32)
             )
-        sp_t = {(0, h): load_sp(0, h, None) for h in range(2)}
+        sp_t = {(0, 0): load_sp(0, 0, None)}
+        wc_w = new("wc_w", [2, N], I32)
+        nc.sync.dma_start(wc_w[:], wc_words.rearrange("a p c i -> p a (c i)").bitcast(I32))
+        sp_t[0, 1] = load_sp(0, 1, None)
 
         v_w = [new(f"v_w{a}", [S], U32) for a in range(2)]
         v_s = [new(f"v_s{a}", [S], U8) for a in range(2)]
@@ -113,19 +117,24 @@ def tile_list_headbox_setpoint_step_kernel(
         for h in range(2):
             sp_t[1, h] = load_sp(1, h, f"tab_w{h}")
 
-        wf_dw, wf_ds = [], []
+        wf_dw, wf_ds = {}, []
 
-        def deal_wf(b):
-            words = new(f"wf_dw{b}", [2, PACK, P], U16)
-            nc.vector.tensor_copy(words[:], wf_w[b][:].bitcast(U16).rearrange("p a (m i) -> p a i m", i=PACK))
+        def deal_wf_words(b, first, words):
+            count = words.shape[2]
+            source = wf_w[b][:].bitcast(U16).rearrange("p a (m i) -> p a i m", i=PACK)
+            nc.scalar.copy(words, source[:, :, first : first + count, :])
+            for u in range(count):
+                wf_dw[b, first + u] = words[:, :, u, :]
+
+        def deal_wf_scales(b):
             scales = new(f"wf_ds{b}", [2, PACK, P], U8)
             nc.vector.tensor_copy(
                 scales[:], wf_s[:, :, KP * b : KP * (b + 1)].rearrange("p a (m i) -> p a i m", i=PACK)
             )
-            wf_dw.append(words)
             wf_ds.append(scales)
 
-        deal_wf(0)
+        deal_wf_words(0, 0, new("wf_dw0", [2, 2, P], U16)[:])
+        deal_wf_scales(0)
 
         def round_we(b, a, copies):
             rounded = new(f"we_bf{b}{a}", [PACK * KP], BF16)
@@ -154,7 +163,7 @@ def tile_list_headbox_setpoint_step_kernel(
             for a in range(2):
                 nc.tensor.matmul_mx(
                     bank[:],
-                    lhsT=wf_dw[b][:, a, i, :].bitcast(FP4X4),
+                    lhsT=wf_dw[b, i][:, a, :].bitcast(FP4X4),
                     lhsT_scale=wf_ds[b][:, a, i, :],
                     rhs=v_w[a][:].bitcast(FP8X4),
                     rhs_scale=v_s[a][:],
@@ -163,8 +172,7 @@ def tile_list_headbox_setpoint_step_kernel(
                 )
             return bank
 
-        def error(b, i, quantized):
-            bank = banks[4 * b + i]
+        def error(i, quantized, bank):
             cols = slice(i * P, (i + 1) * P)
             for a, (codes, scales) in enumerate(quantized):
                 nc.tensor.matmul_mx(
@@ -179,79 +187,96 @@ def tile_list_headbox_setpoint_step_kernel(
             return bank
 
         rounded00 = round_we(0, 0, (nc.scalar.copy, nc.vector.tensor_copy))
-        tanh = {0: new("th0", [PACK, S], F32, tag="we00")}
+        tanh = {}
+
+        def hold_tanh(b, first, count, tag):
+            held = new(f"th{b}{first}", [count, S], F32, tag=tag)
+            for u in range(count):
+                tanh[b, first + u] = held[:, u, :]
+
+        hold_tanh(0, 0, 2, "we00")
 
         def tanh_of(b, i):
-            nc.scalar.activation(tanh[b][:, i, :], forward(b, i)[:], TANH)
+            nc.scalar.activation(tanh[b, i], forward(b, i)[:], TANH)
 
         def square_of(b, i):
             sq = new(f"sq{b}{i}", [S], F32)
-            nc.scalar.activation(sq[:], tanh[b][:, i, :], SQUARE)
+            nc.scalar.activation(sq[:], tanh[b, i], SQUARE)
             return sq
 
         rounded01 = round_we(0, 1, (nc.vector.tensor_copy, nc.vector.tensor_copy))
         we0 = [quantize_we(0, 0, rounded00, (0, 512)), quantize_we(0, 1, rounded01, (0, 128, 256, 512))]
-        deal_wf(1)
         sq0 = []
-        for pair in ((0, 1), (2, 3)):
-            for i in pair:
-                tanh_of(0, i)
-            sq0.extend(square_of(0, i) for i in pair)
         for i in range(2):
-            nc.vector.scalar_tensor_tensor(sq0[i][:], sq0[i][:], -1.0, error(0, i, we0)[:], ADD, MULT)
+            tanh_of(0, i)
+            sq0.append(square_of(0, i))
+        later_words = new("wf_dw1", [2, 6, P], U16, tag="we00")
+        deal_wf_words(1, 0, later_words[:, :, 2:, :])
+        deal_wf_words(0, 2, later_words[:, :, :2, :])
+        deal_wf_scales(1)
+        for i in range(2):
+            nc.vector.scalar_tensor_tensor(sq0[i][:], sq0[i][:], -1.0, error(i, we0, banks[i])[:], ADD, MULT)
         for i in range(2):
             nc.vector.tensor_tensor(pages[i][:].indirect(place[:]), sq0[i][:], step[:], MULT)
-        error_banks = {i: error(0, i, we0) for i in (3, 2)}
-        for u, tag in enumerate(("wf_w1", "we_c00", "we_c01", "we_s01")):
+        a0, a1, a2, a3, b0, b1, b2, b3 = banks
+        late_errors = [error(i, we0, banks[i]) for i in (2, 3)]
+        for u, tag in enumerate(("wf_w1", "we_c00")):
             pages.append(new(f"page{u + 2}", [T2], F32, tag=tag))
             nc.gpsimd.memset(pages[-1][:], 0.0)
-        ident = new("ident", [P], F32, tag="we_s00")
-        make_identity(nc, ident[:])
-        we1 = [quantize_we(1, a, round_we(1, a, (nc.scalar.copy,)), (0, 512)) for a in range(2)]
-        wc_dw = [new("wc_dw0", [N], I32, tag="we_bf10")]
-        nc.vector.tensor_copy(
-            wc_dw[0][:].rearrange("p (g t n) -> p g n t", g=2, t=PACK),
-            wc_w[:, 0, :].rearrange("p (g n t) -> p g n t", g=2, t=PACK),
-        )
+        rounded1 = [round_we(1, a, (nc.scalar.copy,)) for a in range(2)]
         wc_ds = new("wc_ds", [N], U8)
         nc.vector.tensor_copy(
             wc_ds[:].rearrange("p (g t n) -> p g t n", g=2, t=PACK),
             wc_s[:].rearrange("p (g n t) -> p g t n", g=2, t=PACK),
         )
-        tanh[1] = new("th1", [PACK, S], F32, tag="we11")
-        slope = new("slope", [2, S], F32, tag="we_bf11")
-        for i in (3, 2):
-            nc.vector.scalar_tensor_tensor(slope[:, i % 2, :], sq0[i][:], -1.0, error_banks[i][:], ADD, MULT)
-        nc.vector.tensor_tensor(sq0[3][:], slope[:, 1, :], step[:], MULT)
-        nc.vector.tensor_tensor(pages[2][:].indirect(place[:]), slope[:, 0, :], step[:], MULT)
-        nc.vector.tensor_copy(pages[3][:].indirect(place[:]), sq0[3][:])
+        we1 = [quantize_we(1, a, rounded1[a], (0, 512)) for a in range(2)]
+        hold_tanh(0, 2, 2, "we10")
+        hold_tanh(1, 0, PACK, "we11")
+        squares = []
+        for b, i in ((0, 2), (0, 3), (1, 0)):
+            tanh_of(b, i)
+            squares.append(square_of(b, i))
+        late_errors.append(error(0, we1, b0))
+        slope = new("slope", [3, S], F32, tag="we_bf11")
+        for u in range(3):
+            nc.vector.scalar_tensor_tensor(slope[:, u, :], squares[u][:], -1.0, late_errors[u][:], ADD, MULT)
+        for u in range(3):
+            nc.gpsimd.tensor_tensor(squares[u][:], slope[:, u, :], step[:], MULT)
 
-        errors = []
+        def put(page, values):
+            nc.vector.tensor_copy(page[:].indirect(place[:]), values[:])
 
-        def corrections(pair):
-            made = [square_of(1, i) for i in pair]
-            for i, sq in zip(pair, made):
-                nc.scalar.activation(sq[:], sq[:], IDENTITY, bias=-1.0)
-                e = new(f"e1{i}", [S], F32)
-                nc.scalar.copy(e[:], error(1, i, we1)[:])
-                errors.append(e)
-            return made
+        put(pages[2], squares[0])
+        put(pages[3], squares[1])
 
-        def add_turned(b, h, pair_pages, sums, quarters):
+        def factor_of(i, both):
+            nc.scalar.activation(both[:, 0, :], tanh[1, i], SQUARE)
+            nc.scalar.activation(both[:, 0, :], both[:, 0, :], IDENTITY, bias=-1.0)
+            nc.gpsimd.tensor_tensor(both[:, 1, :], both[:, 0, :], step[:], MULT)
+            return both[:, 1, :]
+
+        def correction(i, factor, bank):
+            e = new(f"e1{i}", [S], F32)
+            nc.scalar.copy(e[:], error(i, we1, bank)[:])
+            nc.gpsimd.tensor_tensor(e[:], e[:], factor, MULT)
+            return e
+
+        def add_turned(b, h, pair_pages, sums, order):
             sources = [sp_t[b, h][:, e, :] for e in range(2)] + [page[:] for page in pair_pages]
-            for mq in quarters:
-                view = sums[mq][:].rearrange("m (mb e p) -> m mb e p", mb=2, e=2)
-                for u in range(4):
-                    for mb in range(2):
-                        c0 = (2 * mq + mb) * P
-                        nc.tensor.matmul(
-                            view[:, mb, u % 2, :],
-                            sources[u][:, c0 : c0 + P],
-                            ident[:],
-                            start=(u == 0 and mb == 0),
-                            stop=(u == 3 and mb == 1),
-                            is_transpose=True,
-                        )
+            for terms in ((0, 1, 2), (3,)):
+                for mq in order:
+                    view = sums[mq][:].rearrange("m (mb e p) -> m mb e p", mb=2, e=2)
+                    for u in terms:
+                        for mb in range(2):
+                            c0 = (2 * mq + mb) * P
+                            nc.tensor.matmul(
+                                view[:, mb, u % 2, :],
+                                sources[u][:, c0 : c0 + P],
+                                ident[:],
+                                start=(u == 0 and mb == 0),
+                                stop=(u == 3 and mb == 1),
+                                is_transpose=True,
+                            )
 
         def round_turned(targets, sums, quarters):
             for mq in quarters:
@@ -260,89 +285,90 @@ def tile_list_headbox_setpoint_step_kernel(
                     sums[mq][:].rearrange("m (mb e p) -> m mb p e", mb=2, e=2),
                 )
 
-        high, low = banks[:4], banks[4:]
-        for i in range(PACK):
+        for i in range(1, PACK):
             tanh_of(1, i)
-        ready = corrections((0, 1)) + corrections((2, 3))
-        for i in range(PACK):
-            factor = new(f"factor{i}", [S], F32, tag="we_bf11")
-            nc.gpsimd.tensor_tensor(factor[:], ready[i][:], step[:], MULT)
-            nc.gpsimd.tensor_tensor(ready[i][:], errors[i][:], factor[:], MULT)
-        wc_dw.append(new("wc_dw1", [N], I32, tag="we_bf11"))
-        nc.gpsimd.tensor_copy(
-            wc_dw[1][:].rearrange("p (g t n) -> p g t n", g=2, t=PACK),
-            wc_w[:, 1, :].rearrange("p (g n t) -> p g t n", g=2, t=PACK),
-        )
-        zt0 = [new(f"zt0{mh}", [2, 2, 2, 2 * P], BF16, tag=tag) for mh, tag in enumerate(("we_c11", "we11"))]
-        add_turned(0, 0, pages[0:2], high, range(4))
-        round_turned([zt0[mq // 2][:, mq % 2, :, 0, :] for mq in range(4)], high, range(4))
-        late_pages = [pages[4], pages[5], pages[0], pages[1]]
-        for i in range(2):
-            nc.vector.tensor_copy(late_pages[i][:].indirect(place[:]), ready[i][:])
-        add_turned(0, 1, pages[2:4], low, range(4))
-        round_turned([zt0[mq // 2][:, mq % 2, :, 1, :] for mq in range(4)], low, range(4))
-        z_bf0 = new("z_bf0", [T2 * PACK], BF16)
+        ready = {i: correction(i, factor_of(i, new(f"factor{i}", [2, S], F32)), banks[4 + i]) for i in (1, 2)}
+        zt0 = [new(f"zt0{mh}", [2, 2, 2, 2 * P], BF16) for mh in range(2)]
+        sums = [a0, a1, a2, a3]
         for mq in range(4):
-            view = high[mq][:].rearrange("p (mb h m) -> p mb h m", mb=2, h=2)
+            add_turned(0, 0, pages[0:2], sums, (mq,))
+        round_turned([zt0[mq // 2][:, mq % 2, :, 0, :] for mq in range(4)], sums, range(4))
+        last_factor = factor_of(3, late.tile([P, 2, S], F32, name="factor3", offset=0, align_bytes=64))
+        wc_dw = {1: new("wc_dw1", [N], I32, tag="factor2")}
+        for g in range(2):
+            nc.gpsimd.tensor_copy(
+                wc_dw[1][:, KP * g : KP * (g + 1)].rearrange("p (t n) -> p t n", t=PACK),
+                wc_w[:, 1, KP * g : KP * (g + 1)].rearrange("p (n t) -> p t n", t=PACK),
+            )
+        put(pages[0], squares[2])
+        put(pages[1], ready[1])
+        add_turned(0, 1, pages[2:4], sums, range(4))
+        round_turned([zt0[mq // 2][:, mq % 2, :, 1, :] for mq in range(4)], sums, range(4))
+        put(pages[2], ready[2])
+        z_bf0 = [new(f"z_bf0{mh}", [BANK * PACK], BF16) for mh in range(2)]
+        for mq, bank in enumerate((b0, b3, b1, b2)):
+            view = bank[:].rearrange("p (mb h m) -> p mb h m", mb=2, h=2)
             words = zt0[mq // 2][:, mq % 2].bitcast(F32)
             for mb in range(2):
                 for h in range(2):
                     nc.tensor.transpose(view[:, mb, h, :], words[:, mb, h, :], ident[:])
-            target = z_bf0[:].bitcast(F32).rearrange("p (q mb m h) -> p q mb m h", q=4, mb=2, h=2)
-            nc.scalar.copy(target[:, mq], view.rearrange("p mb h m -> p mb m h"))
-        nc.vector.tensor_copy(late_pages[2][:].indirect(place[:]), ready[2][:])
-        add_turned(1, 0, late_pages[0:2], low, range(4))
-        zt1 = [new(f"zt1{mq}", [2, 2 * P], BF16)[:] for mq in range(4)]
-        z_bf1 = [new(f"z_bf1{c}", [width * PACK], BF16) for c, width in enumerate((256, 256, 512))]
-        for quarters in ((0, 1), (2, 3)):
-            round_turned(zt1, low, quarters)
-            for mq in quarters:
-                words = zt1[mq].bitcast(F32)
-                for mb in range(2):
-                    nc.tensor.transpose(high[mq][:, mb * P : (mb + 1) * P], words[:, mb, :], ident[:])
-                target = z_bf1[min(mq, 2)][:].bitcast(F32).rearrange("p (q m h) -> p q m h", m=2 * P, h=2)
-                nc.scalar.copy(target[:, max(mq - 2, 0), :, 0], high[mq][:, : 2 * P])
+            target = z_bf0[mq // 2][:].bitcast(F32).rearrange("p (q mb m h) -> p q mb m h", q=2, mb=2, h=2)
+            nc.scalar.copy(target[:, mq % 2], view.rearrange("p mb h m -> p mb m h"))
+            if mq == 1:
+                ready[3] = correction(3, last_factor, b3)
 
-        chunks = ((0, 256), (256, 256), (512, 512))
-        last_rows = [
-            new(f"last_rows{c}", [2, width], BF16, tag=tag)[:]
-            for c, ((c0, width), tag) in enumerate(zip(chunks, ("e13", "zt11", "zt13")))
-        ]
-        nc.gpsimd.tensor_tensor(last_rows[0][:, 0, :], sp_t[1, 1][:, 0, :256], late_pages[2][:, :256], ADD)
-        nc.vector.tensor_copy(late_pages[3][:].indirect(place[:]), ready[3][:])
-
-        def last_sum(c):
-            cols = slice(chunks[c][0], sum(chunks[c]))
-            for e in range(1 if c == 0 else 0, 2):
-                nc.vector.tensor_tensor(last_rows[c][:, e, :], sp_t[1, 1][:, e, cols], late_pages[2 + e][:, cols], ADD)
-
-        def pair_up(c):
-            nc.vector.tensor_copy(
-                z_bf1[c][:].rearrange("p (m h e) -> p m h e", h=2, e=2)[:, :, 1, :],
-                last_rows[c].rearrange("p e m -> p m e"),
-            )
+        wc_dw[0] = new("wc_dw0", [N], U32, tag="zt01")
+        nc.scalar.copy(
+            wc_dw[0][:].rearrange("p (g t n) -> p g t n", g=2, t=PACK),
+            wc_w[:, 0, :].bitcast(U32).rearrange("p (g n t) -> p g t n", g=2, t=PACK),
+        )
 
         z_q = {}
 
-        def quantize_z(c):
-            cols = slice(chunks[c][0], sum(chunks[c]))
-            whole = slice(PACK * cols.start, PACK * cols.stop)
-            for b, source in enumerate((z_bf0[:, whole], z_bf1[c][:])):
-                tag = {(0, 1): "zt10", (0, 2): "zt12"}.get((b, c))
-                codes = new(f"z_c{b}{c}", [chunks[c][1]], U32, tag=tag)
-                scales = new(f"z_s{b}{c}", [chunks[c][1]], U8)
-                nc.vector.quantize_mx(codes[:].bitcast(FP8X4), scales[:], source)
-                z_q[b, c] = (codes, scales)
+        def quantize_z(name, source, width, tag=None):
+            codes = new(f"z_c{name}", [width], U32, tag=tag)
+            scales = new(f"z_s{name}", [width], U8)
+            nc.vector.quantize_mx(codes[:].bitcast(FP8X4), scales[:], source)
+            return codes, scales
+
+        first_half = quantize_z("00", z_bf0[0][:], BANK)
+        for c in range(2):
+            z_q[0, c] = tuple(part[:, 256 * c : 256 * (c + 1)] for part in first_half)
+
+        add_turned(1, 0, pages[0:2], sums, range(4))
+        zt1 = [new(f"zt1{mq}", [2, 2 * P], BF16)[:] for mq in range(4)]
+        shared = late.tile([P, BANK + 256 * PACK], BF16, name="shared", offset=4 * BANK, align_bytes=64)
+        z_bf1 = [shared[:, BANK:], new("z_bf11", [256 * PACK], BF16)[:], new("z_bf12", [BANK * PACK], BF16)[:]]
+        for quarters in ((0, 1), (2, 3)):
+            round_turned(zt1, sums, quarters)
+            for mq in quarters:
+                bank = (b0, b1, b2, b3)[mq]
+                words = zt1[mq].bitcast(F32)
+                for mb in range(2):
+                    nc.tensor.transpose(bank[:, mb * P : (mb + 1) * P], words[:, mb, :], ident[:])
+                target = z_bf1[min(mq, 2)].bitcast(F32).rearrange("p (q m h) -> p q m h", m=2 * P, h=2)
+                nc.scalar.copy(target[:, max(mq - 2, 0), :, 0], bank[:, : 2 * P])
+
+        chunks = ((0, 256), (256, 256), (512, 512))
+        last_rows = [
+            late.tile([P, 2, width], BF16, name=f"last_rows{c}", offset=4 * c0, align_bytes=64)[:]
+            for c, (c0, width) in enumerate(chunks[:2])
+        ]
+        last_rows.append(shared[:, : 2 * BANK].rearrange("p (e m) -> p e m", e=2))
+        for c, (c0, width) in enumerate(chunks):
+            cols = slice(c0, c0 + width)
+            nc.gpsimd.tensor_tensor(last_rows[c][:, 0, :], sp_t[1, 1][:, 0, cols], pages[2][:, cols], ADD)
+        put(pages[3], ready[3])
 
         y_s = [new(f"y_s{mh}", [2, BANK], U8) for mh in range(2)]
         units = (
-            (0, 0, 256, low[:2], "we010"),
-            (1, 0, 256, low[2:], "we011"),
-            (0, 256, 256, high[:2], "sp00"),
-            (1, 256, 256, high[2:], "sp01"),
-            (0, 512, 512, low, "we00"),
-            (1, 512, 256, high[:2], "tab_w0"),
-            (1, 768, 256, high[2:], "we11"),
+            (0, 0, 256, (a0, a1), "we010"),
+            (1, 0, 256, (a2, a3), "we011"),
+            (0, 256, 256, (b0, b1), "sp00"),
+            (1, 256, 256, (b2, b3), "sp01"),
+            (0, 512, 512, (a0, a1, a2, a3), "we00"),
+            (1, 512, 256, (b0, b1), "tab_w0"),
+            (1, 768, 256, (b2, b3), "we10"),
         )
 
         def last_passes(u, k, a):
@@ -363,10 +389,20 @@ def tile_list_headbox_setpoint_step_kernel(
                     stop=(a == 1 and s == share - 1),
                 )
 
-        for c in range(3):
-            last_sum(c)
-            pair_up(c)
-            quantize_z(c)
+        for u in range(4):
+            for k in range(2):
+                last_passes(u, k, 0)
+
+        for c, (c0, width) in enumerate(chunks):
+            cols = slice(c0, c0 + width)
+            nc.vector.tensor_tensor(last_rows[c][:, 1, :], sp_t[1, 1][:, 1, cols], pages[3][:, cols], ADD)
+            if c == 2:
+                z_q[0, 2] = tuple(part[:] for part in quantize_z("02", z_bf0[1][:], BANK, tag="z_bf11"))
+            nc.vector.tensor_copy(
+                z_bf1[c].rearrange("p (m h e) -> p m h e", h=2, e=2)[:, :, 1, :],
+                last_rows[c].rearrange("p e m -> p m e"),
+            )
+            z_q[1, c] = tuple(part[:] for part in quantize_z(f"1{c}", z_bf1[c], width))
 
         for u, (g, m0, width, group, tag) in enumerate(units):
             cols = slice(m0, m0 + width)
@@ -374,7 +410,7 @@ def tile_list_headbox_setpoint_step_kernel(
             rows = out_0[KP * g : KP * (g + 1), cols].rearrange("(p t) m -> p t m", t=PACK)
             share = BANK // width
             for k, bank in enumerate(group):
-                for a in range(2):
+                for a in range(1 if u < 4 else 0, 2):
                     last_passes(u, k, a)
                 done = share * (k + 1)
                 nc.scalar.copy(y[:, done - share : done, :], bank[:].rearrange("p (s m) -> p s m", s=share))

@@ -233,21 +233,18 @@ def tile_list_headbox_setpoint_step_kernel(
         hold_tanh(0, 2, 2, "we10")
         hold_tanh(1, 0, PACK, "we11")
         squares = []
-        for b, i in ((0, 2), (0, 3), (1, 0)):
+        for b, i in ((0, 2), (0, 3), (1, 0), (1, 1)):
             tanh_of(b, i)
             squares.append(square_of(b, i))
-        late_errors.append(error(0, we1, b0))
-        slope = new("slope", [3, S], F32, tag="we_bf11")
-        for u in range(3):
+        late_errors.extend(error(i, we1, banks[4 + i]) for i in range(2))
+        slope = new("slope", [4, S], F32, tag="we_bf11")
+        for u in range(4):
             nc.vector.scalar_tensor_tensor(slope[:, u, :], squares[u][:], -1.0, late_errors[u][:], ADD, MULT)
-        for u in range(3):
+        for u in range(4):
             nc.gpsimd.tensor_tensor(squares[u][:], slope[:, u, :], step[:], MULT)
 
         def put(page, values):
             nc.vector.tensor_copy(page[:].indirect(place[:]), values[:])
-
-        put(pages[2], squares[0])
-        put(pages[3], squares[1])
 
         def factor_of(i, both):
             nc.scalar.activation(both[:, 0, :], tanh[1, i], SQUARE)
@@ -255,9 +252,8 @@ def tile_list_headbox_setpoint_step_kernel(
             nc.gpsimd.tensor_tensor(both[:, 1, :], both[:, 0, :], step[:], MULT)
             return both[:, 1, :]
 
-        def correction(i, factor, bank):
-            e = new(f"e1{i}", [S], F32)
-            nc.scalar.copy(e[:], error(i, we1, bank)[:])
+        def correction(factor, bank, e):
+            nc.scalar.copy(e[:], bank[:])
             nc.gpsimd.tensor_tensor(e[:], e[:], factor, MULT)
             return e
 
@@ -278,35 +274,44 @@ def tile_list_headbox_setpoint_step_kernel(
                                 is_transpose=True,
                             )
 
-        def round_turned(targets, sums, quarters):
+        def round_turned(copy, targets, sums, quarters):
             for mq in quarters:
-                nc.scalar.copy(
+                copy(
                     targets[mq].rearrange("m mb (p e) -> m mb p e", e=2),
                     sums[mq][:].rearrange("m (mb e p) -> m mb p e", mb=2, e=2),
                 )
 
-        for i in range(1, PACK):
-            tanh_of(1, i)
-        ready = {i: correction(i, factor_of(i, new(f"factor{i}", [2, S], F32)), banks[4 + i]) for i in (1, 2)}
         zt0 = [new(f"zt0{mh}", [2, 2, 2, 2 * P], BF16) for mh in range(2)]
         sums = [a0, a1, a2, a3]
         for mq in range(4):
             add_turned(0, 0, pages[0:2], sums, (mq,))
-        round_turned([zt0[mq // 2][:, mq % 2, :, 0, :] for mq in range(4)], sums, range(4))
-        last_factor = factor_of(3, late.tile([P, 2, S], F32, name="factor3", offset=0, align_bytes=64))
-        wc_dw = {1: new("wc_dw1", [N], I32, tag="factor2")}
-        for g in range(2):
-            nc.gpsimd.tensor_copy(
-                wc_dw[1][:, KP * g : KP * (g + 1)].rearrange("p (t n) -> p t n", t=PACK),
-                wc_w[:, 1, KP * g : KP * (g + 1)].rearrange("p (n t) -> p t n", t=PACK),
+        targets = [zt0[mq // 2][:, mq % 2, :, 0, :] for mq in range(4)]
+        round_turned(nc.scalar.copy, targets, sums, range(4))
+        put(pages[2], squares[0])
+        put(pages[3], squares[1])
+        for i in (2, 3):
+            tanh_of(1, i)
+        for i in (2, 3):
+            error(i, we1, banks[4 + i])
+        ready = {2: correction(factor_of(2, new("factor2", [2, S], F32)), b2, new("e12", [S], F32))}
+        last_factor = factor_of(3, late.tile([P, 2, S], F32, name="factor3", offset=2 * BANK, align_bytes=64))
+        wc_dw = {}
+
+        def deal_wc(a, tag):
+            wc_dw[a] = new(f"wc_dw{a}", [N], U32, tag=tag)
+            nc.scalar.copy(
+                wc_dw[a][:].rearrange("p (g t n) -> p g n t", g=2, t=PACK),
+                wc_w[:, a, :].bitcast(U32).rearrange("p (g n t) -> p g n t", g=2, t=PACK),
             )
+
+        deal_wc(0, "we11")
         put(pages[0], squares[2])
-        put(pages[1], ready[1])
+        put(pages[1], squares[3])
         add_turned(0, 1, pages[2:4], sums, range(4))
-        round_turned([zt0[mq // 2][:, mq % 2, :, 1, :] for mq in range(4)], sums, range(4))
+        round_turned(nc.scalar.copy, [zt0[mq // 2][:, mq % 2, :, 1, :] for mq in range(4)], sums, range(4))
         put(pages[2], ready[2])
         z_bf0 = [new(f"z_bf0{mh}", [BANK * PACK], BF16) for mh in range(2)]
-        for mq, bank in enumerate((b0, b3, b1, b2)):
+        for mq, bank in enumerate((b0, b1, b2, b0)):
             view = bank[:].rearrange("p (mb h m) -> p mb h m", mb=2, h=2)
             words = zt0[mq // 2][:, mq % 2].bitcast(F32)
             for mb in range(2):
@@ -315,13 +320,9 @@ def tile_list_headbox_setpoint_step_kernel(
             target = z_bf0[mq // 2][:].bitcast(F32).rearrange("p (q mb m h) -> p q mb m h", q=2, mb=2, h=2)
             nc.scalar.copy(target[:, mq % 2], view.rearrange("p mb h m -> p mb m h"))
             if mq == 1:
-                ready[3] = correction(3, last_factor, b3)
+                ready[3] = correction(last_factor, b3, new("e13", [S], F32, tag="zt00"))
 
-        wc_dw[0] = new("wc_dw0", [N], U32, tag="zt01")
-        nc.scalar.copy(
-            wc_dw[0][:].rearrange("p (g t n) -> p g t n", g=2, t=PACK),
-            wc_w[:, 0, :].bitcast(U32).rearrange("p (g n t) -> p g t n", g=2, t=PACK),
-        )
+        deal_wc(1, "zt01")
 
         z_q = {}
 
@@ -337,12 +338,12 @@ def tile_list_headbox_setpoint_step_kernel(
 
         add_turned(1, 0, pages[0:2], sums, range(4))
         zt1 = [new(f"zt1{mq}", [2, 2 * P], BF16)[:] for mq in range(4)]
-        shared = late.tile([P, BANK + 256 * PACK], BF16, name="shared", offset=4 * BANK, align_bytes=64)
-        z_bf1 = [shared[:, BANK:], new("z_bf11", [256 * PACK], BF16)[:], new("z_bf12", [BANK * PACK], BF16)[:]]
+        shared = late.tile([P, 2 * BANK], F32, name="shared", offset=8 * BANK, align_bytes=64)
+        z_bf1 = [shared[:, BANK:].bitcast(BF16), new("z_bf11", [256 * PACK], BF16)[:], new("z_bf12", [BANK * PACK], BF16)[:]]
         for quarters in ((0, 1), (2, 3)):
-            round_turned(zt1, sums, quarters)
+            round_turned(nc.scalar.copy, zt1, sums, quarters)
             for mq in quarters:
-                bank = (b0, b1, b2, b3)[mq]
+                bank = (b3, b1, b2, b0)[mq]
                 words = zt1[mq].bitcast(F32)
                 for mb in range(2):
                     nc.tensor.transpose(bank[:, mb * P : (mb + 1) * P], words[:, mb, :], ident[:])
@@ -351,10 +352,10 @@ def tile_list_headbox_setpoint_step_kernel(
 
         chunks = ((0, 256), (256, 256), (512, 512))
         last_rows = [
-            late.tile([P, 2, width], BF16, name=f"last_rows{c}", offset=4 * c0, align_bytes=64)[:]
+            late.tile([P, 2, width], F32, name=f"last_rows{c}", offset=8 * c0, align_bytes=64)[:]
             for c, (c0, width) in enumerate(chunks[:2])
         ]
-        last_rows.append(shared[:, : 2 * BANK].rearrange("p (e m) -> p e m", e=2))
+        last_rows.append(shared[:].rearrange("p (e m) -> p e m", e=2))
         for c, (c0, width) in enumerate(chunks):
             cols = slice(c0, c0 + width)
             nc.gpsimd.tensor_tensor(last_rows[c][:, 0, :], sp_t[1, 1][:, 0, cols], pages[2][:, cols], ADD)
@@ -364,11 +365,11 @@ def tile_list_headbox_setpoint_step_kernel(
         units = (
             (0, 0, 256, (a0, a1), "we010"),
             (1, 0, 256, (a2, a3), "we011"),
-            (0, 256, 256, (b0, b1), "sp00"),
-            (1, 256, 256, (b2, b3), "sp01"),
+            (0, 256, 256, (b3, b1), "sp00"),
+            (1, 256, 256, (b2, b0), "sp01"),
             (0, 512, 512, (a0, a1, a2, a3), "we00"),
-            (1, 512, 256, (b0, b1), "tab_w0"),
-            (1, 768, 256, (b2, b3), "we10"),
+            (1, 512, 256, (b3, b1), "tab_w0"),
+            (1, 768, 256, (b2, b0), "we10"),
         )
 
         def last_passes(u, k, a):

@@ -84,11 +84,11 @@ def tile_list_headbox_setpoint_step_kernel(
             )
 
         nc.sync.dma_start(pick[:], offs)
-        load_words(tab_w[0][:], tab_words[0])
         load_rows(nc.sync, tab_s, tab_scales)
-        load_words(tab_w[1][:], tab_words[1])
+        load_words(tab_w[0][:], tab_words[0])
         load_wf(0)
         load_rows(nc.sync, wf_s, wf_scales)
+        load_words(tab_w[1][:], tab_words[1])
         ident = new("ident", [P], F32)
         make_identity(nc, ident[:])
         we_raw = {(0, 0): [load_we("we00", 0, 0, KP)]}
@@ -117,14 +117,12 @@ def tile_list_headbox_setpoint_step_kernel(
         for h in range(2):
             sp_t[1, h] = load_sp(1, h, f"tab_w{h}")
 
-        wf_dw, wf_ds = {}, []
+        wf_dw, wf_ds = [], []
 
-        def deal_wf_words(b, first, words):
-            count = words.shape[2]
-            source = wf_w[b][:].bitcast(U16).rearrange("p a (m i) -> p a i m", i=PACK)
-            nc.scalar.copy(words, source[:, :, first : first + count, :])
-            for u in range(count):
-                wf_dw[b, first + u] = words[:, :, u, :]
+        def deal_wf_words(b):
+            words = new(f"wf_dw{b}", [2, PACK, P], U16)
+            nc.vector.tensor_copy(words[:], wf_w[b][:].bitcast(U16).rearrange("p a (m i) -> p a i m", i=PACK))
+            wf_dw.append(words)
 
         def deal_wf_scales(b):
             scales = new(f"wf_ds{b}", [2, PACK, P], U8)
@@ -133,7 +131,7 @@ def tile_list_headbox_setpoint_step_kernel(
             )
             wf_ds.append(scales)
 
-        deal_wf_words(0, 0, new("wf_dw0", [2, 2, P], U16)[:])
+        deal_wf_words(0)
         deal_wf_scales(0)
 
         def round_we(b, a, copies):
@@ -158,12 +156,11 @@ def tile_list_headbox_setpoint_step_kernel(
                 )
             return codes, scales
 
-        def forward(b, i):
-            bank = banks[4 + i]
+        def forward(b, i, bank):
             for a in range(2):
                 nc.tensor.matmul_mx(
                     bank[:],
-                    lhsT=wf_dw[b, i][:, a, :].bitcast(FP4X4),
+                    lhsT=wf_dw[b][:, a, i, :].bitcast(FP4X4),
                     lhsT_scale=wf_ds[b][:, a, i, :],
                     rhs=v_w[a][:].bitcast(FP8X4),
                     rhs_scale=v_s[a][:],
@@ -194,10 +191,10 @@ def tile_list_headbox_setpoint_step_kernel(
             for u in range(count):
                 tanh[b, first + u] = held[:, u, :]
 
-        hold_tanh(0, 0, 2, "we00")
+        hold_tanh(0, 0, PACK, "we00")
 
         def tanh_of(b, i):
-            nc.scalar.activation(tanh[b, i], forward(b, i)[:], TANH)
+            nc.scalar.activation(tanh[b, i], forward(b, i, banks[4 + i])[:], TANH)
 
         def square_of(b, i):
             sq = new(f"sq{b}{i}", [S], F32)
@@ -210,10 +207,8 @@ def tile_list_headbox_setpoint_step_kernel(
         for i in range(2):
             tanh_of(0, i)
             sq0.append(square_of(0, i))
-        later_words = new("wf_dw1", [2, 6, P], U16, tag="we00")
-        deal_wf_words(1, 0, later_words[:, :, 2:, :])
-        deal_wf_words(0, 2, later_words[:, :, :2, :])
         deal_wf_scales(1)
+        deal_wf_words(1)
         for i in range(2):
             nc.vector.scalar_tensor_tensor(sq0[i][:], sq0[i][:], -1.0, error(i, we0, banks[i])[:], ADD, MULT)
         for i in range(2):
@@ -223,6 +218,10 @@ def tile_list_headbox_setpoint_step_kernel(
         for u, tag in enumerate(("wf_w1", "we_c00")):
             pages.append(new(f"page{u + 2}", [T2], F32, tag=tag))
             nc.gpsimd.memset(pages[-1][:], 0.0)
+        squares = []
+        for i in (2, 3):
+            tanh_of(0, i)
+            squares.append(square_of(0, i))
         rounded1 = [round_we(1, a, (nc.scalar.copy,)) for a in range(2)]
         wc_ds = new("wc_ds", [N], U8)
         nc.vector.tensor_copy(
@@ -230,17 +229,14 @@ def tile_list_headbox_setpoint_step_kernel(
             wc_s[:].rearrange("p (g n t) -> p g t n", g=2, t=PACK),
         )
         we1 = [quantize_we(1, a, rounded1[a], (0, 512)) for a in range(2)]
-        hold_tanh(0, 2, 2, "we10")
         hold_tanh(1, 0, PACK, "we11")
-        squares = []
-        for b, i in ((0, 2), (0, 3), (1, 0), (1, 1)):
-            tanh_of(b, i)
-            squares.append(square_of(b, i))
-        late_errors.extend(error(i, we1, banks[4 + i]) for i in range(2))
-        slope = new("slope", [4, S], F32, tag="we_bf11")
-        for u in range(4):
+        tanh_of(1, 0)
+        squares.append(square_of(1, 0))
+        late_errors.append(error(0, we1, b0))
+        slope = new("slope", [3, S], F32, tag="we_bf11")
+        for u in range(3):
             nc.vector.scalar_tensor_tensor(slope[:, u, :], squares[u][:], -1.0, late_errors[u][:], ADD, MULT)
-        for u in range(4):
+        for u in range(3):
             nc.gpsimd.tensor_tensor(squares[u][:], slope[:, u, :], step[:], MULT)
 
         def put(page, values):
@@ -289,11 +285,14 @@ def tile_list_headbox_setpoint_step_kernel(
         round_turned(nc.scalar.copy, targets, sums, range(4))
         put(pages[2], squares[0])
         put(pages[3], squares[1])
-        for i in (2, 3):
+        for i in range(1, PACK):
             tanh_of(1, i)
-        for i in (2, 3):
+        for i in range(1, PACK):
             error(i, we1, banks[4 + i])
-        ready = {2: correction(factor_of(2, new("factor2", [2, S], F32)), b2, new("e12", [S], F32))}
+        ready = {
+            i: correction(factor_of(i, new(f"factor{i}", [2, S], F32)), banks[4 + i], new(f"e1{i}", [S], F32))
+            for i in (1, 2)
+        }
         last_factor = factor_of(3, late.tile([P, 2, S], F32, name="factor3", offset=2 * BANK, align_bytes=64))
         wc_dw = {}
 
@@ -306,7 +305,7 @@ def tile_list_headbox_setpoint_step_kernel(
 
         deal_wc(0, "we11")
         put(pages[0], squares[2])
-        put(pages[1], squares[3])
+        put(pages[1], ready[1])
         add_turned(0, 1, pages[2:4], sums, range(4))
         round_turned(nc.scalar.copy, [zt0[mq // 2][:, mq % 2, :, 1, :] for mq in range(4)], sums, range(4))
         put(pages[2], ready[2])
@@ -361,15 +360,15 @@ def tile_list_headbox_setpoint_step_kernel(
             nc.gpsimd.tensor_tensor(last_rows[c][:, 0, :], sp_t[1, 1][:, 0, cols], pages[2][:, cols], ADD)
         put(pages[3], ready[3])
 
-        y_s = [new(f"y_s{mh}", [2, BANK], U8) for mh in range(2)]
+        y_s = new("y_s", [2, T2], U8)
         units = (
             (0, 0, 256, (a0, a1), "we010"),
             (1, 0, 256, (a2, a3), "we011"),
             (0, 256, 256, (b3, b1), "sp00"),
-            (1, 256, 256, (b2, b0), "sp01"),
-            (0, 512, 512, (a0, a1, a2, a3), "we00"),
+            (1, 256, 256, (a0, a1), "sp01"),
+            (0, 512, 512, (b2, b0, a2, a3), "we00"),
             (1, 512, 256, (b3, b1), "tab_w0"),
-            (1, 768, 256, (b2, b0), "we10"),
+            (1, 768, 256, (a0, a1), "we10"),
         )
 
         def last_passes(u, k, a):
@@ -390,7 +389,7 @@ def tile_list_headbox_setpoint_step_kernel(
                     stop=(a == 1 and s == share - 1),
                 )
 
-        for u in range(4):
+        for u in range(3):
             for k in range(2):
                 last_passes(u, k, 0)
 
@@ -411,7 +410,7 @@ def tile_list_headbox_setpoint_step_kernel(
             rows = out_0[KP * g : KP * (g + 1), cols].rearrange("(p t) m -> p t m", t=PACK)
             share = BANK // width
             for k, bank in enumerate(group):
-                for a in range(1 if u < 4 else 0, 2):
+                for a in range(1 if u < 3 else 0, 2):
                     last_passes(u, k, a)
                 done = share * (k + 1)
                 nc.scalar.copy(y[:, done - share : done, :], bank[:].rearrange("p (s m) -> p s m", s=share))
@@ -423,14 +422,15 @@ def tile_list_headbox_setpoint_step_kernel(
                 y_bf[:].rearrange("p (c i t) -> p c t i", i=4, t=PACK),
                 y[:].rearrange("p t (c i) -> p c t i", i=4),
             )
-            y_c = new(f"y_c{u}", [width], U32)
-            plane = y_s[m0 // BANK]
-            nc.vector.quantize_mx(y_c[:].bitcast(FP8X4), plane[:, g, m0 % BANK : m0 % BANK + width], y_bf[:])
-            nc.sync.dma_start(out_1[g, :, cols, :].rearrange("p m t -> p (m t)").bitcast(I32), y_c[:].bitcast(I32))
-            if g == 1 and (m0 + width) % BANK == 0:
-                half = slice(m0 + width - BANK, m0 + width)
-                for r in range(4):
-                    nc.sync.dma_start(
-                        out_2[:, r:16:4, half].rearrange("g q m -> q g m").bitcast(I32),
-                        plane[r:P:32, :, :].bitcast(I32),
-                    )
+            if u < 6:
+                first = m0
+                y_c = new(f"y_c{u}", [BANK if u == 5 else width], U32)
+            nc.vector.quantize_mx(y_c[:, m0 - first : m0 - first + width].bitcast(FP8X4), y_s[:, g, cols], y_bf[:])
+            if u != 5:
+                nc.sync.dma_start(
+                    out_1[g, :, first : m0 + width, :].rearrange("p m t -> p (m t)").bitcast(I32), y_c[:].bitcast(I32)
+                )
+        for r in range(4):
+            nc.sync.dma_start(
+                out_2[:, r:16:4, :].rearrange("g q m -> q g m").bitcast(I32), y_s[r:P:32, :, :].bitcast(I32)
+            )

@@ -230,14 +230,11 @@ def tile_list_headbox_setpoint_step_kernel(
         )
         we1 = [quantize_we(1, a, rounded1[a], (0, 512)) for a in range(2)]
         hold_tanh(1, 0, PACK, "we11")
-        tanh_of(1, 0)
-        squares.append(square_of(1, 0))
-        late_errors.append(error(0, we1, b0))
-        slope = new("slope", [3, S], F32, tag="we_bf11")
-        for u in range(3):
+        slope = new("slope", [2, S], F32, tag="we_bf11")
+        for u in range(2):
             nc.vector.scalar_tensor_tensor(slope[:, u, :], squares[u][:], -1.0, late_errors[u][:], ADD, MULT)
-        for u in range(3):
-            nc.gpsimd.tensor_tensor(squares[u][:], slope[:, u, :], step[:], MULT)
+        for u, engine in enumerate((nc.vector, nc.gpsimd)):
+            engine.tensor_tensor(squares[u][:], slope[:, u, :], step[:], MULT)
 
         def put(page, values):
             nc.vector.tensor_copy(page[:].indirect(place[:]), values[:])
@@ -285,15 +282,15 @@ def tile_list_headbox_setpoint_step_kernel(
         round_turned(nc.scalar.copy, targets, sums, range(4))
         put(pages[2], squares[0])
         put(pages[3], squares[1])
-        for i in range(1, PACK):
+        for i in range(PACK):
             tanh_of(1, i)
-        for i in range(1, PACK):
+        for i in range(PACK):
             error(i, we1, banks[4 + i])
         ready = {
             i: correction(factor_of(i, new(f"factor{i}", [2, S], F32)), banks[4 + i], new(f"e1{i}", [S], F32))
-            for i in (1, 2)
+            for i in range(3)
         }
-        last_factor = factor_of(3, late.tile([P, 2, S], F32, name="factor3", offset=2 * BANK, align_bytes=64))
+        last_factor = factor_of(3, late.tile([P, 2, S], F32, name="factor3", offset=0, align_bytes=64))
         wc_dw = {}
 
         def deal_wc(a, tag):
@@ -304,7 +301,7 @@ def tile_list_headbox_setpoint_step_kernel(
             )
 
         deal_wc(0, "we11")
-        put(pages[0], squares[2])
+        put(pages[0], ready[0])
         put(pages[1], ready[1])
         add_turned(0, 1, pages[2:4], sums, range(4))
         round_turned(nc.scalar.copy, [zt0[mq // 2][:, mq % 2, :, 1, :] for mq in range(4)], sums, range(4))
@@ -337,8 +334,11 @@ def tile_list_headbox_setpoint_step_kernel(
 
         add_turned(1, 0, pages[0:2], sums, range(4))
         zt1 = [new(f"zt1{mq}", [2, 2 * P], BF16)[:] for mq in range(4)]
-        shared = late.tile([P, 2 * BANK], F32, name="shared", offset=8 * BANK, align_bytes=64)
-        z_bf1 = [shared[:, BANK:].bitcast(BF16), new("z_bf11", [256 * PACK], BF16)[:], new("z_bf12", [BANK * PACK], BF16)[:]]
+        z_bf1 = [
+            late.tile([P, 256 * PACK], BF16, name="z_bf10", offset=4096, align_bytes=64)[:],
+            new("z_bf11", [256 * PACK], BF16)[:],
+            new("z_bf12", [BANK * PACK], BF16)[:],
+        ]
         for quarters in ((0, 1), (2, 3)):
             round_turned(nc.scalar.copy, zt1, sums, quarters)
             for mq in quarters:
@@ -350,14 +350,9 @@ def tile_list_headbox_setpoint_step_kernel(
                 nc.scalar.copy(target[:, max(mq - 2, 0), :, 0], bank[:, : 2 * P])
 
         chunks = ((0, 256), (256, 256), (512, 512))
-        last_rows = [
-            late.tile([P, 2, width], F32, name=f"last_rows{c}", offset=8 * c0, align_bytes=64)[:]
-            for c, (c0, width) in enumerate(chunks[:2])
-        ]
-        last_rows.append(shared[:].rearrange("p (e m) -> p e m", e=2))
-        for c, (c0, width) in enumerate(chunks):
-            cols = slice(c0, c0 + width)
-            nc.gpsimd.tensor_tensor(last_rows[c][:, 0, :], sp_t[1, 1][:, 0, cols], pages[2][:, cols], ADD)
+        halves = [late.tile([P, 2, BANK], F32, name=f"last_rows{u}", offset=4096 * u, align_bytes=64) for u in range(2)]
+        last_rows = [halves[0][:, :, :256], halves[0][:, :, 256:], halves[1][:]]
+        nc.gpsimd.tensor_tensor(halves[0][:, 0, :], sp_t[1, 1][:, 0, :BANK], pages[2][:, :BANK], ADD)
         put(pages[3], ready[3])
 
         y_s = new("y_s", [2, T2], U8)
@@ -395,7 +390,8 @@ def tile_list_headbox_setpoint_step_kernel(
 
         for c, (c0, width) in enumerate(chunks):
             cols = slice(c0, c0 + width)
-            nc.vector.tensor_tensor(last_rows[c][:, 1, :], sp_t[1, 1][:, 1, cols], pages[3][:, cols], ADD)
+            for e in range(1 if c < 2 else 0, 2):
+                nc.vector.tensor_tensor(last_rows[c][:, e, :], sp_t[1, 1][:, e, cols], pages[2 + e][:, cols], ADD)
             if c == 2:
                 z_q[0, 2] = tuple(part[:] for part in quantize_z("02", z_bf0[1][:], BANK, tag="z_bf11"))
             nc.vector.tensor_copy(

@@ -291,23 +291,23 @@ def tile_list_headbox_setpoint_step_kernel(
             for i in range(3)
         }
         last_factor = factor_of(3, late.tile([P, 2, S], F32, name="factor3", offset=0, align_bytes=64))
-        wc_dw = {}
-
-        def deal_wc(a, tag):
-            wc_dw[a] = new(f"wc_dw{a}", [N], U32, tag=tag)
-            nc.scalar.copy(
-                wc_dw[a][:].rearrange("p (g t n) -> p g n t", g=2, t=PACK),
-                wc_w[:, a, :].bitcast(U32).rearrange("p (g n t) -> p g n t", g=2, t=PACK),
-            )
-
-        deal_wc(0, "we11")
+        ready[3] = correction(last_factor, b3, late.tile([P, S], F32, name="e13", offset=9216, align_bytes=64))
+        wc_dw = [new("wc_dw0", [N], U32, tag="we11"), new("wc_dw1", [N], I32, tag="factor2")]
+        nc.scalar.copy(
+            wc_dw[0][:].rearrange("p (g t n) -> p g n t", g=2, t=PACK),
+            wc_w[:, 0, :].bitcast(U32).rearrange("p (g n t) -> p g n t", g=2, t=PACK),
+        )
+        nc.gpsimd.tensor_copy(
+            wc_dw[1][:].rearrange("p (g t n) -> p g t n", g=2, t=PACK),
+            wc_w[:, 1, :].rearrange("p (g n t) -> p g t n", g=2, t=PACK),
+        )
         put(pages[0], ready[0])
         put(pages[1], ready[1])
         add_turned(0, 1, pages[2:4], sums, range(4))
         round_turned(nc.scalar.copy, [zt0[mq // 2][:, mq % 2, :, 1, :] for mq in range(4)], sums, range(4))
         put(pages[2], ready[2])
         z_bf0 = [new(f"z_bf0{mh}", [BANK * PACK], BF16) for mh in range(2)]
-        for mq, bank in enumerate((b0, b1, b2, b0)):
+        for mq, bank in enumerate((b0, b1, b2, b3)):
             view = bank[:].rearrange("p (mb h m) -> p mb h m", mb=2, h=2)
             words = zt0[mq // 2][:, mq % 2].bitcast(F32)
             for mb in range(2):
@@ -315,55 +315,70 @@ def tile_list_headbox_setpoint_step_kernel(
                     nc.tensor.transpose(view[:, mb, h, :], words[:, mb, h, :], ident[:])
             target = z_bf0[mq // 2][:].bitcast(F32).rearrange("p (q mb m h) -> p q mb m h", q=2, mb=2, h=2)
             nc.scalar.copy(target[:, mq % 2], view.rearrange("p mb h m -> p mb m h"))
-            if mq == 1:
-                ready[3] = correction(last_factor, b3, new("e13", [S], F32, tag="zt00"))
-
-        deal_wc(1, "zt01")
-
-        z_q = {}
-
-        def quantize_z(name, source, width, tag=None):
-            codes = new(f"z_c{name}", [width], U32, tag=tag)
-            scales = new(f"z_s{name}", [width], U8)
-            nc.vector.quantize_mx(codes[:].bitcast(FP8X4), scales[:], source)
-            return codes, scales
-
-        first_half = quantize_z("00", z_bf0[0][:], BANK)
-        for c in range(2):
-            z_q[0, c] = tuple(part[:, 256 * c : 256 * (c + 1)] for part in first_half)
 
         add_turned(1, 0, pages[0:2], sums, range(4))
+        chunks = ((0, 256), (256, 256), (512, 512))
         zt1 = [new(f"zt1{mq}", [2, 2 * P], BF16)[:] for mq in range(4)]
         z_bf1 = [
             late.tile([P, 256 * PACK], BF16, name="z_bf10", offset=4096, align_bytes=64)[:],
             new("z_bf11", [256 * PACK], BF16)[:],
             new("z_bf12", [BANK * PACK], BF16)[:],
         ]
-        for quarters in ((0, 1), (2, 3)):
+        pairs = {c: new(f"pairs{c}", [2, chunks[c][1]], F32) for c in (1, 2)}
+        first_words = z_bf1[0].bitcast(F32).rearrange("p (m h) -> p h m", h=2)
+        for bank, quarters, target in (
+            (b0, (0,), first_words[:, 0, :]),
+            (b1, (1,), pairs[1][:, 0, :]),
+            (b2, (2, 3), pairs[2][:, 0, :]),
+        ):
             round_turned(nc.scalar.copy, zt1, sums, quarters)
-            for mq in quarters:
-                bank = (b3, b1, b2, b0)[mq]
+            for u, mq in enumerate(quarters):
                 words = zt1[mq].bitcast(F32)
                 for mb in range(2):
-                    nc.tensor.transpose(bank[:, mb * P : (mb + 1) * P], words[:, mb, :], ident[:])
-                target = z_bf1[min(mq, 2)].bitcast(F32).rearrange("p (q m h) -> p q m h", m=2 * P, h=2)
-                nc.scalar.copy(target[:, max(mq - 2, 0), :, 0], bank[:, : 2 * P])
+                    nc.tensor.transpose(bank[:, (2 * u + mb) * P : (2 * u + mb + 1) * P], words[:, mb, :], ident[:])
+            nc.scalar.copy(target, bank[:, : 2 * P * len(quarters)])
 
-        chunks = ((0, 256), (256, 256), (512, 512))
-        halves = [late.tile([P, 2, BANK], F32, name=f"last_rows{u}", offset=4096 * u, align_bytes=64) for u in range(2)]
+        halves = [late.tile([P, 2, BANK], F32, name=f"last_rows{u}", offset=5120 * u, align_bytes=64) for u in range(2)]
         last_rows = [halves[0][:, :, :256], halves[0][:, :, 256:], halves[1][:]]
         nc.gpsimd.tensor_tensor(halves[0][:, 0, :], sp_t[1, 1][:, 0, :BANK], pages[2][:, :BANK], ADD)
         put(pages[3], ready[3])
 
-        y_s = new("y_s", [2, T2], U8)
+        z_q = {}
+
+        def quantize_z(b, c, source, codes):
+            scales = new(f"z_s{b}{c}", [chunks[c][1]], U8)
+            nc.vector.quantize_mx(codes[:].bitcast(FP8X4), scales[:], source)
+            z_q[b, c] = (codes, scales)
+
+        for c, (c0, width) in enumerate(chunks):
+            cols = slice(c0, c0 + width)
+            for e in range(1 if c < 2 else 0, 2):
+                nc.vector.tensor_tensor(last_rows[c][:, e, :], sp_t[1, 1][:, e, cols], pages[2 + e][:, cols], ADD)
+            if c < 2:
+                codes = late.tile([P, width], U32, name=f"z_c0{c}", offset=(9216, 4096)[c], align_bytes=64)
+            else:
+                codes = new("z_c02", [width], U32, tag="z_bf11")
+            quantize_z(0, c, z_bf0[c0 // BANK][:, PACK * (c0 % BANK) : PACK * (c0 % BANK + width)], codes)
+            if c == 0:
+                rounded = z_bf1[c].rearrange("p (m h e) -> p m h e", h=2, e=2)[:, :, 1, :]
+            else:
+                rounded = pairs[c][:, 1, :].bitcast(BF16).rearrange("p (m e) -> p m e", e=2)
+            nc.vector.tensor_copy(rounded, last_rows[c].rearrange("p e m -> p m e"))
+            if c > 0:
+                nc.vector.tensor_copy(
+                    z_bf1[c].bitcast(F32).rearrange("p (m h) -> p m h", h=2), pairs[c][:].rearrange("p h m -> p m h")
+                )
+            quantize_z(1, c, z_bf1[c], new(f"z_c1{c}", [width], U32))
+
+        y_s = [new(f"y_s{mh}", [2, BANK], U8) for mh in range(2)]
         units = (
             (0, 0, 256, (a0, a1), "we010"),
             (1, 0, 256, (a2, a3), "we011"),
-            (0, 256, 256, (b3, b1), "sp00"),
-            (1, 256, 256, (a0, a1), "sp01"),
-            (0, 512, 512, (b2, b0, a2, a3), "we00"),
-            (1, 512, 256, (b3, b1), "tab_w0"),
-            (1, 768, 256, (a0, a1), "we10"),
+            (0, 256, 256, (b3, b0), "sp00"),
+            (1, 256, 256, (b1, b2), "sp01"),
+            (0, 512, 512, (a0, a1, a2, a3), "we00"),
+            (1, 512, 256, (b3, b0), "tab_w0"),
+            (1, 768, 256, (b1, b2), "we10"),
         )
 
         def last_passes(u, k, a):
@@ -380,25 +395,9 @@ def tile_list_headbox_setpoint_step_kernel(
                     lhsT_scale=wc_ds[4 * a :, c0 : c0 + P],
                     rhs=codes[:, cols].bitcast(FP8X4),
                     rhs_scale=scales[:, cols],
-                    start=(a == 0 and s == 0),
-                    stop=(a == 1 and s == share - 1),
+                    start=(a == 1 and s == 0),
+                    stop=(a == 0 and s == share - 1),
                 )
-
-        for u in range(3):
-            for k in range(2):
-                last_passes(u, k, 0)
-
-        for c, (c0, width) in enumerate(chunks):
-            cols = slice(c0, c0 + width)
-            for e in range(1 if c < 2 else 0, 2):
-                nc.vector.tensor_tensor(last_rows[c][:, e, :], sp_t[1, 1][:, e, cols], pages[2 + e][:, cols], ADD)
-            if c == 2:
-                z_q[0, 2] = tuple(part[:] for part in quantize_z("02", z_bf0[1][:], BANK, tag="z_bf11"))
-            nc.vector.tensor_copy(
-                z_bf1[c].rearrange("p (m h e) -> p m h e", h=2, e=2)[:, :, 1, :],
-                last_rows[c].rearrange("p e m -> p m e"),
-            )
-            z_q[1, c] = tuple(part[:] for part in quantize_z(f"1{c}", z_bf1[c], width))
 
         for u, (g, m0, width, group, tag) in enumerate(units):
             cols = slice(m0, m0 + width)
@@ -406,7 +405,7 @@ def tile_list_headbox_setpoint_step_kernel(
             rows = out_0[KP * g : KP * (g + 1), cols].rearrange("(p t) m -> p t m", t=PACK)
             share = BANK // width
             for k, bank in enumerate(group):
-                for a in range(1 if u < 3 else 0, 2):
+                for a in (1, 0):
                     last_passes(u, k, a)
                 done = share * (k + 1)
                 nc.scalar.copy(y[:, done - share : done, :], bank[:].rearrange("p (s m) -> p s m", s=share))
@@ -418,15 +417,14 @@ def tile_list_headbox_setpoint_step_kernel(
                 y_bf[:].rearrange("p (c i t) -> p c t i", i=4, t=PACK),
                 y[:].rearrange("p t (c i) -> p c t i", i=4),
             )
-            if u < 6:
-                first = m0
-                y_c = new(f"y_c{u}", [BANK if u == 5 else width], U32)
-            nc.vector.quantize_mx(y_c[:, m0 - first : m0 - first + width].bitcast(FP8X4), y_s[:, g, cols], y_bf[:])
-            if u != 5:
-                nc.sync.dma_start(
-                    out_1[g, :, first : m0 + width, :].rearrange("p m t -> p (m t)").bitcast(I32), y_c[:].bitcast(I32)
-                )
-        for r in range(4):
-            nc.sync.dma_start(
-                out_2[:, r:16:4, :].rearrange("g q m -> q g m").bitcast(I32), y_s[r:P:32, :, :].bitcast(I32)
-            )
+            y_c = new(f"y_c{u}", [width], U32)
+            plane = y_s[m0 // BANK]
+            nc.vector.quantize_mx(y_c[:].bitcast(FP8X4), plane[:, g, m0 % BANK : m0 % BANK + width], y_bf[:])
+            nc.sync.dma_start(out_1[g, :, cols, :].rearrange("p m t -> p (m t)").bitcast(I32), y_c[:].bitcast(I32))
+            if g == 1 and (m0 + width) % BANK == 0:
+                half = slice(m0 + width - BANK, m0 + width)
+                for r in range(4):
+                    nc.sync.dma_start(
+                        out_2[:, r:16:4, half].rearrange("g q m -> q g m").bitcast(I32),
+                        plane[r:P:32, :, :].bitcast(I32),
+                    )

@@ -186,19 +186,14 @@ def tile_list_headbox_setpoint_step_kernel(
         rounded00 = round_we(0, 0, (nc.scalar.copy, nc.vector.tensor_copy))
         tanh = {}
 
-        def hold_tanh(b, first, count, tag):
-            held = new(f"th{b}{first}", [count, S], F32, tag=tag)
-            for u in range(count):
-                tanh[b, first + u] = held[:, u, :]
-
-        hold_tanh(0, 0, PACK, "we00")
+        tanh[0] = new("th0", [PACK, S], F32, tag="we00")
 
         def tanh_of(b, i):
-            nc.scalar.activation(tanh[b, i], forward(b, i, banks[4 + i])[:], TANH)
+            nc.scalar.activation(tanh[b][:, i, :], forward(b, i, banks[4 + i])[:], TANH)
 
         def square_of(b, i):
             sq = new(f"sq{b}{i}", [S], F32)
-            nc.scalar.activation(sq[:], tanh[b, i], SQUARE)
+            nc.scalar.activation(sq[:], tanh[b][:, i, :], SQUARE)
             return sq
 
         rounded01 = round_we(0, 1, (nc.vector.tensor_copy, nc.vector.tensor_copy))
@@ -218,10 +213,11 @@ def tile_list_headbox_setpoint_step_kernel(
         for u, tag in enumerate(("wf_w1", "we_c00")):
             pages.append(new(f"page{u + 2}", [T2], F32, tag=tag))
             nc.gpsimd.memset(pages[-1][:], 0.0)
-        squares = []
         for i in (2, 3):
             tanh_of(0, i)
-            squares.append(square_of(0, i))
+        both_squares = new("sq02", [2, S], F32)
+        nc.scalar.activation(both_squares[:], tanh[0][:, 2:, :], SQUARE)
+        squares = [both_squares[:, u, :] for u in range(2)]
         rounded1 = [round_we(1, a, (nc.scalar.copy,)) for a in range(2)]
         wc_ds = new("wc_ds", [N], U8)
         nc.vector.tensor_copy(
@@ -229,26 +225,20 @@ def tile_list_headbox_setpoint_step_kernel(
             wc_s[:].rearrange("p (g n t) -> p g t n", g=2, t=PACK),
         )
         we1 = [quantize_we(1, a, rounded1[a], (0, 512)) for a in range(2)]
-        hold_tanh(1, 0, PACK, "we11")
+        tanh[1] = new("th1", [PACK, S], F32, tag="we11")
         slope = new("slope", [2, S], F32, tag="we_bf11")
         for u in range(2):
-            nc.vector.scalar_tensor_tensor(slope[:, u, :], squares[u][:], -1.0, late_errors[u][:], ADD, MULT)
+            nc.vector.scalar_tensor_tensor(slope[:, u, :], squares[u], -1.0, late_errors[u][:], ADD, MULT)
         for u, engine in enumerate((nc.vector, nc.gpsimd)):
-            engine.tensor_tensor(squares[u][:], slope[:, u, :], step[:], MULT)
+            engine.tensor_tensor(squares[u], slope[:, u, :], step[:], MULT)
 
         def put(page, values):
-            nc.vector.tensor_copy(page[:].indirect(place[:]), values[:])
+            nc.vector.tensor_copy(page[:].indirect(place[:]), values)
 
-        def factor_of(i, both):
-            nc.scalar.activation(both[:, 0, :], tanh[1, i], SQUARE)
-            nc.scalar.activation(both[:, 0, :], both[:, 0, :], IDENTITY, bias=-1.0)
-            nc.gpsimd.tensor_tensor(both[:, 1, :], both[:, 0, :], step[:], MULT)
-            return both[:, 1, :]
-
-        def correction(factor, bank, e):
-            nc.scalar.copy(e[:], bank[:])
-            nc.gpsimd.tensor_tensor(e[:], e[:], factor, MULT)
-            return e
+        def slopes_of(first, pair):
+            nc.scalar.activation(pair[:], tanh[1][:, first : first + 2, :], SQUARE)
+            nc.scalar.activation(pair[:], pair[:], IDENTITY, bias=-1.0)
+            return [pair[:, u, :] for u in range(2)]
 
         def add_turned(b, h, pair_pages, sums, order):
             sources = [sp_t[b, h][:, e, :] for e in range(2)] + [page[:] for page in pair_pages]
@@ -286,21 +276,30 @@ def tile_list_headbox_setpoint_step_kernel(
             tanh_of(1, i)
         for i in range(PACK):
             error(i, we1, banks[4 + i])
-        ready = {
-            i: correction(factor_of(i, new(f"factor{i}", [2, S], F32)), banks[4 + i], new(f"e1{i}", [S], F32))
-            for i in range(3)
-        }
-        last_factor = factor_of(3, late.tile([P, 2, S], F32, name="factor3", offset=0, align_bytes=64))
-        ready[3] = correction(last_factor, b3, late.tile([P, S], F32, name="e13", offset=9216, align_bytes=64))
-        wc_dw = [new("wc_dw0", [N], U32, tag="we11"), new("wc_dw1", [N], I32, tag="factor2")]
-        nc.scalar.copy(
-            wc_dw[0][:].rearrange("p (g t n) -> p g n t", g=2, t=PACK),
-            wc_w[:, 0, :].bitcast(U32).rearrange("p (g n t) -> p g n t", g=2, t=PACK),
-        )
-        nc.gpsimd.tensor_copy(
-            wc_dw[1][:].rearrange("p (g t n) -> p g t n", g=2, t=PACK),
-            wc_w[:, 1, :].rearrange("p (g n t) -> p g t n", g=2, t=PACK),
-        )
+        ready = []
+        for first in (0, 2):
+            if first == 0:
+                pair = new("slopes0", [2, S], F32)
+            else:
+                pair = late.tile([P, 2, S], F32, name="slopes2", offset=2048, align_bytes=64)
+            for i, factor in enumerate(slopes_of(first, pair), first):
+                nc.gpsimd.tensor_tensor(factor, factor, step[:], MULT)
+                e = new(f"e1{i}", [S], F32)
+                nc.scalar.copy(e[:], banks[4 + i][:])
+                if i < 3:
+                    nc.gpsimd.tensor_tensor(e[:], e[:], factor, MULT)
+                    ready.append(e[:])
+        last_error, last_factor = e, factor
+        wc_dw = []
+
+        def deal_wc(a, tag):
+            wc_dw.append(new(f"wc_dw{a}", [N], U32, tag=tag))
+            nc.scalar.copy(
+                wc_dw[a][:].rearrange("p (g t n) -> p g n t", g=2, t=PACK),
+                wc_w[:, a, :].bitcast(U32).rearrange("p (g n t) -> p g n t", g=2, t=PACK),
+            )
+
+        deal_wc(0, "we11")
         put(pages[0], ready[0])
         put(pages[1], ready[1])
         add_turned(0, 1, pages[2:4], sums, range(4))
@@ -315,12 +314,26 @@ def tile_list_headbox_setpoint_step_kernel(
                     nc.tensor.transpose(view[:, mb, h, :], words[:, mb, h, :], ident[:])
             target = z_bf0[mq // 2][:].bitcast(F32).rearrange("p (q mb m h) -> p q mb m h", q=2, mb=2, h=2)
             nc.scalar.copy(target[:, mq % 2], view.rearrange("p mb h m -> p mb m h"))
+        deal_wc(1, "zt00")
+        ready.append(new("last_product", [S], F32, tag="zt01")[:])
+        nc.gpsimd.tensor_tensor(ready[3], last_error[:], last_factor, MULT)
+        z_q = {}
+
+        def quantize_z(name, source, codes):
+            scales = new(f"z_s{name}", [codes.shape[1]], U8)
+            nc.vector.quantize_mx(codes[:].bitcast(FP8X4), scales[:], source)
+            return codes, scales
+
+        first_half = quantize_z("00", z_bf0[0][:], new("z_c00", [BANK], U32))
+        for c in range(2):
+            z_q[0, c] = tuple(part[:, 256 * c : 256 * (c + 1)] for part in first_half)
 
         add_turned(1, 0, pages[0:2], sums, range(4))
         chunks = ((0, 256), (256, 256), (512, 512))
         zt1 = [new(f"zt1{mq}", [2, 2 * P], BF16)[:] for mq in range(4)]
+        shared = late.tile([P, 2 * BANK], F32, name="shared", offset=4096, align_bytes=64)
         z_bf1 = [
-            late.tile([P, 256 * PACK], BF16, name="z_bf10", offset=4096, align_bytes=64)[:],
+            shared[:, BANK:].bitcast(BF16),
             new("z_bf11", [256 * PACK], BF16)[:],
             new("z_bf12", [BANK * PACK], BF16)[:],
         ]
@@ -338,27 +351,21 @@ def tile_list_headbox_setpoint_step_kernel(
                     nc.tensor.transpose(bank[:, (2 * u + mb) * P : (2 * u + mb + 1) * P], words[:, mb, :], ident[:])
             nc.scalar.copy(target, bank[:, : 2 * P * len(quarters)])
 
-        halves = [late.tile([P, 2, BANK], F32, name=f"last_rows{u}", offset=5120 * u, align_bytes=64) for u in range(2)]
-        last_rows = [halves[0][:, :, :256], halves[0][:, :, 256:], halves[1][:]]
-        nc.gpsimd.tensor_tensor(halves[0][:, 0, :], sp_t[1, 1][:, 0, :BANK], pages[2][:, :BANK], ADD)
+        halves = [
+            late.tile([P, 2, BANK], F32, name="last_rows", offset=0, align_bytes=64)[:],
+            shared[:].rearrange("p (e m) -> p e m", e=2),
+        ]
+        last_rows = [halves[0][:, :, :256], halves[0][:, :, 256:], halves[1]]
+        for u, rows in enumerate(halves):
+            cols = slice(BANK * u, BANK * (u + 1))
+            nc.gpsimd.tensor_tensor(rows[:, 0, :], sp_t[1, 1][:, 0, cols], pages[2][:, cols], ADD)
         put(pages[3], ready[3])
-
-        z_q = {}
-
-        def quantize_z(b, c, source, codes):
-            scales = new(f"z_s{b}{c}", [chunks[c][1]], U8)
-            nc.vector.quantize_mx(codes[:].bitcast(FP8X4), scales[:], source)
-            z_q[b, c] = (codes, scales)
 
         for c, (c0, width) in enumerate(chunks):
             cols = slice(c0, c0 + width)
-            for e in range(1 if c < 2 else 0, 2):
-                nc.vector.tensor_tensor(last_rows[c][:, e, :], sp_t[1, 1][:, e, cols], pages[2 + e][:, cols], ADD)
-            if c < 2:
-                codes = late.tile([P, width], U32, name=f"z_c0{c}", offset=(9216, 4096)[c], align_bytes=64)
-            else:
-                codes = new("z_c02", [width], U32, tag="z_bf11")
-            quantize_z(0, c, z_bf0[c0 // BANK][:, PACK * (c0 % BANK) : PACK * (c0 % BANK + width)], codes)
+            nc.vector.tensor_tensor(last_rows[c][:, 1, :], sp_t[1, 1][:, 1, cols], pages[3][:, cols], ADD)
+            if c == 2:
+                z_q[0, 2] = quantize_z("02", z_bf0[1][:], new("z_c02", [width], U32, tag="z_bf11"))
             if c == 0:
                 rounded = z_bf1[c].rearrange("p (m h e) -> p m h e", h=2, e=2)[:, :, 1, :]
             else:
@@ -368,7 +375,7 @@ def tile_list_headbox_setpoint_step_kernel(
                 nc.vector.tensor_copy(
                     z_bf1[c].bitcast(F32).rearrange("p (m h) -> p m h", h=2), pairs[c][:].rearrange("p h m -> p m h")
                 )
-            quantize_z(1, c, z_bf1[c], new(f"z_c1{c}", [width], U32))
+            z_q[1, c] = quantize_z(f"1{c}", z_bf1[c], new(f"z_c1{c}", [width], U32))
 
         y_s = [new(f"y_s{mh}", [2, BANK], U8) for mh in range(2)]
         units = (
@@ -395,9 +402,13 @@ def tile_list_headbox_setpoint_step_kernel(
                     lhsT_scale=wc_ds[4 * a :, c0 : c0 + P],
                     rhs=codes[:, cols].bitcast(FP8X4),
                     rhs_scale=scales[:, cols],
-                    start=(a == 1 and s == 0),
-                    stop=(a == 0 and s == share - 1),
+                    start=(a == (0 if u < 3 else 1) and s == 0),
+                    stop=(a == (1 if u < 3 else 0) and s == share - 1),
                 )
+
+        for u in range(3):
+            for k in range(2):
+                last_passes(u, k, 0)
 
         for u, (g, m0, width, group, tag) in enumerate(units):
             cols = slice(m0, m0 + width)
@@ -405,7 +416,7 @@ def tile_list_headbox_setpoint_step_kernel(
             rows = out_0[KP * g : KP * (g + 1), cols].rearrange("(p t) m -> p t m", t=PACK)
             share = BANK // width
             for k, bank in enumerate(group):
-                for a in (1, 0):
+                for a in (1,) if u < 3 else (1, 0):
                     last_passes(u, k, a)
                 done = share * (k + 1)
                 nc.scalar.copy(y[:, done - share : done, :], bank[:].rearrange("p (s m) -> p s m", s=share))

@@ -49,6 +49,9 @@ def tile_list_headbox_setpoint_step_kernel(
         pages = [new(f"page{u}", [T2], F32) for u in range(2)]
         for page in pages:
             nc.vector.memset(page[:], 0.0)
+        ident = new("ident", [P], F32)
+        nc.vector.memset(ident[:], 0.0)
+        make_identity(nc, ident[:], nomemset=True)
 
         pick = lists.tile([P, S // 16], U16, name="pick")
         place = lists.tile([P, S // 16], U16, name="place")
@@ -85,12 +88,10 @@ def tile_list_headbox_setpoint_step_kernel(
 
         nc.sync.dma_start(pick[:], offs)
         load_rows(nc.sync, tab_s, tab_scales)
+        load_rows(nc.sync, wf_s, wf_scales)
         load_words(tab_w[0][:], tab_words[0])
         load_wf(0)
-        load_rows(nc.sync, wf_s, wf_scales)
         load_words(tab_w[1][:], tab_words[1])
-        ident = new("ident", [P], F32)
-        make_identity(nc, ident[:])
         we_raw = {(0, 0): [load_we("we00", 0, 0, KP)]}
         we_raw[0, 1] = [load_we(f"we01{u}", 1, u * KP // 2, KP // 2) for u in range(2)]
         load_wf(1)
@@ -210,7 +211,7 @@ def tile_list_headbox_setpoint_step_kernel(
             nc.vector.tensor_tensor(pages[i][:].indirect(place[:]), sq0[i][:], step[:], MULT)
         a0, a1, a2, a3, b0, b1, b2, b3 = banks
         late_errors = [error(i, we0, banks[i]) for i in (2, 3)]
-        for u, tag in enumerate(("wf_w1", "we_c00")):
+        for u, tag in enumerate(("wf_w1", "we_c01")):
             pages.append(new(f"page{u + 2}", [T2], F32, tag=tag))
             nc.gpsimd.memset(pages[-1][:], 0.0)
         for i in (2, 3):

@@ -237,8 +237,13 @@ def tile_list_headbox_setpoint_step_kernel(
             nc.vector.tensor_copy(page[:].indirect(place[:]), values)
 
         def slopes_of(first, pair):
-            nc.scalar.activation(pair[:], tanh[1][:, first : first + 2, :], SQUARE)
-            nc.scalar.activation(pair[:], pair[:], IDENTITY, bias=-1.0)
+            if first == 0:
+                squared = new("sq10", [2, S], F32)
+                nc.scalar.activation(squared[:], tanh[1][:, :2, :], SQUARE)
+                nc.gpsimd.tensor_scalar(pair[:], squared[:], 1.0, -1.0, MULT, ADD)
+            else:
+                nc.scalar.activation(pair[:], tanh[1][:, 2:, :], SQUARE)
+                nc.scalar.activation(pair[:], pair[:], IDENTITY, bias=-1.0)
             return [pair[:, u, :] for u in range(2)]
 
         def add_turned(b, h, pair_pages, sums, order):
@@ -280,7 +285,7 @@ def tile_list_headbox_setpoint_step_kernel(
         ready = []
         for first in (0, 2):
             if first == 0:
-                pair = new("slopes0", [2, S], F32)
+                pair = new("slopes0", [2, S], F32, tag="we_bf11")
             else:
                 pair = late.tile([P, 2, S], F32, name="slopes2", offset=2048, align_bytes=64)
             for i, factor in enumerate(slopes_of(first, pair), first):
@@ -291,16 +296,11 @@ def tile_list_headbox_setpoint_step_kernel(
                     nc.gpsimd.tensor_tensor(e[:], e[:], factor, MULT)
                     ready.append(e[:])
         last_error, last_factor = e, factor
-        wc_dw = []
-
-        def deal_wc(a, tag):
-            wc_dw.append(new(f"wc_dw{a}", [N], U32, tag=tag))
-            nc.scalar.copy(
-                wc_dw[a][:].rearrange("p (g t n) -> p g n t", g=2, t=PACK),
-                wc_w[:, a, :].bitcast(U32).rearrange("p (g n t) -> p g n t", g=2, t=PACK),
-            )
-
-        deal_wc(0, "we11")
+        wc_dw = new("wc_dw", [2, N], U32, tag="we11")
+        nc.scalar.copy(
+            wc_dw[:].rearrange("p a (g t n) -> p (a g) n t", g=2, t=PACK),
+            wc_w[:].bitcast(U32).rearrange("p a (g n t) -> p (a g) n t", g=2, t=PACK),
+        )
         put(pages[0], ready[0])
         put(pages[1], ready[1])
         add_turned(0, 1, pages[2:4], sums, range(4))
@@ -315,7 +315,6 @@ def tile_list_headbox_setpoint_step_kernel(
                     nc.tensor.transpose(view[:, mb, h, :], words[:, mb, h, :], ident[:])
             target = z_bf0[mq // 2][:].bitcast(F32).rearrange("p (q mb m h) -> p q mb m h", q=2, mb=2, h=2)
             nc.scalar.copy(target[:, mq % 2], view.rearrange("p mb h m -> p mb m h"))
-        deal_wc(1, "zt00")
         ready.append(new("last_product", [S], F32, tag="zt01")[:])
         nc.gpsimd.tensor_tensor(ready[3], last_error[:], last_factor, MULT)
         z_q = {}
@@ -399,7 +398,7 @@ def tile_list_headbox_setpoint_step_kernel(
                 c0 = KP * g + P * (share * k + s)
                 nc.tensor.matmul_mx(
                     group[k][:, s * width : (s + 1) * width],
-                    lhsT=wc_dw[a][:, c0 : c0 + P].bitcast(FP8X4),
+                    lhsT=wc_dw[:, a, c0 : c0 + P].bitcast(FP8X4),
                     lhsT_scale=wc_ds[4 * a :, c0 : c0 + P],
                     rhs=codes[:, cols].bitcast(FP8X4),
                     rhs_scale=scales[:, cols],

@@ -424,14 +424,24 @@ def tile_list_headbox_setpoint_step_kernel(
                 if done % run == 0:
                     nc.sync.dma_start(rows[:, done - run : done, :], y[:, done - run : done, :])
             y_bf = new(f"y_bf{u}", [width * PACK], BF16, tag=f"we_bf0{u % 2}")
-            nc.vector.tensor_copy(
+            copy = nc.scalar.copy if u == len(units) - 1 else nc.vector.tensor_copy
+            copy(
                 y_bf[:].rearrange("p (c i t) -> p c t i", i=4, t=PACK),
                 y[:].rearrange("p t (c i) -> p c t i", i=4),
             )
-            y_c = new(f"y_c{u}", [width], U32)
+            if u < 6:
+                first = m0
+                y_c = new(f"y_c{u}", [BANK if u == 5 else width], U32)
             plane = y_s[m0 // BANK]
-            nc.vector.quantize_mx(y_c[:].bitcast(FP8X4), plane[:, g, m0 % BANK : m0 % BANK + width], y_bf[:])
-            nc.sync.dma_start(out_1[g, :, cols, :].rearrange("p m t -> p (m t)").bitcast(I32), y_c[:].bitcast(I32))
+            nc.vector.quantize_mx(
+                y_c[:, m0 - first : m0 - first + width].bitcast(FP8X4),
+                plane[:, g, m0 % BANK : m0 % BANK + width],
+                y_bf[:],
+            )
+            if u != 5:
+                nc.sync.dma_start(
+                    out_1[g, :, first : m0 + width, :].rearrange("p m t -> p (m t)").bitcast(I32), y_c[:].bitcast(I32)
+                )
             if g == 1 and (m0 + width) % BANK == 0:
                 half = slice(m0 + width - BANK, m0 + width)
                 for r in range(4):

@@ -377,15 +377,14 @@ def tile_list_headbox_setpoint_step_kernel(
                 )
             z_q[1, c] = quantize_z(f"1{c}", z_bf1[c], new(f"z_c1{c}", [width], U32))
 
-        y_s = [new(f"y_s{mh}", [2, BANK], U8) for mh in range(2)]
+        y_s = new("y_s", [T2], U8)
         units = (
             (0, 0, 256, (a0, a1), "we010"),
             (1, 0, 256, (a2, a3), "we011"),
             (0, 256, 256, (b3, b0), "sp00"),
             (1, 256, 256, (b1, b2), "sp01"),
             (0, 512, 512, (a0, a1, a2, a3), "we00"),
-            (1, 512, 256, (b3, b0), "tab_w0"),
-            (1, 768, 256, (b1, b2), "we10"),
+            (1, 512, 512, (b3, b0, b1, b2), "tab_w0"),
         )
 
         def last_passes(u, k, a):
@@ -420,32 +419,19 @@ def tile_list_headbox_setpoint_step_kernel(
                     last_passes(u, k, a)
                 done = share * (k + 1)
                 nc.scalar.copy(y[:, done - share : done, :], bank[:].rearrange("p (s m) -> p s m", s=share))
-                run = 2 if u in (0, 4) else PACK
+                run = 2 if u in (0, 4, 5) else PACK
                 if done % run == 0:
                     nc.sync.dma_start(rows[:, done - run : done, :], y[:, done - run : done, :])
             y_bf = new(f"y_bf{u}", [width * PACK], BF16, tag=f"we_bf0{u % 2}")
-            copy = nc.scalar.copy if u == len(units) - 1 else nc.vector.tensor_copy
-            copy(
-                y_bf[:].rearrange("p (c i t) -> p c t i", i=4, t=PACK),
-                y[:].rearrange("p t (c i) -> p c t i", i=4),
-            )
-            if u < 6:
-                first = m0
-                y_c = new(f"y_c{u}", [BANK if u == 5 else width], U32)
-            plane = y_s[m0 // BANK]
-            nc.vector.quantize_mx(
-                y_c[:, m0 - first : m0 - first + width].bitcast(FP8X4),
-                plane[:, g, m0 % BANK : m0 % BANK + width],
-                y_bf[:],
-            )
-            if u != 5:
-                nc.sync.dma_start(
-                    out_1[g, :, first : m0 + width, :].rearrange("p m t -> p (m t)").bitcast(I32), y_c[:].bitcast(I32)
+            copies = (nc.vector.tensor_copy, nc.scalar.copy) if u == len(units) - 1 else (nc.vector.tensor_copy,)
+            cuts = (0, 384, 512) if u == len(units) - 1 else (0, width)
+            for copy, c0, c1 in zip(copies, cuts, cuts[1:]):
+                copy(
+                    y_bf[:, PACK * c0 : PACK * c1].rearrange("p (c i t) -> p c t i", i=4, t=PACK),
+                    y[:, :, c0:c1].rearrange("p t (c i) -> p c t i", i=4),
                 )
-            if g == 1 and (m0 + width) % BANK == 0:
-                half = slice(m0 + width - BANK, m0 + width)
-                for r in range(4):
-                    nc.sync.dma_start(
-                        out_2[:, r:16:4, half].rearrange("g q m -> q g m").bitcast(I32),
-                        plane[r:P:32, :, :].bitcast(I32),
-                    )
+            y_c = new(f"y_c{u}", [width], U32)
+            nc.vector.quantize_mx(y_c[:].bitcast(FP8X4), y_s[4 * g :, cols], y_bf[:])
+            nc.sync.dma_start(out_1[g, :, cols, :].rearrange("p m t -> p (m t)").bitcast(I32), y_c[:].bitcast(I32))
+        for q in range(4):
+            nc.sync.dma_start(out_2[:, 4 * q : 4 * q + 4, :].bitcast(I32), y_s[32 * q : 32 * q + 8, :].bitcast(I32))

from contextlib import ExitStack

import concourse.mybir as mybir
from concourse.masks import make_identity

K, T, S, T2, H, N = 1024, 2048, 512, 1024, 1024, 1024
FLOPS = 2 * K * H * S * 2 + 2 * H * N * T2

F32 = mybir.dt.float32
BF16 = mybir.dt.bfloat16
I32 = mybir.dt.int32
U32 = mybir.dt.uint32
U16 = mybir.dt.uint16
U8 = mybir.dt.uint8
FP8X4 = mybir.dt.float8_e4m3fn_x4
FP4X4 = mybir.dt.float4_e2m1fn_x4
ADD = mybir.AluOpType.add
MULT = mybir.AluOpType.mult
TANH = mybir.ActivationFunctionType.Tanh
SQUARE = mybir.ActivationFunctionType.Square
IDENTITY = mybir.ActivationFunctionType.Identity

P = 128
PACK = 4
KP = P * PACK
BANK = 512


def tile_list_headbox_setpoint_step_kernel(
    tc, tab_words, tab_scales, offs, we, wf_words, wf_scales, wgs, offs2, sp, wc_words, wc_scales, out_0, out_1, out_2
):
    nc = tc.nc
    with ExitStack() as ctx:
        lists = ctx.enter_context(tc.tile_pool(name="lists", bufs=1))
        sb = ctx.enter_context(tc.tile_pool(name="sb", bufs=1))
        late = ctx.enter_context(tc.tile_pool(name="late", bufs=1))
        psum = ctx.enter_context(tc.psum_pool(name="psum", bufs=1))

        def new(name, shape, dtype, tag=None):
            return sb.tile([P] + shape, dtype, name=name, tag=tag or name, align_bytes=64)

        banks = [psum.tile([P, BANK], F32, name=f"bank{u}") for u in range(8)]

        tab_s = new("tab_s", [2, T], U8)
        wf_s = new("wf_s", [2, H], U8)
        wc_s = new("wc_s", [N], U8)
        for plane in (tab_s, wf_s, wc_s):
            nc.vector.memset(plane[:].bitcast(I32), 0)
        pages = [new(f"page{u}", [T2], F32) for u in range(2)]
        for page in pages:
            nc.vector.memset(page[:], 0.0)
        ident = new("ident", [P], F32)
        nc.vector.memset(ident[:], 0.0)
        make_identity(nc, ident[:], nomemset=True)

        pick = lists.tile([P, S // 16], U16, name="pick")
        place = lists.tile([P, S // 16], U16, name="place")

        def load_words(tile_ap, words):
            nc.sync.dma_start(tile_ap, words.rearrange("p c i -> p (c i)").bitcast(I32))

        def load_rows(queue, rows, scales):
            for r in range(4):
                queue.dma_start(
                    rows[r:P:32, :, :].bitcast(I32),
                    scales[:, r:16:4, :].rearrange("a q c -> q a c").bitcast(I32),
                )

        def load_we(name, a, c0, width):
            raw = new(name, [PACK, width], F32)
            nc.sync.dma_start(raw[:], we[KP * a : KP * (a + 1), c0 : c0 + width].rearrange("(p j) c -> p j c", j=PACK))
            return raw

        def load_sp(b, h, tag):
            rows = new(f"sp{b}{h}", [2, T2], F32, tag=tag)
            source = sp[KP * b : KP * (b + 1), :].rearrange("(p i) m -> p i m", i=PACK)
            nc.sync.dma_start(rows[:], source[:, 2 * h : 2 * h + 2, :])
            return rows

        tab_w = [new(f"tab_w{a}", [T], I32) for a in range(2)]
        wf_w = [new(f"wf_w{b}", [2, 2 * KP], U8) for b in range(2)]

        def load_wf(b):
            nc.sync.dma_start(
                wf_w[b][:].bitcast(I32),
                wf_words[:, :, 2 * KP * b : 2 * KP * (b + 1)].rearrange("a p c -> p a c").bitcast(I32),
            )

        nc.sync.dma_start(pick[:], offs)
        load_rows(nc.sync, tab_s, tab_scales)
        load_rows(nc.sync, wf_s, wf_scales)
        load_words(tab_w[0][:], tab_words[0])
        load_wf(0)
        load_words(tab_w[1][:], tab_words[1])
        we_raw = {(0, 0): [load_we("we00", 0, 0, KP)]}
        we_raw[0, 1] = [load_we(f"we01{u}", 1, u * KP // 2, KP // 2) for u in range(2)]
        load_wf(1)
        step = new("step", [S], F32)
        nc.sync.dma_start(step[:], wgs)
        nc.sync.dma_start(place[:], offs2)
        for a in range(2):
            we_raw[1, a] = [load_we(f"we1{a}", a, KP, KP)]
        for q in range(4):
            nc.sync.dma_start(
                wc_s[32 * q : 32 * q + 8, :].bitcast(I32), wc_scales[:, 4 * q : 4 * q + 4, :].bitcast(I32)
            )
        sp_t = {(0, 0): load_sp(0, 0, None)}
        wc_w = new("wc_w", [2, N], I32)
        nc.sync.dma_start(wc_w[:], wc_words.rearrange("a p c i -> p a (c i)").bitcast(I32))
        sp_t[0, 1] = load_sp(0, 1, None)

        v_w = [new(f"v_w{a}", [S], U32) for a in range(2)]
        v_s = [new(f"v_s{a}", [S], U8) for a in range(2)]
        nc.vector.tensor_copy(v_w[0][:], tab_w[0][:].bitcast(U32).indirect(pick[:]))
        for a in range(2):
            nc.vector.tensor_copy(v_s[a][:], tab_s[:, a, :].indirect(pick[:]))
        nc.vector.tensor_copy(v_w[1][:], tab_w[1][:].bitcast(U32).indirect(pick[:]))
        for h in range(2):
            sp_t[1, h] = load_sp(1, h, f"tab_w{h}")

        wf_dw, wf_ds = [], []

        def deal_wf_words(b):
            words = new(f"wf_dw{b}", [2, PACK, P], U16)
            nc.vector.tensor_copy(words[:], wf_w[b][:].bitcast(U16).rearrange("p a (m i) -> p a i m", i=PACK))
            wf_dw.append(words)

        def deal_wf_scales(b):
            scales = new(f"wf_ds{b}", [2, PACK, P], U8)
            nc.vector.tensor_copy(
                scales[:], wf_s[:, :, KP * b : KP * (b + 1)].rearrange("p a (m i) -> p a i m", i=PACK)
            )
            wf_ds.append(scales)

        deal_wf_words(0)
        deal_wf_scales(0)

        def round_we(b, a, copies):
            rounded = new(f"we_bf{b}{a}", [PACK * KP], BF16)
            raws = we_raw[b, a]
            count = P // len(copies)
            target = rounded[:].rearrange("p (i m j) -> p i m j", i=PACK, j=PACK)
            for u, copy in enumerate(copies):
                raw = raws[u][:] if len(raws) > 1 else raws[0][:, :, PACK * count * u : PACK * count * (u + 1)]
                copy(
                    target[:, :, u * count : (u + 1) * count].rearrange("p i m j -> p m j i"),
                    raw.rearrange("p j (m i) -> p m j i", i=PACK),
                )
            return rounded

        def quantize_we(b, a, rounded, cuts):
            codes = new(f"we_c{b}{a}", [KP], U32)
            scales = new(f"we_s{b}{a}", [KP], U8)
            for c0, c1 in zip(cuts, cuts[1:]):
                nc.vector.quantize_mx(
                    codes[:, c0:c1].bitcast(FP8X4), scales[:, c0:c1], rounded[:, PACK * c0 : PACK * c1]
                )
            return codes, scales

        def forward(b, i, bank):
            for a in range(2):
                nc.tensor.matmul_mx(
                    bank[:],
                    lhsT=wf_dw[b][:, a, i, :].bitcast(FP4X4),
                    lhsT_scale=wf_ds[b][:, a, i, :],
                    rhs=v_w[a][:].bitcast(FP8X4),
                    rhs_scale=v_s[a][:],
                    start=(a == 0),
                    stop=(a == 1),
                )
            return bank

        def error(i, quantized, bank):
            cols = slice(i * P, (i + 1) * P)
            for a, (codes, scales) in enumerate(quantized):
                nc.tensor.matmul_mx(
                    bank[:],
                    lhsT=codes[:, cols].bitcast(FP8X4),
                    lhsT_scale=scales[:, cols],
                    rhs=v_w[a][:].bitcast(FP8X4),
                    rhs_scale=v_s[a][:],
                    start=(a == 0),
                    stop=(a == 1),
                )
            return bank

        rounded00 = round_we(0, 0, (nc.scalar.copy, nc.vector.tensor_copy))
        tanh = {}

        tanh[0] = new("th0", [PACK, S], F32, tag="we00")

        def tanh_of(b, i):
            nc.scalar.activation(tanh[b][:, i, :], forward(b, i, banks[4 + i])[:], TANH)

        def square_of(b, i):
            sq = new(f"sq{b}{i}", [S], F32)
            nc.scalar.activation(sq[:], tanh[b][:, i, :], SQUARE)
            return sq

        rounded01 = round_we(0, 1, (nc.vector.tensor_copy, nc.vector.tensor_copy))
        we0 = [quantize_we(0, 0, rounded00, (0, 512)), quantize_we(0, 1, rounded01, (0, 128, 256, 512))]
        sq0 = []
        for i in range(2):
            tanh_of(0, i)
            sq0.append(square_of(0, i))
        deal_wf_scales(1)
        deal_wf_words(1)
        for i in range(2):
            nc.vector.scalar_tensor_tensor(sq0[i][:], sq0[i][:], -1.0, error(i, we0, banks[i])[:], ADD, MULT)
        for i in range(2):
            nc.vector.tensor_tensor(pages[i][:].indirect(place[:]), sq0[i][:], step[:], MULT)
        a0, a1, a2, a3, b0, b1, b2, b3 = banks
        late_errors = [error(i, we0, banks[i]) for i in (2, 3)]
        for u, tag in enumerate(("wf_w1", "we_c01")):
            pages.append(new(f"page{u + 2}", [T2], F32, tag=tag))
            nc.gpsimd.memset(pages[-1][:], 0.0)
        for i in (2, 3):
            tanh_of(0, i)
        both_squares = new("sq02", [2, S], F32)
        nc.scalar.activation(both_squares[:], tanh[0][:, 2:, :], SQUARE)
        squares = [both_squares[:, u, :] for u in range(2)]
        rounded1 = [round_we(1, a, (nc.scalar.copy,)) for a in range(2)]
        wc_ds = new("wc_ds", [N], U8)
        nc.vector.tensor_copy(
            wc_ds[:].rearrange("p (g t n) -> p g t n", g=2, t=PACK),
            wc_s[:].rearrange("p (g n t) -> p g t n", g=2, t=PACK),
        )
        we1 = [quantize_we(1, a, rounded1[a], (0, 512)) for a in range(2)]
        tanh[1] = new("th1", [PACK, S], F32, tag="we11")
        slope = new("slope", [2, S], F32, tag="we_bf11")
        for u in range(2):
            nc.vector.scalar_tensor_tensor(slope[:, u, :], squares[u], -1.0, late_errors[u][:], ADD, MULT)
        for u, engine in enumerate((nc.vector, nc.gpsimd)):
            engine.tensor_tensor(squares[u], slope[:, u, :], step[:], MULT)

        def put(page, values):
            nc.vector.tensor_copy(page[:].indirect(place[:]), values)

        def slopes_of(first, pair):
            if first == 0:
                squared = new("sq10", [2, S], F32)
                nc.scalar.activation(squared[:], tanh[1][:, :2, :], SQUARE)
                nc.gpsimd.tensor_scalar(pair[:], squared[:], 1.0, -1.0, MULT, ADD)
            else:
                nc.scalar.activation(pair[:], tanh[1][:, 2:, :], SQUARE)
                nc.scalar.activation(pair[:], pair[:], IDENTITY, bias=-1.0)
            return [pair[:, u, :] for u in range(2)]

        def add_turned(b, h, pair_pages, sums, order):
            sources = [sp_t[b, h][:, e, :] for e in range(2)] + [page[:] for page in pair_pages]
            for terms in ((0, 1, 2), (3,)):
                for mq in order:
                    view = sums[mq][:].rearrange("m (mb e p) -> m mb e p", mb=2, e=2)
                    for u in terms:
                        for mb in range(2):
                            c0 = (2 * mq + mb) * P
                            nc.tensor.matmul(
                                view[:, mb, u % 2, :],
                                sources[u][:, c0 : c0 + P],
                                ident[:],
                                start=(u == 0 and mb == 0),
                                stop=(u == 3 and mb == 1),
                                is_transpose=True,
                            )

        def round_turned(copy, targets, sums, quarters):
            for mq in quarters:
                copy(
                    targets[mq].rearrange("m mb (p e) -> m mb p e", e=2),
                    sums[mq][:].rearrange("m (mb e p) -> m mb p e", mb=2, e=2),
                )

        zt0 = [new(f"zt0{mh}", [2, 2, 2, 2 * P], BF16) for mh in range(2)]
        sums = [a0, a1, a2, a3]
        for mq in range(4):
            add_turned(0, 0, pages[0:2], sums, (mq,))
        targets = [zt0[mq // 2][:, mq % 2, :, 0, :] for mq in range(4)]
        round_turned(nc.scalar.copy, targets, sums, range(4))
        put(pages[2], squares[0])
        put(pages[3], squares[1])
        for i in range(PACK):
            tanh_of(1, i)
        for i in range(PACK):
            error(i, we1, banks[4 + i])
        ready = []
        for first in (0, 2):
            if first == 0:
                pair = new("slopes0", [2, S], F32, tag="we_bf11")
            else:
                pair = late.tile([P, 2, S], F32, name="slopes2", offset=2048, align_bytes=64)
            for i, factor in enumerate(slopes_of(first, pair), first):
                nc.gpsimd.tensor_tensor(factor, factor, step[:], MULT)
                e = new(f"e1{i}", [S], F32)
                nc.scalar.copy(e[:], banks[4 + i][:])
                if i < 3:
                    nc.gpsimd.tensor_tensor(e[:], e[:], factor, MULT)
                    ready.append(e[:])
        last_error, last_factor = e, factor
        wc_dw = new("wc_dw", [2, N], U32, tag="we11")
        nc.scalar.copy(
            wc_dw[:].rearrange("p a (g t n) -> p (a g) n t", g=2, t=PACK),
            wc_w[:].bitcast(U32).rearrange("p a (g n t) -> p (a g) n t", g=2, t=PACK),
        )
        put(pages[0], ready[0])
        put(pages[1], ready[1])
        add_turned(0, 1, pages[2:4], sums, range(4))
        round_turned(nc.scalar.copy, [zt0[mq // 2][:, mq % 2, :, 1, :] for mq in range(4)], sums, range(4))
        put(pages[2], ready[2])
        z_bf0 = [new(f"z_bf0{mh}", [BANK * PACK], BF16) for mh in range(2)]
        for mq, bank in enumerate((b0, b1, b2, b3)):
            view = bank[:].rearrange("p (mb h m) -> p mb h m", mb=2, h=2)
            words = zt0[mq // 2][:, mq % 2].bitcast(F32)
            for mb in range(2):
                for h in range(2):
                    nc.tensor.transpose(view[:, mb, h, :], words[:, mb, h, :], ident[:])
            target = z_bf0[mq // 2][:].bitcast(F32).rearrange("p (q mb m h) -> p q mb m h", q=2, mb=2, h=2)
            nc.scalar.copy(target[:, mq % 2], view.rearrange("p mb h m -> p mb m h"))
        ready.append(new("last_product", [S], F32, tag="zt01")[:])
        nc.gpsimd.tensor_tensor(ready[3], last_error[:], last_factor, MULT)
        z_q = {}

        def quantize_z(name, source, codes):
            scales = new(f"z_s{name}", [codes.shape[1]], U8)
            nc.vector.quantize_mx(codes[:].bitcast(FP8X4), scales[:], source)
            return codes, scales

        first_half = quantize_z("00", z_bf0[0][:], new("z_c00", [BANK], U32))
        for c in range(2):
            z_q[0, c] = tuple(part[:, 256 * c : 256 * (c + 1)] for part in first_half)

        add_turned(1, 0, pages[0:2], sums, range(4))
        chunks = ((0, 256), (256, 256), (512, 512))
        zt1 = [new(f"zt1{mq}", [2, 2 * P], BF16)[:] for mq in range(4)]
        shared = late.tile([P, 2 * BANK], F32, name="shared", offset=4096, align_bytes=64)
        z_bf1 = [
            shared[:, BANK:].bitcast(BF16),
            new("z_bf11", [256 * PACK], BF16)[:],
            new("z_bf12", [BANK * PACK], BF16)[:],
        ]
        pairs = {c: new(f"pairs{c}", [2, chunks[c][1]], F32) for c in (1, 2)}
        first_words = z_bf1[0].bitcast(F32).rearrange("p (m h) -> p h m", h=2)
        for bank, quarters, target in (
            (b0, (0,), first_words[:, 0, :]),
            (b1, (1,), pairs[1][:, 0, :]),
            (b2, (2, 3), pairs[2][:, 0, :]),
        ):
            round_turned(nc.scalar.copy, zt1, sums, quarters)
            for u, mq in enumerate(quarters):
                words = zt1[mq].bitcast(F32)
                for mb in range(2):
                    nc.tensor.transpose(bank[:, (2 * u + mb) * P : (2 * u + mb + 1) * P], words[:, mb, :], ident[:])
            nc.scalar.copy(target, bank[:, : 2 * P * len(quarters)])

        halves = [
            late.tile([P, 2, BANK], F32, name="last_rows", offset=0, align_bytes=64)[:],
            shared[:].rearrange("p (e m) -> p e m", e=2),
        ]
        last_rows = [halves[0][:, :, :256], halves[0][:, :, 256:], halves[1]]
        for u, rows in enumerate(halves):
            cols = slice(BANK * u, BANK * (u + 1))
            nc.gpsimd.tensor_tensor(rows[:, 0, :], sp_t[1, 1][:, 0, cols], pages[2][:, cols], ADD)
        put(pages[3], ready[3])

        for c, (c0, width) in enumerate(chunks):
            cols = slice(c0, c0 + width)
            nc.vector.tensor_tensor(last_rows[c][:, 1, :], sp_t[1, 1][:, 1, cols], pages[3][:, cols], ADD)
            if c == 2:
                z_q[0, 2] = quantize_z("02", z_bf0[1][:], new("z_c02", [width], U32, tag="z_bf11"))
            if c == 0:
                rounded = z_bf1[c].rearrange("p (m h e) -> p m h e", h=2, e=2)[:, :, 1, :]
            else:
                rounded = pairs[c][:, 1, :].bitcast(BF16).rearrange("p (m e) -> p m e", e=2)
            nc.vector.tensor_copy(rounded, last_rows[c].rearrange("p e m -> p m e"))
            if c > 0:
                nc.vector.tensor_copy(
                    z_bf1[c].bitcast(F32).rearrange("p (m h) -> p m h", h=2), pairs[c][:].rearrange("p h m -> p m h")
                )
            z_q[1, c] = quantize_z(f"1{c}", z_bf1[c], new(f"z_c1{c}", [width], U32))

        y_s = new("y_s", [T2], U8)
        units = (
            (0, 0, 256, (a0, a1), "we010"),
            (1, 0, 256, (a2, a3), "we011"),
            (0, 256, 256, (b3, b0), "sp00"),
            (1, 256, 256, (b1, b2), "sp01"),
            (0, 512, 512, (a0, a1, a2, a3), "we00"),
            (1, 512, 512, (b3, b0, b1, b2), "tab_w0"),
        )

        def last_passes(u, k, a):
            g, m0, width, group, tag = units[u]
            c = min(m0 // 256, 2)
            cols = slice(m0 - chunks[c][0], m0 - chunks[c][0] + width)
            codes, scales = z_q[a, c]
            share = BANK // width
            for s in range(share):
                c0 = KP * g + P * (share * k + s)
                nc.tensor.matmul_mx(
                    group[k][:, s * width : (s + 1) * width],
                    lhsT=wc_dw[:, a, c0 : c0 + P].bitcast(FP8X4),
                    lhsT_scale=wc_ds[4 * a :, c0 : c0 + P],
                    rhs=codes[:, cols].bitcast(FP8X4),
                    rhs_scale=scales[:, cols],
                    start=(a == (0 if u < 3 else 1) and s == 0),
                    stop=(a == (1 if u < 3 else 0) and s == share - 1),
                )

        for u in range(3):
            for k in range(2):
                last_passes(u, k, 0)

        for u, (g, m0, width, group, tag) in enumerate(units):
            cols = slice(m0, m0 + width)
            y = new(f"y{u}", [PACK, width], F32, tag=tag)
            rows = out_0[KP * g : KP * (g + 1), cols].rearrange("(p t) m -> p t m", t=PACK)
            share = BANK // width
            for k, bank in enumerate(group):
                for a in (1,) if u < 3 else (1, 0):
                    last_passes(u, k, a)
                done = share * (k + 1)
                nc.scalar.copy(y[:, done - share : done, :], bank[:].rearrange("p (s m) -> p s m", s=share))
                run = 2 if u in (0, 4, 5) else PACK
                if done % run == 0:
                    nc.sync.dma_start(rows[:, done - run : done, :], y[:, done - run : done, :])
            y_bf = new(f"y_bf{u}", [width * PACK], BF16, tag=f"we_bf0{u % 2}")
            copies = (nc.vector.tensor_copy, nc.scalar.copy) if u == len(units) - 1 else (nc.vector.tensor_copy,)
            cuts = (0, 384, 512) if u == len(units) - 1 else (0, width)
            for copy, c0, c1 in zip(copies, cuts, cuts[1:]):
                copy(
                    y_bf[:, PACK * c0 : PACK * c1].rearrange("p (c i t) -> p c t i", i=4, t=PACK),
                    y[:, :, c0:c1].rearrange("p t (c i) -> p c t i", i=4),
                )
            y_c = new(f"y_c{u}", [width], U32)
            nc.vector.quantize_mx(y_c[:].bitcast(FP8X4), y_s[4 * g :, cols], y_bf[:])
            nc.sync.dma_start(out_1[g, :, cols, :].rearrange("p m t -> p (m t)").bitcast(I32), y_c[:].bitcast(I32))
        for q in range(4):
            nc.sync.dma_start(out_2[:, 4 * q : 4 * q + 4, :].bitcast(I32), y_s[32 * q : 32 * q + 8, :].bitcast(I32))
